import numpy as np
import ml_dtypes


def mxq(x, axis, fmt="e4m3"):
    dtype, down = {"e4m3": (ml_dtypes.float8_e4m3fn, 7), "e5m2": (ml_dtypes.float8_e5m2, 14)}[fmt]
    v = np.moveaxis(np.asarray(x, np.float32).astype(ml_dtypes.bfloat16).astype(np.float64), axis, -1)
    blocks = v.reshape(v.shape[:-1] + (-1, 32))
    amax = np.abs(blocks).max(-1, keepdims=True)
    byte = np.maximum(np.where(amax > 0, np.frexp(amax)[1] - 1 + 127, 0) - down, 1)
    scale = np.exp2(byte - 127.0)
    codes = (blocks / scale).astype(np.float32).astype(dtype).astype(np.float64)
    return np.moveaxis((codes * scale).reshape(v.shape), -1, axis)


WIDE = False


def mx_kscale(k):
    if not WIDE:
        return np.ones(k)
    levels = np.array([30, -30])
    if k % 512:
        return np.exp2(np.random.permutation(np.resize(levels, k // 32))).repeat(32)
    a = np.empty((k // 512, 16))
    for p in range(k // 512):
        a[p, :8] = np.random.permutation(np.resize(levels, 8))
        for g in range(8):
            far = levels[np.abs(levels - a[p, g]) >= 10]
            a[p, g + 8] = far[np.random.randint(len(far))]
    return np.exp2(a.ravel()).repeat(32)


BF16 = ml_dtypes.bfloat16


def bf(x):
    return np.asarray(x, np.float32).astype(BF16)


def f64(x):
    return np.asarray(x).astype(np.float64)


E2M1 = np.array([0.0, 0.5, 1.0, 1.5, 2.0, 3.0, 4.0, 6.0, -0.0, -0.5, -1.0, -1.5, -2.0, -3.0, -4.0, -6.0])


def pack_weight(w, fmt):
    k, n = w.shape
    w = f64(bf(w)).reshape(k // 32, 32, n)
    amax = np.abs(w).max(1)
    if fmt in ("e4m3", "e5m2"):
        byte = np.frexp(amax)[1] - 1 + 127 - (7 if fmt == "e4m3" else 14)
    else:
        mant, ex = np.frexp(amax / 6.0)
        byte = np.where(mant > 0.5, ex, ex - 1) + 127
    byte = np.clip(np.where(amax > 0, byte, 1), 1, 254)
    scaled = (w * np.exp2(127.0 - byte)[:, None, :]).reshape(k, n).astype(np.float32)
    by_word = np.ascontiguousarray(scaled.reshape(k // 512, 128, 4, n).transpose(0, 1, 3, 2))
    if fmt in ("e4m3", "e5m2"):
        words = by_word.astype(ml_dtypes.float8_e4m3fn if fmt == "e4m3" else ml_dtypes.float8_e5m2).view(np.uint8)
    else:
        c = by_word.astype(ml_dtypes.float4_e2m1fn).view(np.uint8) & 0xF
        words = c[..., 0::2] | (c[..., 1::2] << 4)
    return np.ascontiguousarray(words), np.ascontiguousarray(byte.astype(np.uint8).reshape(k // 512, 16, n))


def unpack_weight(words, scales, fmt):
    g, p, n, _ = words.shape
    if fmt in ("e4m3", "e5m2"):
        vals = np.ascontiguousarray(words).view(ml_dtypes.float8_e4m3fn if fmt == "e4m3" else ml_dtypes.float8_e5m2).astype(np.float64)
    else:
        nib = np.empty((g, p, n, 4), np.uint8)
        nib[..., 0::2] = words & 0xF
        nib[..., 1::2] = words >> 4
        vals = E2M1[nib]
    vals = vals * np.repeat(np.exp2(scales.astype(np.float64) - 127.0), 8, axis=1)[..., None]
    return vals.transpose(0, 1, 3, 2).reshape(g * 512, n)


T, H, C, Q = 2048, 1024, 1024, 1536


def setup_inputs():
    s, t = mx_kscale(T), mx_kscale(H)
    G = np.random.standard_normal((T, C)) * np.exp(0.5 * np.random.standard_normal((T, C)))
    g_words, g_scales = pack_weight(G / s[:, None], "e5m2")
    return {"g_words": g_words, "g_scales": g_scales,
            "phi_train": bf(np.random.standard_normal((T, H)) / np.sqrt(H) * s[:, None] * t),
            "mult": bf(1 + 0.3 * np.random.standard_normal((H, C))),
            "phi_test": bf(np.random.standard_normal((Q, H)) / np.sqrt(H) / t),
            "f0": bf(np.random.standard_normal((Q, C)))}


def reference(g_words, g_scales, phi_train, mult, phi_test, f0):
    G = unpack_weight(g_words, g_scales, "e5m2")
    a = mxq(f64(phi_train), 0, "e4m3").T @ G
    d = a * np.square(f64(mult))
    k = mxq(f64(phi_test), 1, "e4m3") @ mxq(d, 0, "e5m2")
    return f0.astype(np.float64) + k

@@ -1,0 +1,267 @@
+from contextlib import ExitStack
+
+import concourse.mybir as mybir
+from concourse.masks import make_identity
+
+T, H, C, Q = 2048, 1024, 1024, 1536
+FLOPS = 2 * T * H * C + 2 * Q * H * C
+
+F32 = mybir.dt.float32
+BF16 = mybir.dt.bfloat16
+U32 = mybir.dt.uint32
+I32 = mybir.dt.int32
+U8 = mybir.dt.uint8
+E4M3X4 = mybir.dt.float8_e4m3fn_x4
+E5M2X4 = mybir.dt.float8_e5m2_x4
+ACT = mybir.ActivationFunctionType
+ALU = mybir.AluOpType
+
+P = 128
+PACK = 4
+KP = 512
+N = 512
+TG = T // KP
+HG = H // KP
+CH = C // N
+QT = Q // P
+
+
+def schedule():
+    loads = [("P", (0, 0, 1)), ("P", (0, 1, 2)), ("G", (0, 0, 1)), ("P", (1, 0, 2)), ("G", (0, 1, 2))]
+    loads += [("P", (2, 0, 2)), ("P", (3, 0, 2)), ("G", (0, 2, 3)), ("G", (0, 3, 4))]
+    loads += [("M", (0, 0)), ("M", (1, 0)), ("G", (1, 0, TG)), ("M", (0, 1)), ("M", (1, 1))]
+    loads += [("T", (j, j + 2)) for j in range(0, 8, 2)]
+    loads += [("F", (0, 2)), ("T", (8, 10)), ("F", (2, 4)), ("T", (10, 12))]
+    loads += [("F", (j, j + 2)) for j in range(4, QT, 2)]
+    s = []
+    for g in range(TG):
+        for hg in range(HG):
+            s += [("int", "V", g, hg, 0), ("int", "S", g, hg, 1)]
+        for hg in range(HG):
+            s += [("q", g, hg)] + [("mm1", hg, 0, t, g) for t in range(PACK)]
+
+    def sweep(hg, t):
+        return [("mm1", hg, 1, t, g) for g in range(TG)]
+
+    def scale(hg, ch, t):
+        return [("sq", hg, ch, t), ("mul", hg, ch, t)]
+
+    def turn(j):
+        return [("tr", j), ("cp", "S", j)]
+
+    def second(j, ch):
+        return [("mm2", j, ch), ("add", j, ch)]
+
+    for hg in range(HG):
+        for t in range(PACK):
+            s += scale(hg, 0, t) + sweep(hg, t)
+    s += [("di", "S", 0, 0, 0), ("di", "V", 0, 0, 1)]
+    s += scale(0, 1, 0) + [("dq", 0, 0)] + scale(0, 1, 1) + [("di", "V", 1, 0, 1)] + scale(0, 1, 2) + scale(0, 1, 3)
+    s += [("di", "S", 1, 0, 0)]
+    s += scale(1, 1, 0) + [("dq", 1, 0)] + scale(1, 1, 1) + [("di", "V", 0, 1, 1)] + scale(1, 1, 2) + scale(1, 1, 3)
+    s += [("di", "S", 0, 1, 0)]
+    s += turn(0) + turn(1) + [("di", "V", 1, 1, 1), ("dq", 0, 1), ("tq", 0), ("tq", 1)] + turn(2) + turn(3)
+    s += [("di", "S", 1, 1, 0), ("tq", 2), ("tq", 3)]
+    s += turn(4) + turn(5)
+    s += second(0, 0) + [("dq", 1, 1)] + second(1, 0) + [("tq", 4)] + second(2, 0) + [("tq", 5)] + second(3, 0)
+    for j in range(6, QT):
+        s += turn(j) if j < 10 else []
+    for j in range(4):
+        s += second(j, 1) + [("st", j, 0, 2), ("tq", j + 6)]
+    s += turn(10) + turn(11)
+    for j in range(4, QT):
+        s += second(j, 0) + second(j, 1) + [("st", j, 0, 2)]
+        if j < 6:
+            s += [("tq", j + 6)]
+    return loads, s
+
+
+def tile_readout_ntk_step_e3_kernel(tc, g_words, g_scales, phi_train, mult, phi_test, f0, out):
+    nc = tc.nc
+    with ExitStack() as ctx:
+        keep = ctx.enter_context(tc.tile_pool(name="keep", bufs=1))
+        work = ctx.enter_context(tc.tile_pool(name="work", bufs=1))
+        psum = ctx.enter_context(tc.psum_pool(name="psum", bufs=1))
+        ctx.enter_context(tc.manual_schedule())
+
+        ident = keep.tile([P, P], F32, name="ident")
+        warm = keep.tile([P, 8], F32, name="warm")
+        warm_out = keep.tile([P, 8], F32, name="warm_out")
+        g_plane = keep.tile([P, TG, C], U8, name="g_plane", align_bytes=64)
+        g_codes = keep.tile([P, CH, TG, N], U32, name="g_codes", align_bytes=64)
+        p_raw = []
+        for g in range(TG):
+            p_raw.append(work.tile([P, PACK, H], BF16, name="slab", bufs=6, align_bytes=64))
+        p_codes = keep.tile([P, TG, H], U32, name="p_codes", align_bytes=64)
+        p_plane = keep.tile([P, TG, H], U8, name="p_plane", align_bytes=64)
+        m_raw = keep.tile([P, CH, HG, PACK, N], BF16, name="m_raw", align_bytes=64)
+        d_codes = keep.tile([P, CH, HG, N], U32, name="d_codes", align_bytes=64)
+        d_plane = keep.tile([P, CH, HG, N], U8, name="d_plane", align_bytes=64)
+        t_raw = keep.tile([P, QT, H], BF16, name="t_raw", align_bytes=64)
+        t_codes = keep.tile([P, QT, HG * P], U32, name="t_codes", align_bytes=64)
+        t_plane = keep.tile([P, QT, HG * P], U8, name="t_plane", align_bytes=64)
+        f_raw = keep.tile([P, QT, C], BF16, name="f_raw", align_bytes=64)
+
+        g_bytes = g_words.rearrange("g p n t -> p g (n t)")
+        p_rows = phi_train.rearrange("(g p j) h -> p g j h", p=P, j=PACK)
+        m_rows = mult.rearrange("(g p j) c -> p g j c", p=P, j=PACK)
+        t_rows = phi_test.rearrange("(p j) h -> p j h", j=QT)
+        f_rows = f0.rearrange("(p j) c -> p j c", j=QT)
+        out_rows = out.rearrange("(p j) c -> p j c", j=QT)
+
+        tiles = {}
+        free_banks = list(range(8))
+        bank_of = {}
+
+        def take_bank(key):
+            b = free_banks.pop(0)
+            bank_of[key] = b
+            tiles[key] = psum.tile([P, N], F32, name="bank%d" % b)
+            return tiles[key]
+
+        def give_bank(key):
+            free_banks.append(bank_of[key])
+
+        def copy(eng, dst, src):
+            if eng == "V":
+                nc.vector.tensor_copy(out=dst, in_=src)
+            else:
+                nc.scalar.copy(out=dst, in_=src)
+
+        def cols(i, w=N):
+            return slice(i * w, (i + 1) * w)
+
+        def load(kind, a):
+            if kind == "S":
+                for q in range(4):
+                    nc.scalar.dma_start(
+                        out=g_plane[32 * q : 32 * q + 4, :, :].bitcast(I32),
+                        in_=g_scales[:, 4 * q : 4 * q + 4, :].rearrange("g r n -> r g n").bitcast(I32),
+                    )
+            elif kind == "P":
+                g, lo, hi = a
+                nc.sync.dma_start(out=p_raw[g][:, :, lo * KP : hi * KP], in_=p_rows[:, g, :, lo * KP : hi * KP])
+            elif kind == "G":
+                ch, lo, hi = a
+                nc.sync.dma_start(
+                    out=g_codes[:, ch, lo:hi, :].bitcast(I32),
+                    in_=g_bytes[:, lo:hi, cols(ch, PACK * N)].bitcast(I32),
+                )
+            elif kind == "M":
+                hg, ch = a
+                nc.sync.dma_start(out=m_raw[:, ch, hg, :, :], in_=m_rows[:, hg, :, cols(ch)])
+            elif kind == "T":
+                lo, hi = a
+                nc.sync.dma_start(out=t_raw[:, lo:hi, :], in_=t_rows[:, lo:hi, :])
+            elif kind == "F":
+                lo, hi = a
+                nc.sync.dma_start(out=f_raw[:, lo:hi, :], in_=f_rows[:, lo:hi, :])
+
+        def step(s):
+            kind = s[0]
+            if kind == "int":
+                eng, g, hg, hf = s[1:]
+                if ("pg", g, hg) not in tiles:
+                    tiles["pg", g, hg] = work.tile([P, PACK * KP], BF16, name="p_grouped", bufs=3, align_bytes=64)
+                src = p_raw[g][:, :, cols(hg)].rearrange("p j (m t) -> p t m j", t=PACK)[:, 2 * hf : 2 * hf + 2, :, :]
+                dst = tiles["pg", g, hg][:, cols(hf, 1024)].rearrange("p (t m j) -> p t m j", t=2, j=PACK)
+                copy(eng, dst, src)
+            elif kind == "q":
+                g, hg = s[1:]
+                nc.vector.quantize_mx(
+                    out=p_codes[:, g, cols(hg)].bitcast(E4M3X4), scales=p_plane[:, g, cols(hg)], in_=tiles["pg", g, hg][:]
+                )
+            elif kind == "mm1":
+                hg, ch, t, g = s[1:]
+                acc = take_bank(("a", hg, ch, t)) if g == 0 else tiles["a", hg, ch, t]
+                w = cols(hg * PACK + t, P)
+                nc.tensor.matmul_mx(
+                    out=acc[:],
+                    lhsT=p_codes[:, g, w].bitcast(E4M3X4),
+                    lhsT_scale=p_plane[:, g, w],
+                    rhs=g_codes[:, ch, g, :].bitcast(E5M2X4),
+                    rhs_scale=g_plane[:, g, cols(ch)],
+                    start=(g == 0),
+                    stop=(g == TG - 1),
+                )
+            elif kind == "sq":
+                hg, ch, t = s[1:]
+                tiles["m2", hg, ch, t] = work.tile([P, N], F32, name="m_squared", bufs=5, align_bytes=64)
+                nc.scalar.activation(out=tiles["m2", hg, ch, t][:], in_=m_raw[:, ch, hg, t, :], func=ACT.Square)
+            elif kind == "mul":
+                hg, ch, t = s[1:]
+                if ("df", hg, ch) not in tiles:
+                    tiles["df", hg, ch] = work.tile([P, PACK, N], BF16, name="d_flat", bufs=2, align_bytes=64)
+                nc.vector.tensor_tensor(
+                    out=tiles["df", hg, ch][:, t, :], in0=tiles["a", hg, ch, t][:], in1=tiles["m2", hg, ch, t][:], op=ALU.mult
+                )
+                give_bank(("a", hg, ch, t))
+            elif kind == "di":
+                eng, hg, ch, hf = s[1:]
+                if ("dg", hg, ch) not in tiles:
+                    tiles["dg", hg, ch] = work.tile([P, N, PACK], BF16, name="d_grouped", bufs=2, align_bytes=64)
+                w = cols(hf, N // 2)
+                copy(eng, tiles["dg", hg, ch][:, w, :], tiles["df", hg, ch][:, :, w].rearrange("p t c -> p c t"))
+            elif kind == "dq":
+                hg, ch = s[1:]
+                nc.vector.quantize_mx(
+                    out=d_codes[:, ch, hg, :].bitcast(E5M2X4),
+                    scales=d_plane[:, ch, hg, :],
+                    in_=tiles["dg", hg, ch][:].rearrange("p c t -> p (c t)"),
+                )
+            elif kind == "tr":
+                j = s[1]
+                bank = take_bank(("x", j))
+                words = t_raw[:, j, :].bitcast(F32)
+                for hg in range(HG):
+                    for u in range(2):
+                        nc.tensor.transpose(
+                            bank[:, cols(2 * hg + u, P)], words[:, 256 * hg + u : 256 * (hg + 1) : 2], ident[:]
+                        )
+            elif kind == "cp":
+                eng, j = s[1:]
+                tiles["tg", j] = work.tile([P, HG * P * PACK], BF16, name="t_grouped", bufs=4, align_bytes=64)
+                copy(
+                    eng,
+                    tiles["tg", j][:].bitcast(F32).rearrange("p (g q u) -> p g q u", g=HG, u=2),
+                    tiles["x", j][:].rearrange("p (g u q) -> p g q u", g=HG, u=2),
+                )
+                give_bank(("x", j))
+            elif kind == "tq":
+                j = s[1]
+                nc.vector.quantize_mx(out=t_codes[:, j, :].bitcast(E4M3X4), scales=t_plane[:, j, :], in_=tiles["tg", j][:])
+            elif kind == "mm2":
+                j, ch = s[1:]
+                acc = take_bank(("k", j, ch))
+                for hg in range(HG):
+                    nc.tensor.matmul_mx(
+                        out=acc[:],
+                        lhsT=t_codes[:, j, cols(hg, P)].bitcast(E4M3X4),
+                        lhsT_scale=t_plane[:, j, cols(hg, P)],
+                        rhs=d_codes[:, ch, hg, :].bitcast(E5M2X4),
+                        rhs_scale=d_plane[:, ch, hg, :],
+                        start=(hg == 0),
+                        stop=(hg == HG - 1),
+                    )
+            elif kind == "add":
+                j, ch = s[1:]
+                if ("r", j // 2) not in tiles:
+                    tiles["r", j // 2] = work.tile([P, 2, C], F32, name="slab", bufs=6, align_bytes=64)
+                nc.vector.tensor_tensor(
+                    out=tiles["r", j // 2][:, j % 2, cols(ch)], in0=tiles["k", j, ch][:], in1=f_raw[:, j, cols(ch)], op=ALU.add
+                )
+                give_bank(("k", j, ch))
+            elif kind == "st":
+                j, lo, hi = s[1:]
+                nc.sync.dma_start(out=out_rows[:, j, lo * N : hi * N], in_=tiles["r", j // 2][:, j % 2, lo * N : hi * N])
+
+        nc.vector.memset(g_plane[:].rearrange("p g n -> p (g n)").bitcast(U32), 0)
+        nc.vector.memset(warm[:], 1.0)
+        make_identity(nc, ident[:])
+        load("S", None)
+        nc.scalar.activation(out=warm_out[:], in_=warm[:], func=ACT.Square)
+        loads, steps = schedule()
+        for kind, a in loads:
+            load(kind, a)
+        for s in steps:
+            step(s)

@@ -28,15 +28,15 @@ QT = Q // P
 
 def schedule():
     loads = [("P", (0, 0, 1)), ("P", (0, 1, 2)), ("G", (0, 0, 1)), ("P", (1, 0, 2)), ("G", (0, 1, 2))]
-    loads += [("P", (2, 0, 2)), ("P", (3, 0, 2)), ("G", (0, 2, 3)), ("G", (0, 3, 4))]
-    loads += [("M", (0, 0)), ("M", (1, 0)), ("G", (1, 0, TG)), ("M", (0, 1)), ("M", (1, 1))]
-    loads += [("T", (j, j + 2)) for j in range(0, 8, 2)]
-    loads += [("F", (0, 2)), ("T", (8, 10)), ("F", (2, 4)), ("T", (10, 12))]
+    loads += [("P", (2, 0, 2)), ("G", (0, 2, 3)), ("P", (3, 0, 1)), ("P", (3, 1, 2)), ("G", (0, 3, 4))]
+    loads += [("M", (0, 0)), ("G", (1, 0, TG)), ("M", (1, 0)), ("M", (0, 1)), ("T", (0, 2)), ("M", (1, 1))]
+    loads += [("T", (2, 4)), ("T", (4, 6)), ("F", (0, 2)), ("T", (6, 8)), ("T", (8, 10)), ("F", (2, 4)), ("T", (10, 12))]
     loads += [("F", (j, j + 2)) for j in range(4, QT, 2)]
     s = []
+    cut = 68
     for g in range(TG):
         for hg in range(HG):
-            s += [("int", "V", g, hg, 0), ("int", "S", g, hg, 1)]
+            s += [("int", "V", g, hg, 0, cut), ("int", "S", g, hg, cut, P)]
         for hg in range(HG):
             s += [("q", g, hg)] + [("mm1", hg, 0, t, g) for t in range(PACK)]
 
@@ -46,33 +46,36 @@ def schedule():
     def scale(hg, ch, t):
         return [("sq", hg, ch, t), ("mul", hg, ch, t)]
 
-    def turn(j):
-        return [("tr", j), ("cp", "S", j)]
-
     def second(j, ch):
-        return [("mm2", j, ch), ("add", j, ch)]
+        return [("mm2", j, ch), ("add", j, ch)] + ([("st", j, ch, ch + 1)] if j < 6 or j == QT - 1 else [])
 
-    for hg in range(HG):
-        for t in range(PACK):
-            s += scale(hg, 0, t) + sweep(hg, t)
-    s += [("di", "S", 0, 0, 0), ("di", "V", 0, 0, 1)]
-    s += scale(0, 1, 0) + [("dq", 0, 0)] + scale(0, 1, 1) + [("di", "V", 1, 0, 1)] + scale(0, 1, 2) + scale(0, 1, 3)
-    s += [("di", "S", 1, 0, 0)]
-    s += scale(1, 1, 0) + [("dq", 1, 0)] + scale(1, 1, 1) + [("di", "V", 0, 1, 1)] + scale(1, 1, 2) + scale(1, 1, 3)
-    s += [("di", "S", 0, 1, 0)]
-    s += turn(0) + turn(1) + [("di", "V", 1, 1, 1), ("dq", 0, 1), ("tq", 0), ("tq", 1)] + turn(2) + turn(3)
-    s += [("di", "S", 1, 1, 0), ("tq", 2), ("tq", 3)]
-    s += turn(4) + turn(5)
-    s += second(0, 0) + [("dq", 1, 1)] + second(1, 0) + [("tq", 4)] + second(2, 0) + [("tq", 5)] + second(3, 0)
+    def weave(eng, hg, ch, lo, hi):
+        return [("di", eng, hg, ch, lo, hi)] if hi > lo else []
+
+    def each(kind, lo, hi):
+        return [(kind, "S", j) if kind == "cp" else (kind, j) for j in range(lo, hi)]
+
+    for t in range(PACK):
+        s += scale(0, 0, t) + sweep(0, t)
+    s += weave("V", 0, 0, 0, 64)
+    for t in range(PACK):
+        s += scale(1, 0, t)
+    s += sweep(1, 0) + sweep(1, 1)
+    s += weave("S", 0, 0, 64, P)
+    s += scale(0, 1, 0) + [("dq", 0, 0)] + scale(0, 1, 1) + weave("V", 1, 0, 0, 64) + each("tr", 0, 4)
+    s += scale(0, 1, 2) + scale(0, 1, 3) + weave("S", 1, 0, 64, P) + sweep(1, 2) + sweep(1, 3)
+    s += scale(1, 1, 0) + [("dq", 1, 0)] + scale(1, 1, 1) + each("cp", 0, 2) + weave("V", 0, 1, 0, 32)
+    s += each("tq", 0, 2) + [("sq", 1, 1, 2), ("sq", 1, 1, 3)] + each("cp", 2, 4) + [("mul", 1, 1, 2)] + each("tq", 2, 4) + [("mul", 1, 1, 3)]
+    s += second(0, 0) + second(1, 0) + weave("S", 0, 1, 32, P) + each("tr", 4, 8) + weave("V", 1, 1, 0, 32)
+    s += [("dq", 0, 1)] + each("cp", 4, 6) + weave("S", 1, 1, 32, P) + each("cp", 6, 8)
+    s += second(2, 0) + each("tq", 4, 6) + second(3, 0) + each("tr", 8, 10) + [("dq", 1, 1)] + second(4, 0) + second(5, 0) + each("tq", 6, 8)
+    s += each("cp", 8, 10) + each("tr", 10, 12) + each("cp", 10, 12)
+    for j in range(6):
+        s += second(j, 1)
+        if j < 4:
+            s += [("tq", j + 8)]
     for j in range(6, QT):
-        s += turn(j) if j < 10 else []
-    for j in range(4):
-        s += second(j, 1) + [("st", j, 0, 2), ("tq", j + 6)]
-    s += turn(10) + turn(11)
-    for j in range(4, QT):
-        s += second(j, 0) + second(j, 1) + [("st", j, 0, 2)]
-        if j < 6:
-            s += [("tq", j + 6)]
+        s += second(j, 0) + second(j, 1) + ([("st", j, 0, 2)] if j < QT - 1 else [])
     return loads, s
 
 
@@ -160,11 +163,11 @@ def tile_readout_ntk_step_e3_kernel(tc, g_words, g_scales, phi_train, mult, phi_
         def step(s):
             kind = s[0]
             if kind == "int":
-                eng, g, hg, hf = s[1:]
+                eng, g, hg, lo, hi = s[1:]
                 if ("pg", g, hg) not in tiles:
                     tiles["pg", g, hg] = work.tile([P, PACK * KP], BF16, name="p_grouped", bufs=3, align_bytes=64)
-                src = p_raw[g][:, :, cols(hg)].rearrange("p j (m t) -> p t m j", t=PACK)[:, 2 * hf : 2 * hf + 2, :, :]
-                dst = tiles["pg", g, hg][:, cols(hf, 1024)].rearrange("p (t m j) -> p t m j", t=2, j=PACK)
+                src = p_raw[g][:, :, cols(hg)].rearrange("p j (m t) -> p m j t", t=PACK)[:, lo:hi, :, :]
+                dst = tiles["pg", g, hg][:].rearrange("p (t m j) -> p m j t", t=PACK, j=PACK)[:, lo:hi, :, :]
                 copy(eng, dst, src)
             elif kind == "q":
                 g, hg = s[1:]
@@ -197,11 +200,12 @@ def tile_readout_ntk_step_e3_kernel(tc, g_words, g_scales, phi_train, mult, phi_
                 )
                 give_bank(("a", hg, ch, t))
             elif kind == "di":
-                eng, hg, ch, hf = s[1:]
+                eng, hg, ch, lo, hi = s[1:]
                 if ("dg", hg, ch) not in tiles:
                     tiles["dg", hg, ch] = work.tile([P, N, PACK], BF16, name="d_grouped", bufs=2, align_bytes=64)
-                w = cols(hf, N // 2)
-                copy(eng, tiles["dg", hg, ch][:, w, :], tiles["df", hg, ch][:, :, w].rearrange("p t c -> p c t"))
+                src = tiles["df", hg, ch][:].rearrange("p t (c i) -> p c t i", i=PACK)[:, lo:hi, :, :]
+                dst = tiles["dg", hg, ch][:].rearrange("p (c i) t -> p c t i", i=PACK)[:, lo:hi, :, :]
+                copy(eng, dst, src)
             elif kind == "dq":
                 hg, ch = s[1:]
                 nc.vector.quantize_mx(

@@ -18,65 +18,70 @@ ALU = mybir.AluOpType
 
 P = 128
 PACK = 4
-KP = 512
+K_PASS = P * PACK
 N = 512
-TG = T // KP
-HG = H // KP
-CH = C // N
-QT = Q // P
+BANKS = 8
+T_GROUPS = T // K_PASS
+H_GROUPS = H // K_PASS
+ROW_TILES = Q // P
+
+QUADS = [(0, 0), (1, 0), (0, 1), (1, 1)]
+
+TRAIN_CUT = 68
+QUAD_CUTS = [96, 112, 32, 16]
+
+LOADS = [
+    ("train", 0, 0, 1), ("train", 0, 1, 2), ("train", 1, 0, 2), ("g", 0, 1, 0),
+    ("train", 2, 0, 2), ("g", 1, 2, 0), ("train", 3, 0, 2), ("g", 2, 3, 0),
+    ("mult", 0, 0, 1), ("g", 3, 4, 0), ("g", 0, 4, 1), ("mult", 1, 0, 2), ("mult", 0, 1, 2),
+    ("test", 0, 4), ("f0", 0, 4), ("test", 4, 8), ("f0", 4, 8), ("test", 8, 12), ("f0", 8, 12),
+]
+
+TENSOR_ORDER = "AAAAAA TTTT AA XX TTT XXXX TTT YYY X YYYY X TT XY XY XY Y XY"
+VECTOR_ORDER = "mmmm vd mmmm mv mmm md qq mq mv am qa qq av da d aa qq aaaaaaa qq aa q aaaaa q aaaa"
+SCALAR_ORDER = "ssss w ssss ssss ss w c s c s cc w cc w cccccc"
+
+SQUARES_AHEAD = 6
 
 
-def schedule():
-    loads = [("P", (0, 0, 1)), ("P", (0, 1, 2)), ("G", (0, 0, 1)), ("P", (1, 0, 2)), ("G", (0, 1, 2))]
-    loads += [("P", (2, 0, 2)), ("G", (0, 2, 3)), ("P", (3, 0, 1)), ("P", (3, 1, 2)), ("G", (0, 3, 4))]
-    loads += [("M", (0, 0)), ("G", (1, 0, TG)), ("M", (1, 0)), ("M", (0, 1)), ("T", (0, 2)), ("M", (1, 1))]
-    loads += [("T", (2, 4)), ("T", (4, 6)), ("F", (0, 2)), ("T", (6, 8)), ("T", (8, 10)), ("F", (2, 4)), ("T", (10, 12))]
-    loads += [("F", (j, j + 2)) for j in range(4, QT, 2)]
-    s = []
-    cut = 68
-    for g in range(TG):
-        for hg in range(HG):
-            s += [("int", "V", g, hg, 0, cut), ("int", "S", g, hg, cut, P)]
-        for hg in range(HG):
-            s += [("q", g, hg)] + [("mm1", hg, 0, t, g) for t in range(PACK)]
+def merged_order():
+    queues = [list(order.replace(" ", "")) for order in (TENSOR_ORDER, SCALAR_ORDER, VECTOR_ORDER)]
+    count = {kind: 0 for kind in "ATXYsmvwdcqa"}
+    free = 0
+    steps = []
 
-    def sweep(hg, t):
-        return [("mm1", hg, 1, t, g) for g in range(TG)]
+    def ready(kind):
+        i = count[kind]
+        needs = {
+            "A": free > 0,
+            "T": free > 0,
+            "X": free > 0 and count["q"] > i and count["d"] >= H_GROUPS,
+            "Y": free > 0 and count["q"] > i and count["d"] >= len(QUADS),
+            "s": i - count["m"] < SQUARES_AHEAD,
+            "m": count["s"] > i and count["A"] > i - BANKS,
+            "v": count["m"] >= PACK * (i + 1),
+            "w": count["m"] >= PACK * (i + 1),
+            "d": count["v"] > i and count["w"] > i,
+            "c": count["T"] > i,
+            "q": count["c"] > i,
+            "a": count["X"] + count["Y"] > i,
+        }
+        return needs[kind]
 
-    def scale(hg, ch, t):
-        return [("sq", hg, ch, t), ("mul", hg, ch, t)]
+    while any(queues):
+        before = len(steps)
+        for queue in queues:
+            if queue and ready(queue[0]):
+                kind = queue.pop(0)
+                steps.append((kind, count[kind]))
+                count[kind] += 1
+                free += (kind in "mca") - (kind in "ATXY")
+        assert len(steps) > before
+    return steps
 
-    def second(j, ch):
-        return [("mm2", j, ch), ("add", j, ch)] + ([("st", j, ch, ch + 1)] if j < 6 or j == QT - 1 else [])
 
-    def weave(eng, hg, ch, lo, hi):
-        return [("di", eng, hg, ch, lo, hi)] if hi > lo else []
-
-    def each(kind, lo, hi):
-        return [(kind, "S", j) if kind == "cp" else (kind, j) for j in range(lo, hi)]
-
-    for t in range(PACK):
-        s += scale(0, 0, t) + sweep(0, t)
-    s += weave("V", 0, 0, 0, 64)
-    for t in range(PACK):
-        s += scale(1, 0, t)
-    s += sweep(1, 0) + sweep(1, 1)
-    s += weave("S", 0, 0, 64, P)
-    s += scale(0, 1, 0) + [("dq", 0, 0)] + scale(0, 1, 1) + weave("V", 1, 0, 0, 64) + each("tr", 0, 4)
-    s += scale(0, 1, 2) + scale(0, 1, 3) + weave("S", 1, 0, 64, P) + sweep(1, 2) + sweep(1, 3)
-    s += scale(1, 1, 0) + [("dq", 1, 0)] + scale(1, 1, 1) + each("cp", 0, 2) + weave("V", 0, 1, 0, 32)
-    s += each("tq", 0, 2) + [("sq", 1, 1, 2), ("sq", 1, 1, 3)] + each("cp", 2, 4) + [("mul", 1, 1, 2)] + each("tq", 2, 4) + [("mul", 1, 1, 3)]
-    s += second(0, 0) + second(1, 0) + weave("S", 0, 1, 32, P) + each("tr", 4, 8) + weave("V", 1, 1, 0, 32)
-    s += [("dq", 0, 1)] + each("cp", 4, 6) + weave("S", 1, 1, 32, P) + each("cp", 6, 8)
-    s += second(2, 0) + each("tq", 4, 6) + second(3, 0) + each("tr", 8, 10) + [("dq", 1, 1)] + second(4, 0) + second(5, 0) + each("tq", 6, 8)
-    s += each("cp", 8, 10) + each("tr", 10, 12) + each("cp", 10, 12)
-    for j in range(6):
-        s += second(j, 1)
-        if j < 4:
-            s += [("tq", j + 8)]
-    for j in range(6, QT):
-        s += second(j, 0) + second(j, 1) + ([("st", j, 0, 2)] if j < QT - 1 else [])
-    return loads, s
+def cols(i, width):
+    return slice(i * width, (i + 1) * width)
 
 
 def tile_readout_ntk_step_e3_kernel(tc, g_words, g_scales, phi_train, mult, phi_test, f0, out):
@@ -88,184 +93,180 @@ def tile_readout_ntk_step_e3_kernel(tc, g_words, g_scales, phi_train, mult, phi_
         ctx.enter_context(tc.manual_schedule())
 
         ident = keep.tile([P, P], F32, name="ident")
-        warm = keep.tile([P, 8], F32, name="warm")
-        warm_out = keep.tile([P, 8], F32, name="warm_out")
-        g_plane = keep.tile([P, TG, C], U8, name="g_plane", align_bytes=64)
-        g_codes = keep.tile([P, CH, TG, N], U32, name="g_codes", align_bytes=64)
-        p_raw = []
-        for g in range(TG):
-            p_raw.append(work.tile([P, PACK, H], BF16, name="slab", bufs=6, align_bytes=64))
-        p_codes = keep.tile([P, TG, H], U32, name="p_codes", align_bytes=64)
-        p_plane = keep.tile([P, TG, H], U8, name="p_plane", align_bytes=64)
-        m_raw = keep.tile([P, CH, HG, PACK, N], BF16, name="m_raw", align_bytes=64)
-        d_codes = keep.tile([P, CH, HG, N], U32, name="d_codes", align_bytes=64)
-        d_plane = keep.tile([P, CH, HG, N], U8, name="d_plane", align_bytes=64)
-        t_raw = keep.tile([P, QT, H], BF16, name="t_raw", align_bytes=64)
-        t_codes = keep.tile([P, QT, HG * P], U32, name="t_codes", align_bytes=64)
-        t_plane = keep.tile([P, QT, HG * P], U8, name="t_plane", align_bytes=64)
-        f_raw = keep.tile([P, QT, C], BF16, name="f_raw", align_bytes=64)
+        g_scale = keep.tile([P, T_GROUPS, C], U8, name="g_scale", align_bytes=64)
+        g_codes = keep.tile([P, T_GROUPS, C], U32, name="g_codes", align_bytes=64)
+        train_codes = keep.tile([P, T_GROUPS, H], U32, name="train_codes", align_bytes=64)
+        train_scale = keep.tile([P, T_GROUPS, H], U8, name="train_scale", align_bytes=64)
+        mult_sb = keep.tile([P, H_GROUPS, PACK, C], BF16, name="mult_sb", align_bytes=64)
+        d_codes = keep.tile([P, H_GROUPS, C], U32, name="d_codes", align_bytes=64)
+        d_scale = keep.tile([P, H_GROUPS, C], U8, name="d_scale", align_bytes=64)
+        test_sb = keep.tile([P, ROW_TILES, H], BF16, name="test_sb", align_bytes=64)
+        test_codes = keep.tile([P, ROW_TILES, H_GROUPS * P], U32, name="test_codes", align_bytes=64)
+        test_scale = keep.tile([P, ROW_TILES, H_GROUPS * P], U8, name="test_scale", align_bytes=64)
+        f0_sb = keep.tile([P, ROW_TILES, C], BF16, name="f0_sb", align_bytes=64)
 
-        g_bytes = g_words.rearrange("g p n t -> p g (n t)")
-        p_rows = phi_train.rearrange("(g p j) h -> p g j h", p=P, j=PACK)
-        m_rows = mult.rearrange("(g p j) c -> p g j c", p=P, j=PACK)
-        t_rows = phi_test.rearrange("(p j) h -> p j h", j=QT)
-        f_rows = f0.rearrange("(p j) c -> p j c", j=QT)
-        out_rows = out.rearrange("(p j) c -> p j c", j=QT)
+        def slab(shape, dtype):
+            return work.tile(shape, dtype, name="slab", bufs=ROW_TILES // 2, align_bytes=64)
 
-        tiles = {}
-        free_banks = list(range(8))
-        bank_of = {}
+        train_sb = [slab([P, PACK, H], BF16) for g in range(T_GROUPS)]
 
-        def take_bank(key):
-            b = free_banks.pop(0)
-            bank_of[key] = b
-            tiles[key] = psum.tile([P, N], F32, name="bank%d" % b)
-            return tiles[key]
+        g_view = g_words.rearrange("g p n t -> p g (n t)")
+        train_view = phi_train.rearrange("(g p j) h -> p g j h", p=P, j=PACK)
+        mult_view = mult.rearrange("(g p t) c -> p g t c", p=P, t=PACK)
+        test_view = phi_test.rearrange("(p j) h -> p j h", j=ROW_TILES)
+        f0_view = f0.rearrange("(p j) c -> p j c", j=ROW_TILES)
+        out_view = out.rearrange("(p j) c -> p j c", j=ROW_TILES)
 
-        def give_bank(key):
-            free_banks.append(bank_of[key])
+        free_banks = list(range(BANKS))
+        a_banks, turned, sums = {}, {}, []
+        squares, d_flat, d_woven, test_woven, results = {}, {}, {}, {}, {}
 
-        def copy(eng, dst, src):
-            if eng == "V":
-                nc.vector.tensor_copy(out=dst, in_=src)
-            else:
-                nc.scalar.copy(out=dst, in_=src)
+        def open_bank():
+            number = free_banks.pop(0)
+            return number, psum.tile([P, N], F32, name="bank%d" % number)
 
-        def cols(i, w=N):
-            return slice(i * w, (i + 1) * w)
-
-        def load(kind, a):
-            if kind == "S":
-                for q in range(4):
-                    nc.scalar.dma_start(
-                        out=g_plane[32 * q : 32 * q + 4, :, :].bitcast(I32),
-                        in_=g_scales[:, 4 * q : 4 * q + 4, :].rearrange("g r n -> r g n").bitcast(I32),
-                    )
-            elif kind == "P":
-                g, lo, hi = a
-                nc.sync.dma_start(out=p_raw[g][:, :, lo * KP : hi * KP], in_=p_rows[:, g, :, lo * KP : hi * KP])
-            elif kind == "G":
-                ch, lo, hi = a
+        def load(kind, *where):
+            if kind == "train":
+                g, lo, hi = where
+                part = slice(lo * K_PASS, hi * K_PASS)
+                nc.sync.dma_start(out=train_sb[g][:, :, part], in_=train_view[:, g, :, part])
+            elif kind == "g":
+                lo, hi, half = where
                 nc.sync.dma_start(
-                    out=g_codes[:, ch, lo:hi, :].bitcast(I32),
-                    in_=g_bytes[:, lo:hi, cols(ch, PACK * N)].bitcast(I32),
+                    out=g_codes[:, lo:hi, cols(half, N)].bitcast(I32),
+                    in_=g_view[:, lo:hi, cols(half, PACK * N)].bitcast(I32),
                 )
-            elif kind == "M":
-                hg, ch = a
-                nc.sync.dma_start(out=m_raw[:, ch, hg, :, :], in_=m_rows[:, hg, :, cols(ch)])
-            elif kind == "T":
-                lo, hi = a
-                nc.sync.dma_start(out=t_raw[:, lo:hi, :], in_=t_rows[:, lo:hi, :])
-            elif kind == "F":
-                lo, hi = a
-                nc.sync.dma_start(out=f_raw[:, lo:hi, :], in_=f_rows[:, lo:hi, :])
+            elif kind == "mult":
+                hg, lo, hi = where
+                nc.sync.dma_start(out=mult_sb[:, hg, :, lo * N : hi * N], in_=mult_view[:, hg, :, lo * N : hi * N])
+            elif kind == "test":
+                lo, hi = where
+                nc.sync.dma_start(out=test_sb[:, lo:hi, :], in_=test_view[:, lo:hi, :])
+            else:
+                lo, hi = where
+                nc.sync.dma_start(out=f0_sb[:, lo:hi, :], in_=f0_view[:, lo:hi, :])
 
-        def step(s):
-            kind = s[0]
-            if kind == "int":
-                eng, g, hg, lo, hi = s[1:]
-                if ("pg", g, hg) not in tiles:
-                    tiles["pg", g, hg] = work.tile([P, PACK * KP], BF16, name="p_grouped", bufs=3, align_bytes=64)
-                src = p_raw[g][:, :, cols(hg)].rearrange("p j (m t) -> p m j t", t=PACK)[:, lo:hi, :, :]
-                dst = tiles["pg", g, hg][:].rearrange("p (t m j) -> p m j t", t=PACK, j=PACK)[:, lo:hi, :, :]
-                copy(eng, dst, src)
-            elif kind == "q":
-                g, hg = s[1:]
+        def weave_train(g, hg):
+            woven = work.tile([P, PACK * K_PASS], BF16, name="train_woven", bufs=4, align_bytes=64)
+            src = train_sb[g][:, :, cols(hg, K_PASS)].rearrange("p j (m t) -> p m j t", t=PACK)
+            dst = woven[:].rearrange("p (t m j) -> p m j t", t=PACK, j=PACK)
+            nc.vector.tensor_copy(out=dst[:, :TRAIN_CUT, :, :], in_=src[:, :TRAIN_CUT, :, :])
+            if (g, hg) == (0, 0):
+                nc.scalar.activation(out=dst[:, TRAIN_CUT:, :, :], in_=src[:, TRAIN_CUT:, :, :], func=ACT.Copy)
+            else:
+                nc.scalar.copy(out=dst[:, TRAIN_CUT:, :, :], in_=src[:, TRAIN_CUT:, :, :])
+            return woven
+
+        def stage1_pass(hg, half, t, g):
+            if g == 0:
+                a_banks[hg, half, t] = open_bank()
+            features = cols(hg * PACK + t, P)
+            nc.tensor.matmul_mx(
+                out=a_banks[hg, half, t][1][:],
+                lhsT=train_codes[:, g, features].bitcast(E4M3X4),
+                lhsT_scale=train_scale[:, g, features],
+                rhs=g_codes[:, g, cols(half, N)].bitcast(E5M2X4),
+                rhs_scale=g_scale[:, g, cols(half, N)],
+                start=(g == 0),
+                stop=(g == T_GROUPS - 1),
+            )
+
+        def weave_quad(i, copy, steps):
+            if i not in d_woven:
+                d_woven[i] = work.tile([P, N, PACK], BF16, name="d_woven", bufs=2, align_bytes=64)
+            src = d_flat[i][:].rearrange("p t (c e) -> p c t e", e=PACK)
+            dst = d_woven[i][:].rearrange("p (c e) t -> p c t e", e=PACK)
+            copy(out=dst[:, steps, :, :], in_=src[:, steps, :, :])
+
+        def step(kind, i):
+            if kind == "A":
+                for g in range(T_GROUPS):
+                    stage1_pass(i // PACK, 1, i % PACK, g)
+            elif kind == "s":
+                hg, half = QUADS[i // PACK]
+                squares[i] = work.tile([P, N], F32, name="square", bufs=SQUARES_AHEAD, align_bytes=64)
+                nc.scalar.activation(out=squares[i][:], in_=mult_sb[:, hg, i % PACK, cols(half, N)], func=ACT.Square)
+            elif kind == "m":
+                quad, t = divmod(i, PACK)
+                if t == 0:
+                    d_flat[quad] = work.tile([P, PACK, N], BF16, name="d_flat", bufs=2, align_bytes=64)
+                number, bank = a_banks[QUADS[quad] + (t,)]
+                nc.vector.tensor_tensor(out=d_flat[quad][:, t, :], in0=bank[:], in1=squares[i][:], op=ALU.mult)
+                free_banks.append(number)
+            elif kind == "v":
+                weave_quad(i, nc.vector.tensor_copy, slice(0, QUAD_CUTS[i]))
+            elif kind == "w":
+                weave_quad(i, nc.scalar.copy, slice(QUAD_CUTS[i], P))
+            elif kind == "d":
+                hg, half = QUADS[i]
                 nc.vector.quantize_mx(
-                    out=p_codes[:, g, cols(hg)].bitcast(E4M3X4), scales=p_plane[:, g, cols(hg)], in_=tiles["pg", g, hg][:]
+                    out=d_codes[:, hg, cols(half, N)].bitcast(E5M2X4),
+                    scales=d_scale[:, hg, cols(half, N)],
+                    in_=d_woven[i][:].rearrange("p c t -> p (c t)"),
                 )
-            elif kind == "mm1":
-                hg, ch, t, g = s[1:]
-                acc = take_bank(("a", hg, ch, t)) if g == 0 else tiles["a", hg, ch, t]
-                w = cols(hg * PACK + t, P)
-                nc.tensor.matmul_mx(
-                    out=acc[:],
-                    lhsT=p_codes[:, g, w].bitcast(E4M3X4),
-                    lhsT_scale=p_plane[:, g, w],
-                    rhs=g_codes[:, ch, g, :].bitcast(E5M2X4),
-                    rhs_scale=g_plane[:, g, cols(ch)],
-                    start=(g == 0),
-                    stop=(g == TG - 1),
-                )
-            elif kind == "sq":
-                hg, ch, t = s[1:]
-                tiles["m2", hg, ch, t] = work.tile([P, N], F32, name="m_squared", bufs=5, align_bytes=64)
-                nc.scalar.activation(out=tiles["m2", hg, ch, t][:], in_=m_raw[:, ch, hg, t, :], func=ACT.Square)
-            elif kind == "mul":
-                hg, ch, t = s[1:]
-                if ("df", hg, ch) not in tiles:
-                    tiles["df", hg, ch] = work.tile([P, PACK, N], BF16, name="d_flat", bufs=2, align_bytes=64)
-                nc.vector.tensor_tensor(
-                    out=tiles["df", hg, ch][:, t, :], in0=tiles["a", hg, ch, t][:], in1=tiles["m2", hg, ch, t][:], op=ALU.mult
-                )
-                give_bank(("a", hg, ch, t))
-            elif kind == "di":
-                eng, hg, ch, lo, hi = s[1:]
-                if ("dg", hg, ch) not in tiles:
-                    tiles["dg", hg, ch] = work.tile([P, N, PACK], BF16, name="d_grouped", bufs=2, align_bytes=64)
-                src = tiles["df", hg, ch][:].rearrange("p t (c i) -> p c t i", i=PACK)[:, lo:hi, :, :]
-                dst = tiles["dg", hg, ch][:].rearrange("p (c i) t -> p c t i", i=PACK)[:, lo:hi, :, :]
-                copy(eng, dst, src)
-            elif kind == "dq":
-                hg, ch = s[1:]
-                nc.vector.quantize_mx(
-                    out=d_codes[:, ch, hg, :].bitcast(E5M2X4),
-                    scales=d_plane[:, ch, hg, :],
-                    in_=tiles["dg", hg, ch][:].rearrange("p c t -> p (c t)"),
-                )
-            elif kind == "tr":
-                j = s[1]
-                bank = take_bank(("x", j))
-                words = t_raw[:, j, :].bitcast(F32)
-                for hg in range(HG):
+            elif kind == "T":
+                turned[i] = open_bank()
+                words = test_sb[:, i, :].bitcast(F32)
+                for hg in range(H_GROUPS):
                     for u in range(2):
                         nc.tensor.transpose(
-                            bank[:, cols(2 * hg + u, P)], words[:, 256 * hg + u : 256 * (hg + 1) : 2], ident[:]
+                            turned[i][1][:, cols(2 * hg + u, P)], words[:, 2 * P * hg + u : 2 * P * (hg + 1) : 2], ident[:]
                         )
-            elif kind == "cp":
-                eng, j = s[1:]
-                tiles["tg", j] = work.tile([P, HG * P * PACK], BF16, name="t_grouped", bufs=4, align_bytes=64)
-                copy(
-                    eng,
-                    tiles["tg", j][:].bitcast(F32).rearrange("p (g q u) -> p g q u", g=HG, u=2),
-                    tiles["x", j][:].rearrange("p (g u q) -> p g q u", g=HG, u=2),
+            elif kind == "c":
+                number, bank = turned[i]
+                test_woven[i] = work.tile([P, H_GROUPS * K_PASS], BF16, name="test_woven", bufs=4, align_bytes=64)
+                nc.scalar.copy(
+                    out=test_woven[i][:].bitcast(F32).rearrange("p (g r u) -> p g r u", g=H_GROUPS, u=2),
+                    in_=bank[:].rearrange("p (g u r) -> p g r u", g=H_GROUPS, u=2),
                 )
-                give_bank(("x", j))
-            elif kind == "tq":
-                j = s[1]
-                nc.vector.quantize_mx(out=t_codes[:, j, :].bitcast(E4M3X4), scales=t_plane[:, j, :], in_=tiles["tg", j][:])
-            elif kind == "mm2":
-                j, ch = s[1:]
-                acc = take_bank(("k", j, ch))
-                for hg in range(HG):
+                free_banks.append(number)
+            elif kind == "q":
+                nc.vector.quantize_mx(out=test_codes[:, i, :].bitcast(E4M3X4), scales=test_scale[:, i, :], in_=test_woven[i][:])
+            elif kind in "XY":
+                half = 0 if kind == "X" else 1
+                number, bank = open_bank()
+                for hg in range(H_GROUPS):
                     nc.tensor.matmul_mx(
-                        out=acc[:],
-                        lhsT=t_codes[:, j, cols(hg, P)].bitcast(E4M3X4),
-                        lhsT_scale=t_plane[:, j, cols(hg, P)],
-                        rhs=d_codes[:, ch, hg, :].bitcast(E5M2X4),
-                        rhs_scale=d_plane[:, ch, hg, :],
+                        out=bank[:],
+                        lhsT=test_codes[:, i, cols(hg, P)].bitcast(E4M3X4),
+                        lhsT_scale=test_scale[:, i, cols(hg, P)],
+                        rhs=d_codes[:, hg, cols(half, N)].bitcast(E5M2X4),
+                        rhs_scale=d_scale[:, hg, cols(half, N)],
                         start=(hg == 0),
-                        stop=(hg == HG - 1),
+                        stop=(hg == H_GROUPS - 1),
                     )
-            elif kind == "add":
-                j, ch = s[1:]
-                if ("r", j // 2) not in tiles:
-                    tiles["r", j // 2] = work.tile([P, 2, C], F32, name="slab", bufs=6, align_bytes=64)
-                nc.vector.tensor_tensor(
-                    out=tiles["r", j // 2][:, j % 2, cols(ch)], in0=tiles["k", j, ch][:], in1=f_raw[:, j, cols(ch)], op=ALU.add
-                )
-                give_bank(("k", j, ch))
-            elif kind == "st":
-                j, lo, hi = s[1:]
-                nc.sync.dma_start(out=out_rows[:, j, lo * N : hi * N], in_=tiles["r", j // 2][:, j % 2, lo * N : hi * N])
+                sums.append((number, bank, i, half))
+            else:
+                number, bank, j, half = sums[i]
+                if j // 2 not in results:
+                    results[j // 2] = slab([P, 2, C], F32)
+                result = results[j // 2][:, j % 2, cols(half, N)]
+                nc.vector.tensor_tensor(out=result, in0=bank[:], in1=f0_sb[:, j, cols(half, N)], op=ALU.add)
+                free_banks.append(number)
+                nc.sync.dma_start(out=out_view[:, j, cols(half, N)], in_=result)
 
-        nc.vector.memset(g_plane[:].rearrange("p g n -> p (g n)").bitcast(U32), 0)
-        nc.vector.memset(warm[:], 1.0)
+        nc.vector.memset(g_scale[:].rearrange("p g n -> p (g n)").bitcast(U32), 0)
         make_identity(nc, ident[:])
-        load("S", None)
-        nc.scalar.activation(out=warm_out[:], in_=warm[:], func=ACT.Square)
-        loads, steps = schedule()
-        for kind, a in loads:
-            load(kind, a)
-        for s in steps:
-            step(s)
+        for quadrant in range(4):
+            nc.scalar.dma_start(
+                out=g_scale[32 * quadrant : 32 * quadrant + 4, :, :].bitcast(I32),
+                in_=g_scales[:, 4 * quadrant : 4 * quadrant + 4, :].rearrange("g r n -> r g n").bitcast(I32),
+            )
+        for entry in LOADS:
+            load(*entry)
+
+        pieces = [(g, hg) for g in range(T_GROUPS) for hg in range(H_GROUPS)]
+        woven = [weave_train(*pieces[0])]
+        for i, (g, hg) in enumerate(pieces):
+            if i + 1 < len(pieces):
+                woven.append(weave_train(*pieces[i + 1]))
+            nc.vector.quantize_mx(
+                out=train_codes[:, g, cols(hg, K_PASS)].bitcast(E4M3X4),
+                scales=train_scale[:, g, cols(hg, K_PASS)],
+                in_=woven[i][:],
+            )
+            for t in range(PACK):
+                stage1_pass(hg, 0, t, g)
+
+        for kind, i in merged_order():
+            step(kind, i)

@@ -31,8 +31,7 @@ TRAIN_CUT = 68
 QUAD_CUTS = [96, 112, 32, 16]
 
 LOADS = [
-    ("train", 0, 0, 1), ("train", 0, 1, 2), ("train", 1, 0, 2), ("g", 0, 1, 0),
-    ("train", 2, 0, 2), ("g", 1, 2, 0), ("train", 3, 0, 2), ("g", 2, 3, 0),
+    ("train", 0), ("train", 1), ("g", 0, 1, 0), ("train", 2), ("g", 1, 2, 0), ("train", 3), ("g", 2, 3, 0),
     ("mult", 0, 0, 1), ("g", 3, 4, 0), ("g", 0, 4, 1), ("mult", 1, 0, 2), ("mult", 0, 1, 2),
     ("test", 0, 4), ("f0", 0, 4), ("test", 4, 8), ("f0", 4, 8), ("test", 8, 12), ("f0", 8, 12),
 ]
@@ -127,9 +126,8 @@ def tile_readout_ntk_step_e3_kernel(tc, g_words, g_scales, phi_train, mult, phi_
 
         def load(kind, *where):
             if kind == "train":
-                g, lo, hi = where
-                part = slice(lo * K_PASS, hi * K_PASS)
-                nc.sync.dma_start(out=train_sb[g][:, :, part], in_=train_view[:, g, :, part])
+                g = where[0]
+                nc.sync.dma_start(out=train_sb[g][:], in_=train_view[:, g, :, :])
             elif kind == "g":
                 lo, hi, half = where
                 nc.sync.dma_start(
@@ -247,10 +245,10 @@ def tile_readout_ntk_step_e3_kernel(tc, g_words, g_scales, phi_train, mult, phi_
 
         nc.vector.memset(g_scale[:].rearrange("p g n -> p (g n)").bitcast(U32), 0)
         make_identity(nc, ident[:])
-        for quadrant in range(4):
+        for r in range(4):
             nc.scalar.dma_start(
-                out=g_scale[32 * quadrant : 32 * quadrant + 4, :, :].bitcast(I32),
-                in_=g_scales[:, 4 * quadrant : 4 * quadrant + 4, :].rearrange("g r n -> r g n").bitcast(I32),
+                out=g_scale[r:P:32, :, :].bitcast(I32),
+                in_=g_scales[:, r:16:4, :].rearrange("g q n -> q g n").bitcast(I32),
             )
         for entry in LOADS:
             load(*entry)

@@ -24,63 +24,35 @@ BANKS = 8
 T_GROUPS = T // K_PASS
 H_GROUPS = H // K_PASS
 ROW_TILES = Q // P
+LOAD_TILES = 4
 
 QUADS = [(0, 0), (1, 0), (0, 1), (1, 1)]
 
-TRAIN_CUT = 68
-QUAD_CUTS = [96, 112, 32, 16]
-
-LOADS = [
-    ("train", 0), ("train", 1), ("g", 0, 1, 0), ("train", 2), ("g", 1, 2, 0), ("train", 3), ("g", 2, 3, 0),
-    ("mult", 0, 0, 1), ("g", 3, 4, 0), ("g", 0, 4, 1), ("mult", 1, 0, 2), ("mult", 0, 1, 2),
-    ("test", 0, 4), ("f0", 0, 4), ("test", 4, 8), ("f0", 4, 8), ("test", 8, 12), ("f0", 8, 12),
-]
-
-TENSOR_ORDER = "AAAAAA TTTT AA XX TTT XXXX TTT YYY X YYYY X TT XY XY XY Y XY"
-VECTOR_ORDER = "mmmm vd mmmm mv mmm md qq mq mv am qa qq av da d aa qq aaaaaaa qq aa q aaaaa q aaaa"
-SCALAR_ORDER = "ssss w ssss ssss ss w c s c s cc w cc w cccccc"
-
-SQUARES_AHEAD = 6
-
-
-def merged_order():
-    queues = [list(order.replace(" ", "")) for order in (TENSOR_ORDER, SCALAR_ORDER, VECTOR_ORDER)]
-    count = {kind: 0 for kind in "ATXYsmvwdcqa"}
-    free = 0
-    steps = []
-
-    def ready(kind):
-        i = count[kind]
-        needs = {
-            "A": free > 0,
-            "T": free > 0,
-            "X": free > 0 and count["q"] > i and count["d"] >= H_GROUPS,
-            "Y": free > 0 and count["q"] > i and count["d"] >= len(QUADS),
-            "s": i - count["m"] < SQUARES_AHEAD,
-            "m": count["s"] > i and count["A"] > i - BANKS,
-            "v": count["m"] >= PACK * (i + 1),
-            "w": count["m"] >= PACK * (i + 1),
-            "d": count["v"] > i and count["w"] > i,
-            "c": count["T"] > i,
-            "q": count["c"] > i,
-            "a": count["X"] + count["Y"] > i,
-        }
-        return needs[kind]
-
-    while any(queues):
-        before = len(steps)
-        for queue in queues:
-            if queue and ready(queue[0]):
-                kind = queue.pop(0)
-                steps.append((kind, count[kind]))
-                count[kind] += 1
-                free += (kind in "mca") - (kind in "ATXY")
-        assert len(steps) > before
-    return steps
+TRAIN_CUT = 64
+QUAD_CUTS = [128, 96, 64, 40]
+SQUARES_AHEAD = 2
+EARLY_BANKS = 2
+SORTED_FROM = 8
+Q_LAG = 1
 
 
 def cols(i, width):
     return slice(i * width, (i + 1) * width)
+
+
+def tensor_steps():
+    a = [("A", i) for i in range(BANKS)]
+    t = [("T", j) for j in range(ROW_TILES)]
+    x = [("S", j, 0) for j in range(ROW_TILES)]
+    y = [("S", j, 1) for j in range(ROW_TILES)]
+    steps = a[:6]
+    for pair, between in enumerate((a[6:7], a[7:8] + x[0:2], x[2:4], y[0:4])):
+        steps += t[2 * pair : 2 * pair + 2] + between
+    for j in range(4, ROW_TILES):
+        if j == SORTED_FROM - 2:
+            steps += t[SORTED_FROM:]
+        steps += [x[j], y[j]]
+    return steps
 
 
 def tile_readout_ntk_step_e3_kernel(tc, g_words, g_scales, phi_train, mult, phi_test, f0, out):
@@ -91,23 +63,26 @@ def tile_readout_ntk_step_e3_kernel(tc, g_words, g_scales, phi_train, mult, phi_
         psum = ctx.enter_context(tc.psum_pool(name="psum", bufs=1))
         ctx.enter_context(tc.manual_schedule())
 
-        ident = keep.tile([P, P], F32, name="ident")
-        g_scale = keep.tile([P, T_GROUPS, C], U8, name="g_scale", align_bytes=64)
-        g_codes = keep.tile([P, T_GROUPS, C], U32, name="g_codes", align_bytes=64)
-        train_codes = keep.tile([P, T_GROUPS, H], U32, name="train_codes", align_bytes=64)
-        train_scale = keep.tile([P, T_GROUPS, H], U8, name="train_scale", align_bytes=64)
-        mult_sb = keep.tile([P, H_GROUPS, PACK, C], BF16, name="mult_sb", align_bytes=64)
-        d_codes = keep.tile([P, H_GROUPS, C], U32, name="d_codes", align_bytes=64)
-        d_scale = keep.tile([P, H_GROUPS, C], U8, name="d_scale", align_bytes=64)
-        test_sb = keep.tile([P, ROW_TILES, H], BF16, name="test_sb", align_bytes=64)
-        test_codes = keep.tile([P, ROW_TILES, H_GROUPS * P], U32, name="test_codes", align_bytes=64)
-        test_scale = keep.tile([P, ROW_TILES, H_GROUPS * P], U8, name="test_scale", align_bytes=64)
-        f0_sb = keep.tile([P, ROW_TILES, C], BF16, name="f0_sb", align_bytes=64)
+        def kept(name, shape, dtype):
+            return keep.tile(shape, dtype, name=name, align_bytes=64)
 
         def slab(shape, dtype):
-            return work.tile(shape, dtype, name="slab", bufs=ROW_TILES // 2, align_bytes=64)
+            return work.tile(shape, dtype, name="slab", bufs=4, align_bytes=64)
 
-        train_sb = [slab([P, PACK, H], BF16) for g in range(T_GROUPS)]
+        ident = kept("ident", [P, P], F32)
+        g_scale = [kept("g_scale%d" % half, [P, T_GROUPS, N], U8) for half in range(2)]
+        g_codes = [kept("g_codes%d" % half, [P, T_GROUPS, N], U32) for half in range(2)]
+        train_codes = kept("train_codes", [P, T_GROUPS, H], U32)
+        train_scale = kept("train_scale", [P, T_GROUPS, H], U8)
+        mult_sb = [kept("mult%d" % quad, [P, PACK, N], BF16) for quad in range(len(QUADS))]
+        d_codes = kept("d_codes", [P, H_GROUPS, C], U32)
+        d_scale = kept("d_scale", [P, H_GROUPS, C], U8)
+        test_sb = [kept("test%d" % i, [P, LOAD_TILES, H], BF16) for i in range(ROW_TILES // LOAD_TILES)]
+        f0_sb = [kept("f0_%d" % i, [P, LOAD_TILES, C], BF16) for i in range(ROW_TILES // LOAD_TILES)]
+        test_codes = kept("test_codes", [P, ROW_TILES, H_GROUPS * P], U32)
+        test_scale = kept("test_scale", [P, ROW_TILES, H_GROUPS * P], U8)
+        train_sb = [slab([P, PACK, H], BF16) for g in range(T_GROUPS - 1)]
+        train_last = [kept("train_last%d" % hg, [P, PACK, K_PASS], BF16) for hg in range(H_GROUPS)]
 
         g_view = g_words.rearrange("g p n t -> p g (n t)")
         train_view = phi_train.rearrange("(g p j) h -> p g j h", p=P, j=PACK)
@@ -116,37 +91,45 @@ def tile_readout_ntk_step_e3_kernel(tc, g_words, g_scales, phi_train, mult, phi_
         f0_view = f0.rearrange("(p j) c -> p j c", j=ROW_TILES)
         out_view = out.rearrange("(p j) c -> p j c", j=ROW_TILES)
 
-        free_banks = list(range(BANKS))
-        a_banks, turned, sums = {}, {}, []
-        squares, d_flat, d_woven, test_woven, results = {}, {}, {}, {}, {}
+        banks = []
+        a_banks, squares, d_flat, d_woven, in_order, test_woven, results = {}, {}, {}, {}, {}, {}, {}
 
         def open_bank():
-            number = free_banks.pop(0)
-            return number, psum.tile([P, N], F32, name="bank%d" % number)
+            banks.append(psum.tile([P, N], F32, name="bank%d" % (len(banks) % BANKS)))
+            return banks[-1]
 
-        def load(kind, *where):
-            if kind == "train":
-                g = where[0]
-                nc.sync.dma_start(out=train_sb[g][:], in_=train_view[:, g, :, :])
-            elif kind == "g":
-                lo, hi, half = where
+        def load_train(g):
+            nc.sync.dma_start(out=train_sb[g][:], in_=train_view[:, g, :, :])
+
+        def load_train_last(hg):
+            nc.sync.dma_start(out=train_last[hg][:], in_=train_view[:, T_GROUPS - 1, :, cols(hg, K_PASS)])
+
+        def load_g(lo, hi, half):
+            nc.sync.dma_start(
+                out=g_codes[half][:, lo:hi, :].bitcast(I32), in_=g_view[:, lo:hi, cols(half, PACK * N)].bitcast(I32)
+            )
+
+        def load_g_scale(half):
+            for r in range(4):
                 nc.sync.dma_start(
-                    out=g_codes[:, lo:hi, cols(half, N)].bitcast(I32),
-                    in_=g_view[:, lo:hi, cols(half, PACK * N)].bitcast(I32),
+                    out=g_scale[half][r:P:32, :, :].bitcast(I32),
+                    in_=g_scales[:, r:16:4, cols(half, N)].rearrange("g q n -> q g n").bitcast(I32),
                 )
-            elif kind == "mult":
-                hg, lo, hi = where
-                nc.sync.dma_start(out=mult_sb[:, hg, :, lo * N : hi * N], in_=mult_view[:, hg, :, lo * N : hi * N])
-            elif kind == "test":
-                lo, hi = where
-                nc.sync.dma_start(out=test_sb[:, lo:hi, :], in_=test_view[:, lo:hi, :])
-            else:
-                lo, hi = where
-                nc.sync.dma_start(out=f0_sb[:, lo:hi, :], in_=f0_view[:, lo:hi, :])
+
+        def load_mult(quad, lo, hi):
+            hg, half = QUADS[quad]
+            nc.sync.dma_start(out=mult_sb[quad][:, lo:hi, :], in_=mult_view[:, hg, lo:hi, cols(half, N)])
+
+        def load_test(i):
+            nc.sync.dma_start(out=test_sb[i][:], in_=test_view[:, cols(i, LOAD_TILES), :])
+
+        def load_f0(i):
+            nc.sync.dma_start(out=f0_sb[i][:], in_=f0_view[:, cols(i, LOAD_TILES), :])
 
         def weave_train(g, hg):
-            woven = work.tile([P, PACK * K_PASS], BF16, name="train_woven", bufs=4, align_bytes=64)
-            src = train_sb[g][:, :, cols(hg, K_PASS)].rearrange("p j (m t) -> p m j t", t=PACK)
+            woven = work.tile([P, PACK * K_PASS], BF16, name="train_woven", bufs=3, align_bytes=64)
+            raw = train_last[hg][:] if g == T_GROUPS - 1 else train_sb[g][:, :, cols(hg, K_PASS)]
+            src = raw.rearrange("p j (m t) -> p m j t", t=PACK)
             dst = woven[:].rearrange("p (t m j) -> p m j t", t=PACK, j=PACK)
             nc.vector.tensor_copy(out=dst[:, :TRAIN_CUT, :, :], in_=src[:, :TRAIN_CUT, :, :])
             if (g, hg) == (0, 0):
@@ -155,103 +138,131 @@ def tile_readout_ntk_step_e3_kernel(tc, g_words, g_scales, phi_train, mult, phi_
                 nc.scalar.copy(out=dst[:, TRAIN_CUT:, :, :], in_=src[:, TRAIN_CUT:, :, :])
             return woven
 
-        def stage1_pass(hg, half, t, g):
+        def stage1_pass(i, g):
+            hg, half = QUADS[i // PACK]
             if g == 0:
-                a_banks[hg, half, t] = open_bank()
-            features = cols(hg * PACK + t, P)
+                a_banks[i] = open_bank()
+            features = cols(hg * PACK + i % PACK, P)
             nc.tensor.matmul_mx(
-                out=a_banks[hg, half, t][1][:],
+                out=a_banks[i][:],
                 lhsT=train_codes[:, g, features].bitcast(E4M3X4),
                 lhsT_scale=train_scale[:, g, features],
-                rhs=g_codes[:, g, cols(half, N)].bitcast(E5M2X4),
-                rhs_scale=g_scale[:, g, cols(half, N)],
+                rhs=g_codes[half][:, g, :].bitcast(E5M2X4),
+                rhs_scale=g_scale[half][:, g, :],
                 start=(g == 0),
                 stop=(g == T_GROUPS - 1),
             )
 
-        def weave_quad(i, copy, steps):
-            if i not in d_woven:
-                d_woven[i] = work.tile([P, N, PACK], BF16, name="d_woven", bufs=2, align_bytes=64)
-            src = d_flat[i][:].rearrange("p t (c e) -> p c t e", e=PACK)
-            dst = d_woven[i][:].rearrange("p (c e) t -> p c t e", e=PACK)
-            copy(out=dst[:, steps, :, :], in_=src[:, steps, :, :])
+        def square(i):
+            squares[i] = work.tile([P, N], F32, name="square", bufs=SQUARES_AHEAD + 2, align_bytes=64)
+            nc.scalar.activation(out=squares[i][:], in_=mult_sb[i // PACK][:, i % PACK, :], func=ACT.Square)
 
-        def step(kind, i):
-            if kind == "A":
-                for g in range(T_GROUPS):
-                    stage1_pass(i // PACK, 1, i % PACK, g)
-            elif kind == "s":
-                hg, half = QUADS[i // PACK]
-                squares[i] = work.tile([P, N], F32, name="square", bufs=SQUARES_AHEAD, align_bytes=64)
-                nc.scalar.activation(out=squares[i][:], in_=mult_sb[:, hg, i % PACK, cols(half, N)], func=ACT.Square)
-            elif kind == "m":
-                quad, t = divmod(i, PACK)
-                if t == 0:
-                    d_flat[quad] = work.tile([P, PACK, N], BF16, name="d_flat", bufs=2, align_bytes=64)
-                number, bank = a_banks[QUADS[quad] + (t,)]
-                nc.vector.tensor_tensor(out=d_flat[quad][:, t, :], in0=bank[:], in1=squares[i][:], op=ALU.mult)
-                free_banks.append(number)
-            elif kind == "v":
-                weave_quad(i, nc.vector.tensor_copy, slice(0, QUAD_CUTS[i]))
-            elif kind == "w":
-                weave_quad(i, nc.scalar.copy, slice(QUAD_CUTS[i], P))
-            elif kind == "d":
-                hg, half = QUADS[i]
-                nc.vector.quantize_mx(
-                    out=d_codes[:, hg, cols(half, N)].bitcast(E5M2X4),
-                    scales=d_scale[:, hg, cols(half, N)],
-                    in_=d_woven[i][:].rearrange("p c t -> p (c t)"),
-                )
-            elif kind == "T":
-                turned[i] = open_bank()
-                words = test_sb[:, i, :].bitcast(F32)
-                for hg in range(H_GROUPS):
-                    for u in range(2):
-                        nc.tensor.transpose(
-                            turned[i][1][:, cols(2 * hg + u, P)], words[:, 2 * P * hg + u : 2 * P * (hg + 1) : 2], ident[:]
-                        )
-            elif kind == "c":
-                number, bank = turned[i]
-                test_woven[i] = work.tile([P, H_GROUPS * K_PASS], BF16, name="test_woven", bufs=4, align_bytes=64)
-                nc.scalar.copy(
-                    out=test_woven[i][:].bitcast(F32).rearrange("p (g r u) -> p g r u", g=H_GROUPS, u=2),
-                    in_=bank[:].rearrange("p (g u r) -> p g r u", g=H_GROUPS, u=2),
-                )
-                free_banks.append(number)
-            elif kind == "q":
-                nc.vector.quantize_mx(out=test_codes[:, i, :].bitcast(E4M3X4), scales=test_scale[:, i, :], in_=test_woven[i][:])
-            elif kind in "XY":
-                half = 0 if kind == "X" else 1
-                number, bank = open_bank()
-                for hg in range(H_GROUPS):
-                    nc.tensor.matmul_mx(
-                        out=bank[:],
-                        lhsT=test_codes[:, i, cols(hg, P)].bitcast(E4M3X4),
-                        lhsT_scale=test_scale[:, i, cols(hg, P)],
-                        rhs=d_codes[:, hg, cols(half, N)].bitcast(E5M2X4),
-                        rhs_scale=d_scale[:, hg, cols(half, N)],
-                        start=(hg == 0),
-                        stop=(hg == H_GROUPS - 1),
-                    )
-                sums.append((number, bank, i, half))
-            else:
-                number, bank, j, half = sums[i]
-                if j // 2 not in results:
-                    results[j // 2] = slab([P, 2, C], F32)
-                result = results[j // 2][:, j % 2, cols(half, N)]
-                nc.vector.tensor_tensor(out=result, in0=bank[:], in1=f0_sb[:, j, cols(half, N)], op=ALU.add)
-                free_banks.append(number)
-                nc.sync.dma_start(out=out_view[:, j, cols(half, N)], in_=result)
+        def multiply(i):
+            quad, t = divmod(i, PACK)
+            if t == 0:
+                d_flat[quad] = work.tile([P, PACK, N], BF16, name="d_flat", bufs=3, align_bytes=64)
+            nc.vector.tensor_tensor(out=d_flat[quad][:, t, :], in0=a_banks[i][:], in1=squares[i][:], op=ALU.mult)
 
-        nc.vector.memset(g_scale[:].rearrange("p g n -> p (g n)").bitcast(U32), 0)
-        make_identity(nc, ident[:])
-        for r in range(4):
-            nc.scalar.dma_start(
-                out=g_scale[r:P:32, :, :].bitcast(I32),
-                in_=g_scales[:, r:16:4, :].rearrange("g q n -> q g n").bitcast(I32),
+        def weave_d(quad, copy, part):
+            if quad not in d_woven:
+                d_woven[quad] = work.tile([P, N, PACK], BF16, name="d_woven", bufs=2, align_bytes=64)
+            if part.start < part.stop:
+                src = d_flat[quad][:].rearrange("p t (c e) -> p c t e", e=PACK)
+                dst = d_woven[quad][:].rearrange("p (c e) t -> p c t e", e=PACK)
+                copy(out=dst[:, part, :, :], in_=src[:, part, :, :])
+
+        def weave_d_vector(quad):
+            weave_d(quad, nc.vector.tensor_copy, slice(0, QUAD_CUTS[quad]))
+
+        def weave_d_scalar(quad):
+            weave_d(quad, nc.scalar.copy, slice(QUAD_CUTS[quad], P))
+
+        def quantise_d(quad):
+            hg, half = QUADS[quad]
+            nc.vector.quantize_mx(
+                out=d_codes[:, hg, cols(half, N)].bitcast(E5M2X4),
+                scales=d_scale[:, hg, cols(half, N)],
+                in_=d_woven[quad][:].rearrange("p c t -> p (c t)"),
             )
-        for entry in LOADS:
-            load(*entry)
+
+        def test_words(j):
+            return test_sb[j // LOAD_TILES][:, j % LOAD_TILES, :].bitcast(F32)
+
+        def sort_words(j):
+            in_order[j] = work.tile([P, H // 2], F32, name="in_order", bufs=ROW_TILES - SORTED_FROM, align_bytes=64)
+            nc.scalar.copy(
+                out=in_order[j][:].rearrange("p (g u r) -> p g r u", g=H_GROUPS, u=2),
+                in_=test_words(j).rearrange("p (g r u) -> p g r u", g=H_GROUPS, u=2),
+            )
+
+        def turn(j):
+            bank = open_bank()
+            for hg in range(H_GROUPS):
+                for u in range(2):
+                    if j in in_order:
+                        words = in_order[j][:, cols(2 * hg + u, P)]
+                    else:
+                        words = test_words(j)[:, 2 * P * hg + u : 2 * P * (hg + 1) : 2]
+                    nc.tensor.transpose(bank[:, cols(2 * hg + u, P)], words, ident[:])
+
+        def copy_turned(j, bank):
+            test_woven[j] = work.tile([P, H], BF16, name="test_woven", bufs=4, align_bytes=64)
+            nc.scalar.copy(
+                out=test_woven[j][:].bitcast(F32).rearrange("p (g r u) -> p g r u", g=H_GROUPS, u=2),
+                in_=bank[:].rearrange("p (g u r) -> p g r u", g=H_GROUPS, u=2),
+            )
+
+        def quantise_test(j):
+            nc.vector.quantize_mx(out=test_codes[:, j, :].bitcast(E4M3X4), scales=test_scale[:, j, :], in_=test_woven[j][:])
+
+        def stage2(j, half):
+            bank = open_bank()
+            for hg in range(H_GROUPS):
+                nc.tensor.matmul_mx(
+                    out=bank[:],
+                    lhsT=test_codes[:, j, cols(hg, P)].bitcast(E4M3X4),
+                    lhsT_scale=test_scale[:, j, cols(hg, P)],
+                    rhs=d_codes[:, hg, cols(half, N)].bitcast(E5M2X4),
+                    rhs_scale=d_scale[:, hg, cols(half, N)],
+                    start=(hg == 0),
+                    stop=(hg == H_GROUPS - 1),
+                )
+
+        def add_and_store(j, half, bank):
+            if j // 2 not in results:
+                results[j // 2] = slab([P, 2, C], F32)
+            result = results[j // 2][:, j % 2, cols(half, N)]
+            f0_part = f0_sb[j // LOAD_TILES][:, j % LOAD_TILES, cols(half, N)]
+            nc.vector.tensor_tensor(out=result, in0=bank[:], in1=f0_part, op=ALU.add)
+            nc.sync.dma_start(out=out_view[:, j, cols(half, N)], in_=result)
+
+        for half in range(2):
+            nc.vector.memset(g_scale[half][:].rearrange("p g n -> p (g n)").bitcast(U32), 0)
+        make_identity(nc, ident[:])
+
+        load_train(0)
+        load_train(1)
+        load_g_scale(0)
+        load_g(0, 1, 0)
+        load_train(2)
+        load_g(1, 2, 0)
+        load_train_last(0)
+        load_g(2, 3, 0)
+        load_train_last(1)
+        load_g(3, 4, 0)
+        load_mult(0, 0, 2)
+        load_mult(0, 2, 4)
+        load_g_scale(1)
+        load_g(0, 2, 1)
+        load_g(2, 4, 1)
+        load_mult(1, 0, 4)
+        load_mult(2, 0, 4)
+        load_test(0)
+        load_mult(3, 0, 4)
+        load_f0(0)
+        for i in range(1, ROW_TILES // LOAD_TILES):
+            load_test(i)
+            load_f0(i)
 
         pieces = [(g, hg) for g in range(T_GROUPS) for hg in range(H_GROUPS)]
         woven = [weave_train(*pieces[0])]
@@ -264,7 +275,53 @@ def tile_readout_ntk_step_e3_kernel(tc, g_words, g_scales, phi_train, mult, phi_
                 in_=woven[i][:],
             )
             for t in range(PACK):
-                stage1_pass(hg, 0, t, g)
+                stage1_pass(hg * PACK + t, g)
 
-        for kind, i in merged_order():
-            step(kind, i)
+        steps = [("A", i - BANKS) for i in range(BANKS)] + tensor_steps()
+        place = {step: n for n, step in enumerate(steps)}
+        last_a = place["A", BANKS - 1]
+        later = {}
+
+        def at(n, work_item, *args):
+            later.setdefault(n, []).append((work_item, args))
+
+        for i in range(2 * BANKS):
+            at(max(place["A", i - BANKS] - SQUARES_AHEAD, 0) - 1, square, i)
+        for j in range(SORTED_FROM, ROW_TILES):
+            at(place["T", SORTED_FROM - 1], sort_words, j)
+        for j in range(ROW_TILES):
+            at(place["T", j] + Q_LAG * (j >= 4), quantise_test, j)
+        at(3, weave_d_vector, 0)
+        at(3, weave_d_scalar, 0)
+        at(3, quantise_d, 0)
+        at(7, weave_d_scalar, 1)
+        at(8, weave_d_vector, 1)
+        at(9, quantise_d, 1)
+        at(last_a - 3, weave_d_vector, 2)
+        at(last_a - 1, weave_d_scalar, 2)
+        at(last_a, weave_d_scalar, 3)
+        at(last_a + 1, quantise_d, 2)
+        at(last_a + 1, weave_d_vector, 3)
+        at(last_a + 2, quantise_d, 3)
+
+        for work_item, args in later.get(-1, []):
+            work_item(*args)
+        for n, step in enumerate(steps):
+            if step[0] == "A":
+                i = step[1] + BANKS
+                if i == BANKS:
+                    for early in range(EARLY_BANKS):
+                        for g in range(2):
+                            stage1_pass(BANKS + early, g)
+                if i >= BANKS:
+                    for g in range(2 if i < BANKS + EARLY_BANKS else 0, T_GROUPS):
+                        stage1_pass(i, g)
+                multiply(i)
+            elif step[0] == "T":
+                turn(step[1])
+                copy_turned(step[1], banks[n])
+            else:
+                stage2(step[1], step[2])
+                add_and_store(step[1], step[2], banks[n])
+            for work_item, args in later.get(n, []):
+                work_item(*args)

@@ -29,8 +29,28 @@ LOAD_TILES = 4
 QUADS = [(0, 0), (1, 0), (0, 1), (1, 1)]
 
 TRAIN_CUT = 64
-QUAD_CUTS = [128, 96, 64, 40]
+QUAD_CUTS = [128,0,0,48]
+S_CUTS = [128,0,128,128]
+WTAG = [0,1,0,1]
+D1_AT = 12
+W1_AT = 7
+V1_AT = 8
+W3_AT = 0
+PE = "AAAAA TT A TT AA XX TT XX TT YYYY XY XY TTTT XY XY XY XY XY XY"
+SHARED = []
+STORE_LAG = 2
+Q_AT = [0,1,2,2,1,1]
+SORT_AT = -9
 SQUARES_AHEAD = 2
+SQ = 2
+QW = 2
+A_FIRST = 6
+V2_AT = -3
+W2_AT = -2
+D2_AT = 1
+V3_AT = 1
+D3_AT = 2
+PAIR_FROM = 12
 EARLY_BANKS = 2
 SORTED_FROM = 8
 Q_LAG = 1
@@ -41,17 +61,11 @@ def cols(i, width):
 
 
 def tensor_steps():
-    a = [("A", i) for i in range(BANKS)]
-    t = [("T", j) for j in range(ROW_TILES)]
-    x = [("S", j, 0) for j in range(ROW_TILES)]
-    y = [("S", j, 1) for j in range(ROW_TILES)]
-    steps = a[:6]
-    for pair, between in enumerate((a[6:7], a[7:8] + x[0:2], x[2:4], y[0:4])):
-        steps += t[2 * pair : 2 * pair + 2] + between
-    for j in range(4, ROW_TILES):
-        if j == SORTED_FROM - 2:
-            steps += t[SORTED_FROM:]
-        steps += [x[j], y[j]]
+    n = {"A": 0, "T": 0, "X": 0, "Y": 0}
+    steps = []
+    for k in PE.replace(" ", ""):
+        steps.append((k, n[k]) if k in "AT" else ("S", n[k], "XY".index(k)))
+        n[k] += 1
     return steps
 
 
@@ -67,12 +81,10 @@ def tile_readout_ntk_step_e3_kernel(tc, g_words, g_scales, phi_train, mult, phi_
             return keep.tile(shape, dtype, name=name, align_bytes=64)
 
         def slab(shape, dtype):
-            return work.tile(shape, dtype, name="slab", bufs=4, align_bytes=64)
+            return work.tile(shape, dtype, name="slab", bufs=7, align_bytes=64)
 
         ident = kept("ident", [P, P], F32)
         g_scale = [kept("g_scale%d" % half, [P, T_GROUPS, N], U8) for half in range(2)]
-        g_codes = [kept("g_codes%d" % half, [P, T_GROUPS, N], U32) for half in range(2)]
-        train_codes = kept("train_codes", [P, T_GROUPS, H], U32)
         train_scale = kept("train_scale", [P, T_GROUPS, H], U8)
         mult_sb = [kept("mult%d" % quad, [P, PACK, N], BF16) for quad in range(len(QUADS))]
         d_codes = kept("d_codes", [P, H_GROUPS, C], U32)
@@ -82,6 +94,8 @@ def tile_readout_ntk_step_e3_kernel(tc, g_words, g_scales, phi_train, mult, phi_
         test_codes = kept("test_codes", [P, ROW_TILES, H_GROUPS * P], U32)
         test_scale = kept("test_scale", [P, ROW_TILES, H_GROUPS * P], U8)
         train_sb = [slab([P, PACK, H], BF16) for g in range(T_GROUPS - 1)]
+        g_codes = [slab([P, T_GROUPS, N], U32) for half in range(2)]
+        train_codes = [slab([P, T_GROUPS, K_PASS], U32) for hg in range(H_GROUPS)]
         train_last = [kept("train_last%d" % hg, [P, PACK, K_PASS], BF16) for hg in range(H_GROUPS)]
 
         g_view = g_words.rearrange("g p n t -> p g (n t)")
@@ -145,7 +159,7 @@ def tile_readout_ntk_step_e3_kernel(tc, g_words, g_scales, phi_train, mult, phi_
             features = cols(hg * PACK + i % PACK, P)
             nc.tensor.matmul_mx(
                 out=a_banks[i][:],
-                lhsT=train_codes[:, g, features].bitcast(E4M3X4),
+                lhsT=train_codes[hg][:, g, cols(i % PACK, P)].bitcast(E4M3X4),
                 lhsT_scale=train_scale[:, g, features],
                 rhs=g_codes[half][:, g, :].bitcast(E5M2X4),
                 rhs_scale=g_scale[half][:, g, :],
@@ -154,18 +168,20 @@ def tile_readout_ntk_step_e3_kernel(tc, g_words, g_scales, phi_train, mult, phi_
             )
 
         def square(i):
-            squares[i] = work.tile([P, N], F32, name="square", bufs=SQUARES_AHEAD + 2, align_bytes=64)
-            nc.scalar.activation(out=squares[i][:], in_=mult_sb[i // PACK][:, i % PACK, :], func=ACT.Square)
+            tile = work.tile([P, SQ, N], F32, name="square", bufs=SQUARES_AHEAD // SQ + 2, align_bytes=64)
+            nc.scalar.activation(out=tile[:], in_=mult_sb[i // PACK][:, i % PACK : i % PACK + SQ, :], func=ACT.Square)
+            for k in range(SQ):
+                squares[i + k] = tile[:, k, :]
 
         def multiply(i):
             quad, t = divmod(i, PACK)
             if t == 0:
                 d_flat[quad] = work.tile([P, PACK, N], BF16, name="d_flat", bufs=3, align_bytes=64)
-            nc.vector.tensor_tensor(out=d_flat[quad][:, t, :], in0=a_banks[i][:], in1=squares[i][:], op=ALU.mult)
+            nc.vector.tensor_tensor(out=d_flat[quad][:, t, :], in0=a_banks[i][:], in1=squares[i], op=ALU.mult)
 
         def weave_d(quad, copy, part):
             if quad not in d_woven:
-                d_woven[quad] = work.tile([P, N, PACK], BF16, name="d_woven", bufs=2, align_bytes=64)
+                d_woven[quad] = work.tile([P, N, PACK], BF16, name="d_woven%d" % WTAG[quad], bufs=1, align_bytes=64)
             if part.start < part.stop:
                 src = d_flat[quad][:].rearrange("p t (c e) -> p c t e", e=PACK)
                 dst = d_woven[quad][:].rearrange("p (c e) t -> p c t e", e=PACK)
@@ -175,7 +191,16 @@ def tile_readout_ntk_step_e3_kernel(tc, g_words, g_scales, phi_train, mult, phi_
             weave_d(quad, nc.vector.tensor_copy, slice(0, QUAD_CUTS[quad]))
 
         def weave_d_scalar(quad):
-            weave_d(quad, nc.scalar.copy, slice(QUAD_CUTS[quad], P))
+            weave_d(quad, nc.scalar.copy, slice(QUAD_CUTS[quad], S_CUTS[quad]))
+
+        def gpsimd_copy(out, in_):
+            nc.gpsimd.tensor_scalar(out=out, in0=in_, scalar1=1.0, scalar2=0.0, op0=ALU.mult, op1=ALU.add)
+
+        def weave_d_gpsimd(quad):
+            weave_d(quad, None, slice(0, 0))
+            part = slice(PACK * S_CUTS[quad], N)
+            if part.start < part.stop:
+                gpsimd_copy(d_woven[quad][:, part, :], d_flat[quad][:, :, part].rearrange("p t c -> p c t"))
 
         def quantise_d(quad):
             hg, half = QUADS[quad]
@@ -206,14 +231,19 @@ def tile_readout_ntk_step_e3_kernel(tc, g_words, g_scales, phi_train, mult, phi_
                     nc.tensor.transpose(bank[:, cols(2 * hg + u, P)], words, ident[:])
 
         def copy_turned(j, bank):
-            test_woven[j] = work.tile([P, H], BF16, name="test_woven", bufs=4, align_bytes=64)
+            if j % QW == 0:
+                test_woven[j // QW] = work.tile([P, QW, H], BF16, name="test_woven", bufs=4 // QW + (QW == 4), align_bytes=64)
             nc.scalar.copy(
-                out=test_woven[j][:].bitcast(F32).rearrange("p (g r u) -> p g r u", g=H_GROUPS, u=2),
+                out=test_woven[j // QW][:, j % QW, :].bitcast(F32).rearrange("p (g r u) -> p g r u", g=H_GROUPS, u=2),
                 in_=bank[:].rearrange("p (g u r) -> p g r u", g=H_GROUPS, u=2),
             )
 
         def quantise_test(j):
-            nc.vector.quantize_mx(out=test_codes[:, j, :].bitcast(E4M3X4), scales=test_scale[:, j, :], in_=test_woven[j][:])
+            nc.vector.quantize_mx(
+                out=test_codes[:, cols(j, QW), :].rearrange("p j c -> p (j c)").bitcast(E4M3X4),
+                scales=test_scale[:, cols(j, QW), :].rearrange("p j c -> p (j c)"),
+                in_=test_woven[j][:].rearrange("p j c -> p (j c)"),
+            )
 
         def stage2(j, half):
             bank = open_bank()
@@ -228,14 +258,25 @@ def tile_readout_ntk_step_e3_kernel(tc, g_words, g_scales, phi_train, mult, phi_
                     stop=(hg == H_GROUPS - 1),
                 )
 
-        def add_and_store(j, half, bank):
+        def add(j, half, bank, on_vector):
             if j // 2 not in results:
                 results[j // 2] = slab([P, 2, C], F32)
             result = results[j // 2][:, j % 2, cols(half, N)]
             f0_part = f0_sb[j // LOAD_TILES][:, j % LOAD_TILES, cols(half, N)]
-            nc.vector.tensor_tensor(out=result, in0=bank[:], in1=f0_part, op=ALU.add)
-            nc.sync.dma_start(out=out_view[:, j, cols(half, N)], in_=result)
+            if on_vector:
+                nc.vector.tensor_tensor(out=result, in0=bank[:], in1=f0_part, op=ALU.add)
+            else:
+                nc.scalar.copy(out=result, in_=bank[:])
+                nc.gpsimd.tensor_tensor(out=result, in0=result, in1=f0_part, op=ALU.add)
 
+        def store(j, half):
+            stored.append((j, half))
+            if j < PAIR_FROM or j == ROW_TILES - 1:
+                nc.sync.dma_start(out=out_view[:, j, cols(half, N)], in_=results[j // 2][:, j % 2, cols(half, N)])
+            elif (j, 1 - half) in stored:
+                nc.sync.dma_start(out=out_view[:, j, :], in_=results[j // 2][:, j % 2, :])
+
+        stored = []
         for half in range(2):
             nc.vector.memset(g_scale[half][:].rearrange("p g n -> p (g n)").bitcast(U32), 0)
         make_identity(nc, ident[:])
@@ -270,7 +311,7 @@ def tile_readout_ntk_step_e3_kernel(tc, g_words, g_scales, phi_train, mult, phi_
             if i + 1 < len(pieces):
                 woven.append(weave_train(*pieces[i + 1]))
             nc.vector.quantize_mx(
-                out=train_codes[:, g, cols(hg, K_PASS)].bitcast(E4M3X4),
+                out=train_codes[hg][:, g, :].bitcast(E4M3X4),
                 scales=train_scale[:, g, cols(hg, K_PASS)],
                 in_=woven[i][:],
             )
@@ -285,24 +326,27 @@ def tile_readout_ntk_step_e3_kernel(tc, g_words, g_scales, phi_train, mult, phi_
         def at(n, work_item, *args):
             later.setdefault(n, []).append((work_item, args))
 
-        for i in range(2 * BANKS):
+        for i in range(0, 2 * BANKS, SQ):
             at(max(place["A", i - BANKS] - SQUARES_AHEAD, 0) - 1, square, i)
         for j in range(SORTED_FROM, ROW_TILES):
-            at(place["T", SORTED_FROM - 1], sort_words, j)
-        for j in range(ROW_TILES):
-            at(place["T", j] + Q_LAG * (j >= 4), quantise_test, j)
+            at(place["T", SORTED_FROM] + SORT_AT, sort_words, j)
+        for j in range(QW - 1, ROW_TILES, QW):
+            at(place["T", j] + Q_AT[j // QW], quantise_test, j // QW)
         at(3, weave_d_vector, 0)
         at(3, weave_d_scalar, 0)
         at(3, quantise_d, 0)
-        at(7, weave_d_scalar, 1)
-        at(8, weave_d_vector, 1)
-        at(9, quantise_d, 1)
-        at(last_a - 3, weave_d_vector, 2)
-        at(last_a - 1, weave_d_scalar, 2)
-        at(last_a, weave_d_scalar, 3)
-        at(last_a + 1, quantise_d, 2)
-        at(last_a + 1, weave_d_vector, 3)
-        at(last_a + 2, quantise_d, 3)
+        at(7, weave_d_gpsimd, 1)
+        at(W1_AT, weave_d_scalar, 1)
+        at(V1_AT, weave_d_vector, 1)
+        at(D1_AT, quantise_d, 1)
+        at(max(D1_AT if WTAG[1] == WTAG[2] else 0, 11), weave_d_gpsimd, 2)
+        at(last_a + V2_AT, weave_d_vector, 2)
+        at(last_a + W2_AT, weave_d_scalar, 2)
+        at(last_a + W3_AT, weave_d_scalar, 3)
+        at(last_a + D2_AT, quantise_d, 2)
+        at(last_a + max(W3_AT, D2_AT if WTAG[2] == WTAG[3] else 0), weave_d_gpsimd, 3)
+        at(last_a + V3_AT, weave_d_vector, 3)
+        at(last_a + D3_AT, quantise_d, 3)
 
         for work_item, args in later.get(-1, []):
             work_item(*args)
@@ -322,6 +366,8 @@ def tile_readout_ntk_step_e3_kernel(tc, g_words, g_scales, phi_train, mult, phi_
                 copy_turned(step[1], banks[n])
             else:
                 stage2(step[1], step[2])
-                add_and_store(step[1], step[2], banks[n])
+                shared = n in SHARED
+                add(step[1], step[2], banks[n], not shared)
+                at(n + STORE_LAG * shared, store, step[1], step[2])
             for work_item, args in later.get(n, []):
                 work_item(*args)

@@ -84,7 +84,7 @@ def tile_readout_ntk_step_e3_kernel(tc, g_words, g_scales, phi_train, mult, phi_
             return work.tile(shape, dtype, name="slab", bufs=7, align_bytes=64)
 
         ident = kept("ident", [P, P], F32)
-        g_scale = [kept("g_scale%d" % half, [P, T_GROUPS, N], U8) for half in range(2)]
+        g_scale = kept("g_scale", [P, T_GROUPS, C], U8)
         train_scale = kept("train_scale", [P, T_GROUPS, H], U8)
         mult_sb = [kept("mult%d" % quad, [P, PACK, N], BF16) for quad in range(len(QUADS))]
         d_codes = kept("d_codes", [P, H_GROUPS, C], U32)
@@ -123,11 +123,11 @@ def tile_readout_ntk_step_e3_kernel(tc, g_words, g_scales, phi_train, mult, phi_
                 out=g_codes[half][:, lo:hi, :].bitcast(I32), in_=g_view[:, lo:hi, cols(half, PACK * N)].bitcast(I32)
             )
 
-        def load_g_scale(half):
+        def load_g_scale():
             for r in range(4):
-                nc.sync.dma_start(
-                    out=g_scale[half][r:P:32, :, :].bitcast(I32),
-                    in_=g_scales[:, r:16:4, cols(half, N)].rearrange("g q n -> q g n").bitcast(I32),
+                nc.scalar.dma_start(
+                    out=g_scale[r:P:32, :, :].bitcast(I32),
+                    in_=g_scales[:, r:16:4, :].rearrange("g q n -> q g n").bitcast(I32),
                 )
 
         def load_mult(quad, lo, hi):
@@ -162,7 +162,7 @@ def tile_readout_ntk_step_e3_kernel(tc, g_words, g_scales, phi_train, mult, phi_
                 lhsT=train_codes[hg][:, g, cols(i % PACK, P)].bitcast(E4M3X4),
                 lhsT_scale=train_scale[:, g, features],
                 rhs=g_codes[half][:, g, :].bitcast(E5M2X4),
-                rhs_scale=g_scale[half][:, g, :],
+                rhs_scale=g_scale[:, g, cols(half, N)],
                 start=(g == 0),
                 stop=(g == T_GROUPS - 1),
             )
@@ -277,13 +277,12 @@ def tile_readout_ntk_step_e3_kernel(tc, g_words, g_scales, phi_train, mult, phi_
                 nc.sync.dma_start(out=out_view[:, j, :], in_=results[j // 2][:, j % 2, :])
 
         stored = []
-        for half in range(2):
-            nc.vector.memset(g_scale[half][:].rearrange("p g n -> p (g n)").bitcast(U32), 0)
+        nc.vector.memset(g_scale[:].rearrange("p g n -> p (g n)").bitcast(U32), 0)
         make_identity(nc, ident[:])
 
+        load_g_scale()
         load_train(0)
         load_train(1)
-        load_g_scale(0)
         load_g(0, 1, 0)
         load_train(2)
         load_g(1, 2, 0)
@@ -291,9 +290,7 @@ def tile_readout_ntk_step_e3_kernel(tc, g_words, g_scales, phi_train, mult, phi_
         load_g(2, 3, 0)
         load_train_last(1)
         load_g(3, 4, 0)
-        load_mult(0, 0, 2)
-        load_mult(0, 2, 4)
-        load_g_scale(1)
+        load_mult(0, 0, 4)
         load_g(0, 2, 1)
         load_g(2, 4, 1)
         load_mult(1, 0, 4)

@@ -28,30 +28,40 @@ LOAD_TILES = 4
 
 QUADS = [(0, 0), (1, 0), (0, 1), (1, 1)]
 
-TRAIN_CUT = 64
-QUAD_CUTS = [128,0,0,48]
-S_CUTS = [128,0,128,128]
+TRAIN_CUT = 68
+QUAD_CUTS = [0,0,0,64]
+S_CUTS = [0,0,128,128]
 WTAG = [0,1,0,1]
-D1_AT = 12
+D1_AT = 13
 W1_AT = 7
 V1_AT = 8
 W3_AT = 0
-PE = "AAAAA TT A TT AA XX TT XX TT YYYY XY XY TTTT XY XY XY XY XY XY"
-SHARED = []
-STORE_LAG = 2
-Q_AT = [0,1,2,2,1,1]
-SORT_AT = -9
-SQUARES_AHEAD = 2
+PE = "AAAAAA TT A TT A XX TTTT XX YYYY XY XY TT XY XY TT XY XY XY XY"
+SHARED = [33,40,46]
+STORE_LAG = 3
+Q_AT = [0,1,4,4,1,1]
+SORT_AT = -7
+D0_AT = 13
+VSORT = [4,5,6,7]
+VSORT_AT = 16
+TAIL = "m1 G m2 m3 x0 x1 f0 f1 x2 f2"
+LAST_SPLIT = 0
+G3_AT = 0
+SQUARES_AHEAD = 4
 SQ = 2
 QW = 2
 A_FIRST = 6
 V2_AT = -3
-W2_AT = -2
-D2_AT = 1
-V3_AT = 1
-D3_AT = 2
+W2_AT = -4
+D2_AT = -1
+V3_AT = 0
+D3_AT = 1
 PAIR_FROM = 12
-EARLY_BANKS = 2
+PAIR_TO = 11
+LAST_CUT = 84
+SPLIT0 = 0
+HEAD = "t0 t1 g0 t2 g1 a g2 b g3"
+EARLY_BANKS = 3
 SORTED_FROM = 8
 Q_LAG = 1
 
@@ -96,6 +106,7 @@ def tile_readout_ntk_step_e3_kernel(tc, g_words, g_scales, phi_train, mult, phi_
         train_sb = [slab([P, PACK, H], BF16) for g in range(T_GROUPS - 1)]
         g_codes = [slab([P, T_GROUPS, N], U32) for half in range(2)]
         train_codes = [slab([P, T_GROUPS, K_PASS], U32) for hg in range(H_GROUPS)]
+        train_first = [kept("train_first%d" % hg, [P, PACK, K_PASS], BF16) for hg in range(H_GROUPS * SPLIT0)]
         train_last = [kept("train_last%d" % hg, [P, PACK, K_PASS], BF16) for hg in range(H_GROUPS)]
 
         g_view = g_words.rearrange("g p n t -> p g (n t)")
@@ -142,14 +153,15 @@ def tile_readout_ntk_step_e3_kernel(tc, g_words, g_scales, phi_train, mult, phi_
 
         def weave_train(g, hg):
             woven = work.tile([P, PACK * K_PASS], BF16, name="train_woven", bufs=3, align_bytes=64)
-            raw = train_last[hg][:] if g == T_GROUPS - 1 else train_sb[g][:, :, cols(hg, K_PASS)]
+            raw = train_last[hg][:] if g == T_GROUPS - 1 else train_first[hg][:] if g == 0 and SPLIT0 else train_sb[g][:, :, cols(hg, K_PASS)]
             src = raw.rearrange("p j (m t) -> p m j t", t=PACK)
             dst = woven[:].rearrange("p (t m j) -> p m j t", t=PACK, j=PACK)
-            nc.vector.tensor_copy(out=dst[:, :TRAIN_CUT, :, :], in_=src[:, :TRAIN_CUT, :, :])
+            cut = LAST_CUT if (g, hg) == (T_GROUPS - 1, H_GROUPS - 1) else TRAIN_CUT
+            nc.vector.tensor_copy(out=dst[:, :cut, :, :], in_=src[:, :cut, :, :])
             if (g, hg) == (0, 0):
-                nc.scalar.activation(out=dst[:, TRAIN_CUT:, :, :], in_=src[:, TRAIN_CUT:, :, :], func=ACT.Copy)
+                nc.scalar.activation(out=dst[:, cut:, :, :], in_=src[:, cut:, :, :], func=ACT.Copy)
             else:
-                nc.scalar.copy(out=dst[:, TRAIN_CUT:, :, :], in_=src[:, TRAIN_CUT:, :, :])
+                nc.scalar.copy(out=dst[:, cut:, :, :], in_=src[:, cut:, :, :])
             return woven
 
         def stage1_pass(i, g):
@@ -213,12 +225,19 @@ def tile_readout_ntk_step_e3_kernel(tc, g_words, g_scales, phi_train, mult, phi_
         def test_words(j):
             return test_sb[j // LOAD_TILES][:, j % LOAD_TILES, :].bitcast(F32)
 
-        def sort_words(j):
-            in_order[j] = work.tile([P, H // 2], F32, name="in_order", bufs=ROW_TILES - SORTED_FROM, align_bytes=64)
-            nc.scalar.copy(
-                out=in_order[j][:].rearrange("p (g u r) -> p g r u", g=H_GROUPS, u=2),
-                in_=test_words(j).rearrange("p (g r u) -> p g r u", g=H_GROUPS, u=2),
+        def sort_words(j, count, copy):
+            if j % LOAD_TILES == 0:
+                tile = work.tile([P, LOAD_TILES, H // 2], F32, name="in_order", bufs=1, align_bytes=64)
+                for k in range(LOAD_TILES):
+                    in_order[j + k] = tile[:, k, :]
+                sorted_tiles[j // LOAD_TILES] = tile
+            rows = slice(j % LOAD_TILES, j % LOAD_TILES + count)
+            copy(
+                out=sorted_tiles[j // LOAD_TILES][:, rows, :].rearrange("p j (g u r) -> p (j g) r u", g=H_GROUPS, u=2),
+                in_=test_sb[j // LOAD_TILES][:, rows, :].rearrange("p j h -> p (j h)").bitcast(F32).rearrange("p (g r u) -> p g r u", r=P, u=2),
             )
+
+        sorted_tiles = {}
 
         def turn(j):
             bank = open_bank()
@@ -271,7 +290,7 @@ def tile_readout_ntk_step_e3_kernel(tc, g_words, g_scales, phi_train, mult, phi_
 
         def store(j, half):
             stored.append((j, half))
-            if j < PAIR_FROM or j == ROW_TILES - 1:
+            if j < PAIR_FROM or j >= PAIR_TO:
                 nc.sync.dma_start(out=out_view[:, j, cols(half, N)], in_=results[j // 2][:, j % 2, cols(half, N)])
             elif (j, 1 - half) in stored:
                 nc.sync.dma_start(out=out_view[:, j, :], in_=results[j // 2][:, j % 2, :])
@@ -281,26 +300,26 @@ def tile_readout_ntk_step_e3_kernel(tc, g_words, g_scales, phi_train, mult, phi_
         make_identity(nc, ident[:])
 
         load_g_scale()
-        load_train(0)
-        load_train(1)
-        load_g(0, 1, 0)
-        load_train(2)
-        load_g(1, 2, 0)
-        load_train_last(0)
-        load_g(2, 3, 0)
-        load_train_last(1)
-        load_g(3, 4, 0)
+        for e in HEAD.split():
+            if e[0] == "t":
+                load_train(int(e[1]))
+            elif e[0] == "g":
+                load_g(int(e[1]), int(e[1]) + 1, 0)
+            elif e in "ab":
+                load_train_last("ab".index(e))
+            else:
+                nc.sync.dma_start(out=train_first["AB".index(e)][:], in_=train_view[:, 0, :, cols("AB".index(e), K_PASS)])
         load_mult(0, 0, 4)
         load_g(0, 2, 1)
-        load_g(2, 4, 1)
-        load_mult(1, 0, 4)
-        load_mult(2, 0, 4)
-        load_test(0)
-        load_mult(3, 0, 4)
-        load_f0(0)
-        for i in range(1, ROW_TILES // LOAD_TILES):
-            load_test(i)
-            load_f0(i)
+        for e in TAIL.split():
+            if e[0] == "G":
+                load_g(2, 4, 1)
+            elif e[0] == "m":
+                load_mult(int(e[1]), 0, 4)
+            elif e[0] == "x":
+                load_test(int(e[1]))
+            else:
+                load_f0(int(e[1]))
 
         pieces = [(g, hg) for g in range(T_GROUPS) for hg in range(H_GROUPS)]
         woven = [weave_train(*pieces[0])]
@@ -325,14 +344,16 @@ def tile_readout_ntk_step_e3_kernel(tc, g_words, g_scales, phi_train, mult, phi_
 
         for i in range(0, 2 * BANKS, SQ):
             at(max(place["A", i - BANKS] - SQUARES_AHEAD, 0) - 1, square, i)
-        for j in range(SORTED_FROM, ROW_TILES):
-            at(place["T", SORTED_FROM] + SORT_AT, sort_words, j)
+        for j in range(SORTED_FROM, ROW_TILES, 2):
+            at(place["T", SORTED_FROM] + SORT_AT, sort_words, j, 2, nc.scalar.copy)
         for j in range(QW - 1, ROW_TILES, QW):
             at(place["T", j] + Q_AT[j // QW], quantise_test, j // QW)
         at(3, weave_d_vector, 0)
         at(3, weave_d_scalar, 0)
-        at(3, quantise_d, 0)
-        at(7, weave_d_gpsimd, 1)
+        at(3, weave_d_gpsimd, 0)
+        at(D0_AT, quantise_d, 0)
+        at(VSORT_AT, sort_words, 4, 4, nc.vector.tensor_copy)
+        at(max(7, D0_AT if WTAG[0] == WTAG[1] else 0), weave_d_gpsimd, 1)
         at(W1_AT, weave_d_scalar, 1)
         at(V1_AT, weave_d_vector, 1)
         at(D1_AT, quantise_d, 1)
@@ -341,7 +362,7 @@ def tile_readout_ntk_step_e3_kernel(tc, g_words, g_scales, phi_train, mult, phi_
         at(last_a + W2_AT, weave_d_scalar, 2)
         at(last_a + W3_AT, weave_d_scalar, 3)
         at(last_a + D2_AT, quantise_d, 2)
-        at(last_a + max(W3_AT, D2_AT if WTAG[2] == WTAG[3] else 0), weave_d_gpsimd, 3)
+        at(last_a + G3_AT, weave_d_gpsimd, 3)
         at(last_a + V3_AT, weave_d_vector, 3)
         at(last_a + D3_AT, quantise_d, 3)
 

@@ -28,55 +28,16 @@ LOAD_TILES = 4
 
 QUADS = [(0, 0), (1, 0), (0, 1), (1, 1)]
 
-TRAIN_CUT = 68
-QUAD_CUTS = [0,0,0,64]
-S_CUTS = [0,0,128,128]
-WTAG = [0,1,0,1]
-D1_AT = 13
-W1_AT = 7
-V1_AT = 8
-W3_AT = 0
-PE = "AAAAAA TT A TT A XX TTTT XX YYYY XY XY TT XY XY TT XY XY XY XY"
-SHARED = [33,40,46]
-STORE_LAG = 3
-Q_AT = [0,1,4,4,1,1]
-SORT_AT = -7
-D0_AT = 13
-VSORT = [4,5,6,7]
-VSORT_AT = 16
-TAIL = "m1 G m2 m3 x0 x1 f0 f1 x2 f2"
-LAST_SPLIT = 0
-G3_AT = 0
-SQUARES_AHEAD = 4
-SQ = 2
-QW = 2
-A_FIRST = 6
-V2_AT = -3
-W2_AT = -4
-D2_AT = -1
-V3_AT = 0
-D3_AT = 1
-PAIR_FROM = 12
-PAIR_TO = 11
-LAST_CUT = 84
-SPLIT0 = 0
-HEAD = "t0 t1 g0 t2 g1 a g2 b g3"
+VECTOR_STEPS = 32
+VECTOR_STEPS_LAST = 42
+SQUARES_AHEAD = 3
 EARLY_BANKS = 3
-SORTED_FROM = 8
-Q_LAG = 1
+BANKS_BEFORE_TURNS = 6
+SLOW_STORE_LAG = 4
 
 
 def cols(i, width):
     return slice(i * width, (i + 1) * width)
-
-
-def tensor_steps():
-    n = {"A": 0, "T": 0, "X": 0, "Y": 0}
-    steps = []
-    for k in PE.replace(" ", ""):
-        steps.append((k, n[k]) if k in "AT" else ("S", n[k], "XY".index(k)))
-        n[k] += 1
-    return steps
 
 
 def tile_readout_ntk_step_e3_kernel(tc, g_words, g_scales, phi_train, mult, phi_test, f0, out):
@@ -90,8 +51,11 @@ def tile_readout_ntk_step_e3_kernel(tc, g_words, g_scales, phi_train, mult, phi_
         def kept(name, shape, dtype):
             return keep.tile(shape, dtype, name=name, align_bytes=64)
 
+        def rotating(name, shape, dtype, bufs):
+            return work.tile(shape, dtype, name=name, bufs=bufs, align_bytes=64)
+
         def slab(shape, dtype):
-            return work.tile(shape, dtype, name="slab", bufs=7, align_bytes=64)
+            return rotating("slab", shape, dtype, 7)
 
         ident = kept("ident", [P, P], F32)
         g_scale = kept("g_scale", [P, T_GROUPS, C], U8)
@@ -106,22 +70,23 @@ def tile_readout_ntk_step_e3_kernel(tc, g_words, g_scales, phi_train, mult, phi_
         train_sb = [slab([P, PACK, H], BF16) for g in range(T_GROUPS - 1)]
         g_codes = [slab([P, T_GROUPS, N], U32) for half in range(2)]
         train_codes = [slab([P, T_GROUPS, K_PASS], U32) for hg in range(H_GROUPS)]
-        train_first = [kept("train_first%d" % hg, [P, PACK, K_PASS], BF16) for hg in range(H_GROUPS * SPLIT0)]
         train_last = [kept("train_last%d" % hg, [P, PACK, K_PASS], BF16) for hg in range(H_GROUPS)]
 
         g_view = g_words.rearrange("g p n t -> p g (n t)")
         train_view = phi_train.rearrange("(g p j) h -> p g j h", p=P, j=PACK)
         mult_view = mult.rearrange("(g p t) c -> p g t c", p=P, t=PACK)
-        test_view = phi_test.rearrange("(p j) h -> p j h", j=ROW_TILES)
-        f0_view = f0.rearrange("(p j) c -> p j c", j=ROW_TILES)
-        out_view = out.rearrange("(p j) c -> p j c", j=ROW_TILES)
+        test_view = phi_test.rearrange("(i p j) h -> p i j h", p=P, j=LOAD_TILES)
+        f0_view = f0.rearrange("(i p j) c -> p i j c", p=P, j=LOAD_TILES)
+        out_view = out.rearrange("(i p j) c -> p i j c", p=P, j=LOAD_TILES)
 
         banks = []
-        a_banks, squares, d_flat, d_woven, in_order, test_woven, results = {}, {}, {}, {}, {}, {}, {}
+        a_banks, squares, d_flat, d_woven, sorted_words, test_woven, results = {}, {}, {}, {}, {}, {}, {}
+        waiting_stores = []
 
-        def open_bank():
+        def next_bank():
             banks.append(psum.tile([P, N], F32, name="bank%d" % (len(banks) % BANKS)))
             return banks[-1]
+
 
         def load_train(g):
             nc.sync.dma_start(out=train_sb[g][:], in_=train_view[:, g, :, :])
@@ -134,85 +99,93 @@ def tile_readout_ntk_step_e3_kernel(tc, g_words, g_scales, phi_train, mult, phi_
                 out=g_codes[half][:, lo:hi, :].bitcast(I32), in_=g_view[:, lo:hi, cols(half, PACK * N)].bitcast(I32)
             )
 
-        def load_g_scale():
-            for r in range(4):
-                nc.scalar.dma_start(
-                    out=g_scale[r:P:32, :, :].bitcast(I32),
-                    in_=g_scales[:, r:16:4, :].rearrange("g q n -> q g n").bitcast(I32),
-                )
-
-        def load_mult(quad, lo, hi):
+        def load_mult(quad):
             hg, half = QUADS[quad]
-            nc.sync.dma_start(out=mult_sb[quad][:, lo:hi, :], in_=mult_view[:, hg, lo:hi, cols(half, N)])
+            nc.sync.dma_start(out=mult_sb[quad][:], in_=mult_view[:, hg, :, cols(half, N)])
 
         def load_test(i):
-            nc.sync.dma_start(out=test_sb[i][:], in_=test_view[:, cols(i, LOAD_TILES), :])
+            nc.sync.dma_start(out=test_sb[i][:], in_=test_view[:, i, :, :])
 
         def load_f0(i):
-            nc.sync.dma_start(out=f0_sb[i][:], in_=f0_view[:, cols(i, LOAD_TILES), :])
+            nc.sync.dma_start(out=f0_sb[i][:], in_=f0_view[:, i, :, :])
+
 
         def weave_train(g, hg):
-            woven = work.tile([P, PACK * K_PASS], BF16, name="train_woven", bufs=3, align_bytes=64)
-            raw = train_last[hg][:] if g == T_GROUPS - 1 else train_first[hg][:] if g == 0 and SPLIT0 else train_sb[g][:, :, cols(hg, K_PASS)]
-            src = raw.rearrange("p j (m t) -> p m j t", t=PACK)
-            dst = woven[:].rearrange("p (t m j) -> p m j t", t=PACK, j=PACK)
-            cut = LAST_CUT if (g, hg) == (T_GROUPS - 1, H_GROUPS - 1) else TRAIN_CUT
-            nc.vector.tensor_copy(out=dst[:, :cut, :, :], in_=src[:, :cut, :, :])
+            last = g == T_GROUPS - 1
+            raw = train_last[hg][:] if last else train_sb[g][:, :, cols(hg, K_PASS)]
+            woven = rotating("train_woven", [P, PACK * K_PASS], BF16, 3)
+            src = raw.rearrange("p j (m n t) -> p m t n j", n=2, t=PACK)
+            dst = woven[:].rearrange("p (t m n j) -> p m t n j", t=PACK, n=2, j=PACK)
+            cut = VECTOR_STEPS_LAST if last and hg == H_GROUPS - 1 else VECTOR_STEPS
+            nc.vector.tensor_copy(out=dst[:, :cut, :, :, :], in_=src[:, :cut, :, :, :])
             if (g, hg) == (0, 0):
-                nc.scalar.activation(out=dst[:, cut:, :, :], in_=src[:, cut:, :, :], func=ACT.Copy)
+                src = raw.rearrange("p j (m t) -> p m j t", t=PACK)
+                dst = woven[:].rearrange("p (t m j) -> p m j t", t=PACK, j=PACK)
+                nc.scalar.activation(out=dst[:, 2 * cut :, :, :], in_=src[:, 2 * cut :, :, :], func=ACT.Copy)
             else:
-                nc.scalar.copy(out=dst[:, cut:, :, :], in_=src[:, cut:, :, :])
+                nc.scalar.copy(out=dst[:, cut:, :, :, :], in_=src[:, cut:, :, :, :])
             return woven
+
+        def quantise_train(g, hg, woven):
+            nc.vector.quantize_mx(
+                out=train_codes[hg][:, g, :].bitcast(E4M3X4), scales=train_scale[:, g, cols(hg, K_PASS)], in_=woven[:]
+            )
 
         def stage1_pass(i, g):
             hg, half = QUADS[i // PACK]
             if g == 0:
-                a_banks[i] = open_bank()
-            features = cols(hg * PACK + i % PACK, P)
+                a_banks[i] = next_bank()
             nc.tensor.matmul_mx(
                 out=a_banks[i][:],
                 lhsT=train_codes[hg][:, g, cols(i % PACK, P)].bitcast(E4M3X4),
-                lhsT_scale=train_scale[:, g, features],
+                lhsT_scale=train_scale[:, g, cols(hg * PACK + i % PACK, P)],
                 rhs=g_codes[half][:, g, :].bitcast(E5M2X4),
                 rhs_scale=g_scale[:, g, cols(half, N)],
                 start=(g == 0),
                 stop=(g == T_GROUPS - 1),
             )
 
-        def square(i):
-            tile = work.tile([P, SQ, N], F32, name="square", bufs=SQUARES_AHEAD // SQ + 2, align_bytes=64)
-            nc.scalar.activation(out=tile[:], in_=mult_sb[i // PACK][:, i % PACK : i % PACK + SQ, :], func=ACT.Square)
-            for k in range(SQ):
-                squares[i + k] = tile[:, k, :]
 
-        def multiply(i):
+        def square_pair(pair):
+            quad, first = divmod(2 * pair, PACK)
+            squares[pair] = rotating("square", [P, 2, N], F32, SQUARES_AHEAD + 1)
+            nc.scalar.activation(out=squares[pair][:], in_=mult_sb[quad][:, first : first + 2, :], func=ACT.Square)
+
+        def scale_bank(i):
             quad, t = divmod(i, PACK)
             if t == 0:
-                d_flat[quad] = work.tile([P, PACK, N], BF16, name="d_flat", bufs=3, align_bytes=64)
-            nc.vector.tensor_tensor(out=d_flat[quad][:, t, :], in0=a_banks[i][:], in1=squares[i], op=ALU.mult)
+                d_flat[quad] = rotating("d_flat", [P, PACK, N], BF16, 3)
+            nc.vector.tensor_tensor(
+                out=d_flat[quad][:, t, :], in0=a_banks[i][:], in1=squares[i // 2][:, i % 2, :], op=ALU.mult
+            )
+            if i % 2 == 1 and i // 2 + SQUARES_AHEAD < BANKS:
+                square_pair(i // 2 + SQUARES_AHEAD)
 
-        def weave_d(quad, copy, part):
+        def sum_and_scale(i):
+            for g in range(2 if i < BANKS + EARLY_BANKS else 0, T_GROUPS):
+                stage1_pass(i, g)
+            scale_bank(i)
+
+        def woven_tile(quad):
             if quad not in d_woven:
-                d_woven[quad] = work.tile([P, N, PACK], BF16, name="d_woven%d" % WTAG[quad], bufs=1, align_bytes=64)
-            if part.start < part.stop:
-                src = d_flat[quad][:].rearrange("p t (c e) -> p c t e", e=PACK)
-                dst = d_woven[quad][:].rearrange("p (c e) t -> p c t e", e=PACK)
-                copy(out=dst[:, part, :, :], in_=src[:, part, :, :])
+                d_woven[quad] = rotating("d_woven", [P, N, PACK], BF16, 3)
+            return d_woven[quad]
 
-        def weave_d_vector(quad):
-            weave_d(quad, nc.vector.tensor_copy, slice(0, QUAD_CUTS[quad]))
+        def weave_d_half(quad, part, copy):
+            src = d_flat[quad][:].rearrange("p t (c e) -> p c t e", e=PACK)
+            dst = woven_tile(quad)[:].rearrange("p (c e) t -> p c t e", e=PACK)
+            steps = cols(part, N // PACK // 2)
+            copy(out=dst[:, steps, :, :], in_=src[:, steps, :, :])
 
-        def weave_d_scalar(quad):
-            weave_d(quad, nc.scalar.copy, slice(QUAD_CUTS[quad], S_CUTS[quad]))
-
-        def gpsimd_copy(out, in_):
-            nc.gpsimd.tensor_scalar(out=out, in0=in_, scalar1=1.0, scalar2=0.0, op0=ALU.mult, op1=ALU.add)
-
-        def weave_d_gpsimd(quad):
-            weave_d(quad, None, slice(0, 0))
-            part = slice(PACK * S_CUTS[quad], N)
-            if part.start < part.stop:
-                gpsimd_copy(d_woven[quad][:, part, :], d_flat[quad][:, :, part].rearrange("p t c -> p c t"))
+        def weave_d_on_gpsimd(quad):
+            nc.gpsimd.tensor_scalar(
+                out=woven_tile(quad)[:],
+                in0=d_flat[quad][:].rearrange("p t c -> p c t"),
+                scalar1=1.0,
+                scalar2=0.0,
+                op0=ALU.mult,
+                op1=ALU.add,
+            )
 
         def quantise_d(quad):
             hg, half = QUADS[quad]
@@ -222,50 +195,45 @@ def tile_readout_ntk_step_e3_kernel(tc, g_words, g_scales, phi_train, mult, phi_
                 in_=d_woven[quad][:].rearrange("p c t -> p (c t)"),
             )
 
-        def test_words(j):
-            return test_sb[j // LOAD_TILES][:, j % LOAD_TILES, :].bitcast(F32)
 
-        def sort_words(j, count, copy):
-            if j % LOAD_TILES == 0:
-                tile = work.tile([P, LOAD_TILES, H // 2], F32, name="in_order", bufs=1, align_bytes=64)
-                for k in range(LOAD_TILES):
-                    in_order[j + k] = tile[:, k, :]
-                sorted_tiles[j // LOAD_TILES] = tile
-            rows = slice(j % LOAD_TILES, j % LOAD_TILES + count)
+        def sort_words(first, count, copy):
+            load, row = divmod(first, LOAD_TILES)
+            if row == 0:
+                sorted_words[load] = rotating("sorted_words", [P, LOAD_TILES, H // 2], F32, 1)
+            words = test_sb[load][:, row : row + count, :].rearrange("p j h -> p (j h)").bitcast(F32)
             copy(
-                out=sorted_tiles[j // LOAD_TILES][:, rows, :].rearrange("p j (g u r) -> p (j g) r u", g=H_GROUPS, u=2),
-                in_=test_sb[j // LOAD_TILES][:, rows, :].rearrange("p j h -> p (j h)").bitcast(F32).rearrange("p (g r u) -> p g r u", r=P, u=2),
+                out=sorted_words[load][:, row : row + count, :].rearrange("p j (g u r) -> p (j g) r u", g=H_GROUPS, u=2),
+                in_=words.rearrange("p (g r u) -> p g r u", r=P, u=2),
             )
 
-        sorted_tiles = {}
-
         def turn(j):
-            bank = open_bank()
+            load, row = divmod(j, LOAD_TILES)
+            bank = next_bank()
             for hg in range(H_GROUPS):
                 for u in range(2):
-                    if j in in_order:
-                        words = in_order[j][:, cols(2 * hg + u, P)]
+                    if load in sorted_words:
+                        words = sorted_words[load][:, row, cols(2 * hg + u, P)]
                     else:
-                        words = test_words(j)[:, 2 * P * hg + u : 2 * P * (hg + 1) : 2]
+                        words = test_sb[load][:, row, :].bitcast(F32)[:, 2 * P * hg + u : 2 * P * (hg + 1) : 2]
                     nc.tensor.transpose(bank[:, cols(2 * hg + u, P)], words, ident[:])
-
-        def copy_turned(j, bank):
-            if j % QW == 0:
-                test_woven[j // QW] = work.tile([P, QW, H], BF16, name="test_woven", bufs=4 // QW + (QW == 4), align_bytes=64)
+            if j % 2 == 0:
+                test_woven[j // 2] = rotating("test_woven", [P, 2, H], BF16, 2)
             nc.scalar.copy(
-                out=test_woven[j // QW][:, j % QW, :].bitcast(F32).rearrange("p (g r u) -> p g r u", g=H_GROUPS, u=2),
+                out=test_woven[j // 2][:, j % 2, :].bitcast(F32).rearrange("p (g r u) -> p g r u", g=H_GROUPS, u=2),
                 in_=bank[:].rearrange("p (g u r) -> p g r u", g=H_GROUPS, u=2),
             )
 
-        def quantise_test(j):
+        def quantise_test(pair):
             nc.vector.quantize_mx(
-                out=test_codes[:, cols(j, QW), :].rearrange("p j c -> p (j c)").bitcast(E4M3X4),
-                scales=test_scale[:, cols(j, QW), :].rearrange("p j c -> p (j c)"),
-                in_=test_woven[j][:].rearrange("p j c -> p (j c)"),
+                out=test_codes[:, cols(pair, 2), :].rearrange("p j c -> p (j c)").bitcast(E4M3X4),
+                scales=test_scale[:, cols(pair, 2), :].rearrange("p j c -> p (j c)"),
+                in_=test_woven[pair][:].rearrange("p j c -> p (j c)"),
             )
 
-        def stage2(j, half):
-            bank = open_bank()
+
+        def stage2(j, half, on_vector=True):
+            load, row = divmod(j, LOAD_TILES)
+            bank = next_bank()
             for hg in range(H_GROUPS):
                 nc.tensor.matmul_mx(
                     out=bank[:],
@@ -276,116 +244,113 @@ def tile_readout_ntk_step_e3_kernel(tc, g_words, g_scales, phi_train, mult, phi_
                     start=(hg == 0),
                     stop=(hg == H_GROUPS - 1),
                 )
-
-        def add(j, half, bank, on_vector):
             if j // 2 not in results:
                 results[j // 2] = slab([P, 2, C], F32)
             result = results[j // 2][:, j % 2, cols(half, N)]
-            f0_part = f0_sb[j // LOAD_TILES][:, j % LOAD_TILES, cols(half, N)]
+            f0_part = f0_sb[load][:, row, cols(half, N)]
             if on_vector:
                 nc.vector.tensor_tensor(out=result, in0=bank[:], in1=f0_part, op=ALU.add)
+                nc.sync.dma_start(out=out_view[:, load, row, cols(half, N)], in_=result)
             else:
                 nc.scalar.copy(out=result, in_=bank[:])
                 nc.gpsimd.tensor_tensor(out=result, in0=result, in1=f0_part, op=ALU.add)
+                waiting_stores.append((len(banks) + SLOW_STORE_LAG, out_view[:, load, row, cols(half, N)], result))
+            while waiting_stores and waiting_stores[0][0] <= len(banks):
+                due, target, source = waiting_stores.pop(0)
+                nc.sync.dma_start(out=target, in_=source)
 
-        def store(j, half):
-            stored.append((j, half))
-            if j < PAIR_FROM or j >= PAIR_TO:
-                nc.sync.dma_start(out=out_view[:, j, cols(half, N)], in_=results[j // 2][:, j % 2, cols(half, N)])
-            elif (j, 1 - half) in stored:
-                nc.sync.dma_start(out=out_view[:, j, :], in_=results[j // 2][:, j % 2, :])
-
-        stored = []
         nc.vector.memset(g_scale[:].rearrange("p g n -> p (g n)").bitcast(U32), 0)
         make_identity(nc, ident[:])
+        for r in range(4):
+            nc.scalar.dma_start(
+                out=g_scale[r:P:32, :, :].bitcast(I32),
+                in_=g_scales[:, r:16:4, :].rearrange("g q n -> q g n").bitcast(I32),
+            )
 
-        load_g_scale()
-        for e in HEAD.split():
-            if e[0] == "t":
-                load_train(int(e[1]))
-            elif e[0] == "g":
-                load_g(int(e[1]), int(e[1]) + 1, 0)
-            elif e in "ab":
-                load_train_last("ab".index(e))
-            else:
-                nc.sync.dma_start(out=train_first["AB".index(e)][:], in_=train_view[:, 0, :, cols("AB".index(e), K_PASS)])
-        load_mult(0, 0, 4)
-        load_g(0, 2, 1)
-        for e in TAIL.split():
-            if e[0] == "G":
-                load_g(2, 4, 1)
-            elif e[0] == "m":
-                load_mult(int(e[1]), 0, 4)
-            elif e[0] == "x":
-                load_test(int(e[1]))
-            else:
-                load_f0(int(e[1]))
+        load_train(0)
+        for g in range(T_GROUPS - 2):
+            load_train(g + 1)
+            load_g(g, g + 1, 0)
+        for hg in range(H_GROUPS):
+            load_train_last(hg)
+            load_g(T_GROUPS - 2 + hg, T_GROUPS - 1 + hg, 0)
+        for quad in range(2):
+            load_mult(quad)
+            load_g(2 * quad, 2 * quad + 2, 1)
+        for quad in range(2, len(QUADS)):
+            load_mult(quad)
+        load_test(0)
+        load_test(1)
+        load_f0(0)
+        load_f0(1)
+        load_test(2)
+        load_f0(2)
 
         pieces = [(g, hg) for g in range(T_GROUPS) for hg in range(H_GROUPS)]
         woven = [weave_train(*pieces[0])]
         for i, (g, hg) in enumerate(pieces):
             if i + 1 < len(pieces):
                 woven.append(weave_train(*pieces[i + 1]))
-            nc.vector.quantize_mx(
-                out=train_codes[hg][:, g, :].bitcast(E4M3X4),
-                scales=train_scale[:, g, cols(hg, K_PASS)],
-                in_=woven[i][:],
-            )
+            quantise_train(g, hg, woven[i])
             for t in range(PACK):
                 stage1_pass(hg * PACK + t, g)
 
-        steps = [("A", i - BANKS) for i in range(BANKS)] + tensor_steps()
-        place = {step: n for n, step in enumerate(steps)}
-        last_a = place["A", BANKS - 1]
-        later = {}
+        for pair in range(SQUARES_AHEAD):
+            square_pair(pair)
+        for i in range(BANKS):
+            scale_bank(i)
+            if i % PACK == PACK - 1:
+                weave_d_on_gpsimd(i // PACK)
+        for i in range(BANKS, BANKS + EARLY_BANKS):
+            for g in range(2):
+                stage1_pass(i, g)
+        for i in range(BANKS, BANKS + BANKS_BEFORE_TURNS):
+            sum_and_scale(i)
 
-        def at(n, work_item, *args):
-            later.setdefault(n, []).append((work_item, args))
+        quantise_d(0)
+        sort_words(LOAD_TILES, LOAD_TILES, nc.vector.tensor_copy)
+        quantise_d(1)
+        weave_d_half(2, 0, nc.scalar.copy)
+        turn(0)
+        turn(1)
+        quantise_test(0)
+        weave_d_half(2, 1, nc.scalar.copy)
+        sum_and_scale(2 * BANKS - 2)
+        turn(2)
+        turn(3)
+        quantise_d(2)
+        sum_and_scale(2 * BANKS - 1)
+        quantise_test(1)
 
-        for i in range(0, 2 * BANKS, SQ):
-            at(max(place["A", i - BANKS] - SQUARES_AHEAD, 0) - 1, square, i)
-        for j in range(SORTED_FROM, ROW_TILES, 2):
-            at(place["T", SORTED_FROM] + SORT_AT, sort_words, j, 2, nc.scalar.copy)
-        for j in range(QW - 1, ROW_TILES, QW):
-            at(place["T", j] + Q_AT[j // QW], quantise_test, j // QW)
-        at(3, weave_d_vector, 0)
-        at(3, weave_d_scalar, 0)
-        at(3, weave_d_gpsimd, 0)
-        at(D0_AT, quantise_d, 0)
-        at(VSORT_AT, sort_words, 4, 4, nc.vector.tensor_copy)
-        at(max(7, D0_AT if WTAG[0] == WTAG[1] else 0), weave_d_gpsimd, 1)
-        at(W1_AT, weave_d_scalar, 1)
-        at(V1_AT, weave_d_vector, 1)
-        at(D1_AT, quantise_d, 1)
-        at(max(D1_AT if WTAG[1] == WTAG[2] else 0, 11), weave_d_gpsimd, 2)
-        at(last_a + V2_AT, weave_d_vector, 2)
-        at(last_a + W2_AT, weave_d_scalar, 2)
-        at(last_a + W3_AT, weave_d_scalar, 3)
-        at(last_a + D2_AT, quantise_d, 2)
-        at(last_a + G3_AT, weave_d_gpsimd, 3)
-        at(last_a + V3_AT, weave_d_vector, 3)
-        at(last_a + D3_AT, quantise_d, 3)
+        weave_d_half(3, 1, nc.scalar.copy)
+        weave_d_half(3, 0, nc.vector.tensor_copy)
+        stage2(0, 0)
+        quantise_d(3)
+        stage2(1, 0)
+        for j in range(LOAD_TILES, 2 * LOAD_TILES):
+            turn(j)
+        for first in range(2 * LOAD_TILES, ROW_TILES, 2):
+            sort_words(first, 2, nc.scalar.copy)
+        stage2(2, 0)
+        stage2(3, 0)
+        quantise_test(2)
+        stage2(0, 1)
+        stage2(1, 1)
+        quantise_test(3)
+        stage2(2, 1)
+        stage2(3, 1)
 
-        for work_item, args in later.get(-1, []):
-            work_item(*args)
-        for n, step in enumerate(steps):
-            if step[0] == "A":
-                i = step[1] + BANKS
-                if i == BANKS:
-                    for early in range(EARLY_BANKS):
-                        for g in range(2):
-                            stage1_pass(BANKS + early, g)
-                if i >= BANKS:
-                    for g in range(2 if i < BANKS + EARLY_BANKS else 0, T_GROUPS):
-                        stage1_pass(i, g)
-                multiply(i)
-            elif step[0] == "T":
-                turn(step[1])
-                copy_turned(step[1], banks[n])
-            else:
-                stage2(step[1], step[2])
-                shared = n in SHARED
-                add(step[1], step[2], banks[n], not shared)
-                at(n + STORE_LAG * shared, store, step[1], step[2])
-            for work_item, args in later.get(n, []):
-                work_item(*args)
+        pairs = ROW_TILES // 2
+        turned_pairs = 2 * LOAD_TILES // 2
+        for pair in range(LOAD_TILES // 2, pairs):
+            ahead = pair + 1
+            fresh = turned_pairs <= ahead < pairs
+            if fresh:
+                turn(2 * ahead)
+                turn(2 * ahead + 1)
+            stage2(2 * pair, 0)
+            if fresh:
+                quantise_test(ahead)
+            stage2(2 * pair, 1)
+            stage2(2 * pair + 1, 0, on_vector=(pair == pairs - 1))
+            stage2(2 * pair + 1, 1)

@@ -29,9 +29,13 @@ LOAD_TILES = 4
 QUADS = [(0, 0), (1, 0), (0, 1), (1, 1)]
 
 VECTOR_STEPS = 32
-VECTOR_STEPS_LAST = 42
+VECTOR_STEPS_LAST = 24
 SQUARES_AHEAD = 3
-EARLY_BANKS = 3
+EARLY_BANKS = 4
+G_FIRST = 1
+BEFORE = 3
+BETWEEN = 4
+FIRST_EARLY = 4
 BANKS_BEFORE_TURNS = 6
 SLOW_STORE_LAG = 4
 
@@ -151,14 +155,14 @@ def tile_readout_ntk_step_e3_kernel(tc, g_words, g_scales, phi_train, mult, phi_
             squares[pair] = rotating("square", [P, 2, N], F32, SQUARES_AHEAD + 1)
             nc.scalar.activation(out=squares[pair][:], in_=mult_sb[quad][:, first : first + 2, :], func=ACT.Square)
 
-        def scale_bank(i):
+        def scale_bank(i, square_ahead=True):
             quad, t = divmod(i, PACK)
             if t == 0:
                 d_flat[quad] = rotating("d_flat", [P, PACK, N], BF16, 3)
             nc.vector.tensor_tensor(
                 out=d_flat[quad][:, t, :], in0=a_banks[i][:], in1=squares[i // 2][:, i % 2, :], op=ALU.mult
             )
-            if i % 2 == 1 and i // 2 + SQUARES_AHEAD < BANKS:
+            if square_ahead and i % 2 == 1 and i // 2 + SQUARES_AHEAD < BANKS:
                 square_pair(i // 2 + SQUARES_AHEAD)
 
         def sum_and_scale(i):
@@ -196,12 +200,12 @@ def tile_readout_ntk_step_e3_kernel(tc, g_words, g_scales, phi_train, mult, phi_
             )
 
 
-        def sort_words(first, count, copy):
+        def sort_words(first, count):
             load, row = divmod(first, LOAD_TILES)
             if row == 0:
                 sorted_words[load] = rotating("sorted_words", [P, LOAD_TILES, H // 2], F32, 1)
             words = test_sb[load][:, row : row + count, :].rearrange("p j h -> p (j h)").bitcast(F32)
-            copy(
+            nc.scalar.copy(
                 out=sorted_words[load][:, row : row + count, :].rearrange("p j (g u r) -> p (j g) r u", g=H_GROUPS, u=2),
                 in_=words.rearrange("p (g r u) -> p g r u", r=P, u=2),
             )
@@ -271,44 +275,58 @@ def tile_readout_ntk_step_e3_kernel(tc, g_words, g_scales, phi_train, mult, phi_
         for g in range(T_GROUPS - 2):
             load_train(g + 1)
             load_g(g, g + 1, 0)
-        for hg in range(H_GROUPS):
-            load_train_last(hg)
-            load_g(T_GROUPS - 2 + hg, T_GROUPS - 1 + hg, 0)
-        for quad in range(2):
-            load_mult(quad)
-            load_g(2 * quad, 2 * quad + 2, 1)
+        load_train_last(0)
+        load_g(T_GROUPS - 2, T_GROUPS, 0)
+        load_mult(0)
+        if G_FIRST:
+            load_g(0, 2, 1)
+        load_train_last(1)
+        if not G_FIRST:
+            load_g(0, 2, 1)
+        load_mult(1)
+        load_g(2, 4, 1)
         for quad in range(2, len(QUADS)):
             load_mult(quad)
-        load_test(0)
-        load_test(1)
-        load_f0(0)
-        load_f0(1)
-        load_test(2)
-        load_f0(2)
+        for i in range(ROW_TILES // LOAD_TILES):
+            load_test(i)
+            load_f0(i)
 
-        pieces = [(g, hg) for g in range(T_GROUPS) for hg in range(H_GROUPS)]
+        pieces = sorted(((g, hg) for g in range(T_GROUPS) for hg in range(H_GROUPS)), key=lambda x: (x[0] + x[1], x[1]))
         woven = [weave_train(*pieces[0])]
-        for i, (g, hg) in enumerate(pieces):
-            if i + 1 < len(pieces):
+        for i, (g, hg) in enumerate(pieces[:-1]):
+            if i + 2 < len(pieces):
                 woven.append(weave_train(*pieces[i + 1]))
             quantise_train(g, hg, woven[i])
             for t in range(PACK):
                 stage1_pass(hg * PACK + t, g)
-
-        for pair in range(SQUARES_AHEAD):
+        for pair in range(2):
             square_pair(pair)
-        for i in range(BANKS):
-            scale_bank(i)
-            if i % PACK == PACK - 1:
-                weave_d_on_gpsimd(i // PACK)
-        for i in range(BANKS, BANKS + EARLY_BANKS):
+        for i in range(BEFORE):
+            scale_bank(i, False)
+        last = weave_train(*pieces[-1])
+        for i in range(BEFORE, BETWEEN):
+            scale_bank(i, False)
+        quantise_train(*pieces[-1], last)
+        for i in range(BETWEEN, PACK):
+            scale_bank(i, False)
+        weave_d_on_gpsimd(0)
+        for i in range(BANKS, BANKS + FIRST_EARLY):
             for g in range(2):
                 stage1_pass(i, g)
+        for t in range(PACK):
+            stage1_pass(PACK + t, T_GROUPS - 1)
+        for i in range(BANKS + FIRST_EARLY, BANKS + EARLY_BANKS):
+            for g in range(2):
+                stage1_pass(i, g)
+        for pair in range(2, 2 + SQUARES_AHEAD):
+            square_pair(pair)
+        for i in range(PACK, BANKS):
+            scale_bank(i)
+        weave_d_on_gpsimd(1)
         for i in range(BANKS, BANKS + BANKS_BEFORE_TURNS):
             sum_and_scale(i)
 
         quantise_d(0)
-        sort_words(LOAD_TILES, LOAD_TILES, nc.vector.tensor_copy)
         quantise_d(1)
         weave_d_half(2, 0, nc.scalar.copy)
         turn(0)
@@ -327,13 +345,15 @@ def tile_readout_ntk_step_e3_kernel(tc, g_words, g_scales, phi_train, mult, phi_
         stage2(0, 0)
         quantise_d(3)
         stage2(1, 0)
-        for j in range(LOAD_TILES, 2 * LOAD_TILES):
-            turn(j)
-        for first in range(2 * LOAD_TILES, ROW_TILES, 2):
-            sort_words(first, 2, nc.scalar.copy)
+        turn(4)
+        turn(5)
         stage2(2, 0)
         stage2(3, 0)
         quantise_test(2)
+        turn(6)
+        turn(7)
+        for first in range(2 * LOAD_TILES, ROW_TILES, 2):
+            sort_words(first, 2)
         stage2(0, 1)
         stage2(1, 1)
         quantise_test(3)

@@ -28,16 +28,13 @@ LOAD_TILES = 4
 
 QUADS = [(0, 0), (1, 0), (0, 1), (1, 1)]
 
+
 VECTOR_STEPS = 32
-VECTOR_STEPS_LAST = 24
 SQUARES_AHEAD = 3
-EARLY_BANKS = 4
-G_FIRST = 1
-BEFORE = 3
-BETWEEN = 4
-FIRST_EARLY = 4
-BANKS_BEFORE_TURNS = 6
-SLOW_STORE_LAG = 4
+RUN = 8
+WHOLE = (0, 1, 2)
+SLABS = 7
+SLOTS = [1, 1, 1, 1]
 
 
 def cols(i, width):
@@ -59,7 +56,7 @@ def tile_readout_ntk_step_e3_kernel(tc, g_words, g_scales, phi_train, mult, phi_
             return work.tile(shape, dtype, name=name, bufs=bufs, align_bytes=64)
 
         def slab(shape, dtype):
-            return rotating("slab", shape, dtype, 7)
+            return rotating("slab", shape, dtype, SLABS)
 
         ident = kept("ident", [P, P], F32)
         g_scale = kept("g_scale", [P, T_GROUPS, C], U8)
@@ -71,10 +68,10 @@ def tile_readout_ntk_step_e3_kernel(tc, g_words, g_scales, phi_train, mult, phi_
         f0_sb = [kept("f0_%d" % i, [P, LOAD_TILES, C], BF16) for i in range(ROW_TILES // LOAD_TILES)]
         test_codes = kept("test_codes", [P, ROW_TILES, H_GROUPS * P], U32)
         test_scale = kept("test_scale", [P, ROW_TILES, H_GROUPS * P], U8)
-        train_sb = [slab([P, PACK, H], BF16) for g in range(T_GROUPS - 1)]
+        train_sb = {g: slab([P, PACK, H], BF16) for g in WHOLE}
         g_codes = [slab([P, T_GROUPS, N], U32) for half in range(2)]
         train_codes = [slab([P, T_GROUPS, K_PASS], U32) for hg in range(H_GROUPS)]
-        train_last = [kept("train_last%d" % hg, [P, PACK, K_PASS], BF16) for hg in range(H_GROUPS)]
+        halves = {}
 
         g_view = g_words.rearrange("g p n t -> p g (n t)")
         train_view = phi_train.rearrange("(g p j) h -> p g j h", p=P, j=PACK)
@@ -84,19 +81,19 @@ def tile_readout_ntk_step_e3_kernel(tc, g_words, g_scales, phi_train, mult, phi_
         out_view = out.rearrange("(i p j) c -> p i j c", p=P, j=LOAD_TILES)
 
         banks = []
-        a_banks, squares, d_flat, d_woven, sorted_words, test_woven, results = {}, {}, {}, {}, {}, {}, {}
-        waiting_stores = []
+        d_flat = {}
+        a_banks, squares, d_woven, sorted_words, test_woven, turned, results = {}, {}, {}, {}, {}, {}, {}
 
         def next_bank():
             banks.append(psum.tile([P, N], F32, name="bank%d" % (len(banks) % BANKS)))
             return banks[-1]
 
-
         def load_train(g):
             nc.sync.dma_start(out=train_sb[g][:], in_=train_view[:, g, :, :])
 
-        def load_train_last(hg):
-            nc.sync.dma_start(out=train_last[hg][:], in_=train_view[:, T_GROUPS - 1, :, cols(hg, K_PASS)])
+        def load_half(g, hg):
+            halves[g, hg] = rotating("half", [P, PACK, K_PASS], BF16, 2)
+            nc.sync.dma_start(out=halves[g, hg][:], in_=train_view[:, g, :, cols(hg, K_PASS)])
 
         def load_g(lo, hi, half):
             nc.sync.dma_start(
@@ -113,14 +110,11 @@ def tile_readout_ntk_step_e3_kernel(tc, g_words, g_scales, phi_train, mult, phi_
         def load_f0(i):
             nc.sync.dma_start(out=f0_sb[i][:], in_=f0_view[:, i, :, :])
 
-
-        def weave_train(g, hg):
-            last = g == T_GROUPS - 1
-            raw = train_last[hg][:] if last else train_sb[g][:, :, cols(hg, K_PASS)]
+        def weave_train(g, hg, cut=VECTOR_STEPS):
+            raw = halves[g, hg][:] if (g, hg) in halves else train_sb[g][:, :, cols(hg, K_PASS)]
             woven = rotating("train_woven", [P, PACK * K_PASS], BF16, 3)
             src = raw.rearrange("p j (m n t) -> p m t n j", n=2, t=PACK)
             dst = woven[:].rearrange("p (t m n j) -> p m t n j", t=PACK, n=2, j=PACK)
-            cut = VECTOR_STEPS_LAST if last and hg == H_GROUPS - 1 else VECTOR_STEPS
             nc.vector.tensor_copy(out=dst[:, :cut, :, :, :], in_=src[:, :cut, :, :, :])
             if (g, hg) == (0, 0):
                 src = raw.rearrange("p j (m t) -> p m j t", t=PACK)
@@ -135,56 +129,99 @@ def tile_readout_ntk_step_e3_kernel(tc, g_words, g_scales, phi_train, mult, phi_
                 out=train_codes[hg][:, g, :].bitcast(E4M3X4), scales=train_scale[:, g, cols(hg, K_PASS)], in_=woven[:]
             )
 
-        def stage1_pass(i, g):
-            hg, half = QUADS[i // PACK]
-            if g == 0:
+        woven = {}
+
+        def weave(g, hg, cut=VECTOR_STEPS):
+            woven[g, hg] = weave_train(g, hg, cut)
+
+        def quant(g, hg):
+            quantise_train(g, hg, woven[g, hg])
+            quad_group(hg, g)
+
+        def stage1_pass(i, g, e):
+            quad = i // PACK
+            hg, half = QUADS[quad]
+            slots = SLOTS[quad]
+            width = N // slots
+            region, block = divmod(i % PACK, slots)
+            t = region * slots + e
+            first = g == 0 and e == 0
+            if first:
                 a_banks[i] = next_bank()
             nc.tensor.matmul_mx(
-                out=a_banks[i][:],
-                lhsT=train_codes[hg][:, g, cols(i % PACK, P)].bitcast(E4M3X4),
-                lhsT_scale=train_scale[:, g, cols(hg * PACK + i % PACK, P)],
-                rhs=g_codes[half][:, g, :].bitcast(E5M2X4),
-                rhs_scale=g_scale[:, g, cols(half, N)],
-                start=(g == 0),
-                stop=(g == T_GROUPS - 1),
+                out=a_banks[i][:, cols(e, width)],
+                lhsT=train_codes[hg][:, g, cols(t, P)].bitcast(E4M3X4),
+                lhsT_scale=train_scale[:, g, cols(hg * PACK + t, P)],
+                rhs=g_codes[half][:, g, cols(block, width)].bitcast(E5M2X4),
+                rhs_scale=g_scale[:, g, cols(half * slots + block, width)],
+                start=first,
+                stop=(g == T_GROUPS - 1 and e == slots - 1),
             )
 
+        def quad_group(quad, g):
+            slots = SLOTS[quad]
+            for region in range(PACK // slots):
+                for e in range(slots):
+                    for block in range(slots):
+                        stage1_pass(quad * PACK + region * slots + block, g, e)
 
-        def square_pair(pair):
-            quad, first = divmod(2 * pair, PACK)
-            squares[pair] = rotating("square", [P, 2, N], F32, SQUARES_AHEAD + 1)
-            nc.scalar.activation(out=squares[pair][:], in_=mult_sb[quad][:, first : first + 2, :], func=ACT.Square)
+        def bank_groups(i, lo, hi):
+            for g in range(lo, hi):
+                for e in range(SLOTS[i // PACK]):
+                    stage1_pass(i, g, e)
 
-        def scale_bank(i, square_ahead=True):
-            quad, t = divmod(i, PACK)
-            if t == 0:
-                d_flat[quad] = rotating("d_flat", [P, PACK, N], BF16, 3)
+        def square(first, count):
+            quad, place = divmod(first, PACK)
+            slots = SLOTS[quad]
+            region, block = divmod(place, slots)
+            if first % 2 == 0:
+                squares[first // 2] = rotating("square", [P, 2 * N], F32, SQUARES_AHEAD + 1)
+            dst = squares[first // 2][:, first % 2 * N : (first % 2 + count) * N]
+            width = N // slots
+            if slots == 1:
+                src = mult_sb[quad][:, place : place + count, :]
+                nc.scalar.activation(out=dst.rearrange("p (t c) -> p t c", c=N), in_=src, func=ACT.Square)
+            else:
+                src = mult_sb[quad][:, cols(region, slots), block * width : (block + count) * width]
+                nc.scalar.activation(
+                    out=dst.rearrange("p (b e c) -> p b e c", e=slots, c=width),
+                    in_=src.rearrange("p e (b c) -> p b e c", c=width),
+                    func=ACT.Square,
+                )
+
+        def scale_bank(i):
+            quad, place = divmod(i, PACK)
+            slots = SLOTS[quad]
+            if place == 0:
+                d_flat[quad] = rotating("d_flat", [P, PACK * N], BF16, 3)
+                if slots == PACK:
+                    d_woven[quad] = d_flat[quad]
+            run = RUN // slots
             nc.vector.tensor_tensor(
-                out=d_flat[quad][:, t, :], in0=a_banks[i][:], in1=squares[i // 2][:, i % 2, :], op=ALU.mult
+                out=d_flat[quad][:, cols(place, N)].rearrange("p (c i e) -> p c e i", e=slots, i=run),
+                in0=a_banks[i][:].rearrange("p (e c i) -> p c e i", e=slots, i=run),
+                in1=squares[i // 2][:, cols(i % 2, N)].rearrange("p (e c i) -> p c e i", e=slots, i=run),
+                op=ALU.mult,
             )
-            if square_ahead and i % 2 == 1 and i // 2 + SQUARES_AHEAD < BANKS:
-                square_pair(i // 2 + SQUARES_AHEAD)
 
-        def sum_and_scale(i):
-            for g in range(2 if i < BANKS + EARLY_BANKS else 0, T_GROUPS):
-                stage1_pass(i, g)
-            scale_bank(i)
-
-        def woven_tile(quad):
+        def weave_d(quad, copy, lo=0, hi=N, view=F32):
             if quad not in d_woven:
-                d_woven[quad] = rotating("d_woven", [P, N, PACK], BF16, 3)
-            return d_woven[quad]
-
-        def weave_d_half(quad, part, copy):
-            src = d_flat[quad][:].rearrange("p t (c e) -> p c t e", e=PACK)
-            dst = woven_tile(quad)[:].rearrange("p (c e) t -> p c t e", e=PACK)
-            steps = cols(part, N // PACK // 2)
-            copy(out=dst[:, steps, :, :], in_=src[:, steps, :, :])
+                d_woven[quad] = rotating("d_woven", [P, PACK * N], BF16, 3)
+            if SLOTS[quad] == 2:
+                src = d_flat[quad][:].bitcast(view).rearrange("p (u c) -> p c u", u=2)
+                dst = d_woven[quad][:].bitcast(view).rearrange("p (c u) -> p c u", u=2)
+                copy(out=dst[:, lo:hi, :], in_=src[:, lo:hi, :])
+            else:
+                src = d_flat[quad][:].rearrange("p (t c e) -> p c t e", t=PACK, e=PACK)
+                dst = d_woven[quad][:].rearrange("p (c e t) -> p c t e", t=PACK, e=PACK)
+                copy(out=dst[:, lo // PACK : hi // PACK, :, :], in_=src[:, lo // PACK : hi // PACK, :, :])
 
         def weave_d_on_gpsimd(quad):
+            slots = SLOTS[quad]
+            d_woven[quad] = rotating("d_woven", [P, PACK * N], BF16, 3)
             nc.gpsimd.tensor_scalar(
-                out=woven_tile(quad)[:],
-                in0=d_flat[quad][:].rearrange("p t c -> p c t"),
+                out=d_woven[quad][:].rearrange("p (c u e) -> p c u e", e=slots, u=PACK // slots),
+                in0=d_flat[quad][:].rearrange("p (u c e) -> p c u e", e=slots, u=PACK // slots),
                 scalar1=1.0,
                 scalar2=0.0,
                 op0=ALU.mult,
@@ -196,35 +233,37 @@ def tile_readout_ntk_step_e3_kernel(tc, g_words, g_scales, phi_train, mult, phi_
             nc.vector.quantize_mx(
                 out=d_codes[:, hg, cols(half, N)].bitcast(E5M2X4),
                 scales=d_scale[:, hg, cols(half, N)],
-                in_=d_woven[quad][:].rearrange("p c t -> p (c t)"),
+                in_=d_woven[quad][:],
             )
 
-
-        def sort_words(first, count):
+        def sort_words(first, count, copy):
             load, row = divmod(first, LOAD_TILES)
-            if row == 0:
-                sorted_words[load] = rotating("sorted_words", [P, LOAD_TILES, H // 2], F32, 1)
+            tile = rotating("sorted_words", [P, count, H // 2], F32, 3)
+            for j in range(count):
+                sorted_words[first + j] = tile[:, j, :]
             words = test_sb[load][:, row : row + count, :].rearrange("p j h -> p (j h)").bitcast(F32)
-            nc.scalar.copy(
-                out=sorted_words[load][:, row : row + count, :].rearrange("p j (g u r) -> p (j g) r u", g=H_GROUPS, u=2),
+            copy(
+                out=tile[:].rearrange("p j (g u r) -> p (j g) r u", g=H_GROUPS, u=2),
                 in_=words.rearrange("p (g r u) -> p g r u", r=P, u=2),
             )
 
         def turn(j):
             load, row = divmod(j, LOAD_TILES)
-            bank = next_bank()
+            bank = turned[j] = next_bank()
             for hg in range(H_GROUPS):
                 for u in range(2):
-                    if load in sorted_words:
-                        words = sorted_words[load][:, row, cols(2 * hg + u, P)]
+                    if j in sorted_words:
+                        words = sorted_words[j][:, cols(2 * hg + u, P)]
                     else:
                         words = test_sb[load][:, row, :].bitcast(F32)[:, 2 * P * hg + u : 2 * P * (hg + 1) : 2]
                     nc.tensor.transpose(bank[:, cols(2 * hg + u, P)], words, ident[:])
+
+        def fetch(j, copy=nc.scalar.copy):
             if j % 2 == 0:
                 test_woven[j // 2] = rotating("test_woven", [P, 2, H], BF16, 2)
-            nc.scalar.copy(
+            copy(
                 out=test_woven[j // 2][:, j % 2, :].bitcast(F32).rearrange("p (g r u) -> p g r u", g=H_GROUPS, u=2),
-                in_=bank[:].rearrange("p (g u r) -> p g r u", g=H_GROUPS, u=2),
+                in_=turned[j][:].rearrange("p (g u r) -> p g r u", g=H_GROUPS, u=2),
             )
 
         def quantise_test(pair):
@@ -233,7 +272,6 @@ def tile_readout_ntk_step_e3_kernel(tc, g_words, g_scales, phi_train, mult, phi_
                 scales=test_scale[:, cols(pair, 2), :].rearrange("p j c -> p (j c)"),
                 in_=test_woven[pair][:].rearrange("p j c -> p (j c)"),
             )
-
 
         def stage2(j, half, on_vector=True):
             load, row = divmod(j, LOAD_TILES)
@@ -254,14 +292,16 @@ def tile_readout_ntk_step_e3_kernel(tc, g_words, g_scales, phi_train, mult, phi_
             f0_part = f0_sb[load][:, row, cols(half, N)]
             if on_vector:
                 nc.vector.tensor_tensor(out=result, in0=bank[:], in1=f0_part, op=ALU.add)
-                nc.sync.dma_start(out=out_view[:, load, row, cols(half, N)], in_=result)
             else:
                 nc.scalar.copy(out=result, in_=bank[:])
                 nc.gpsimd.tensor_tensor(out=result, in0=result, in1=f0_part, op=ALU.add)
-                waiting_stores.append((len(banks) + SLOW_STORE_LAG, out_view[:, load, row, cols(half, N)], result))
-            while waiting_stores and waiting_stores[0][0] <= len(banks):
-                due, target, source = waiting_stores.pop(0)
-                nc.sync.dma_start(out=target, in_=source)
+
+        def store(j, count=1, half=None):
+            load, row = divmod(j, LOAD_TILES)
+            part = slice(0, C) if half is None else cols(half, N)
+            nc.sync.dma_start(
+                out=out_view[:, load, row : row + count, part], in_=results[j // 2][:, j % 2 : j % 2 + count, part]
+            )
 
         nc.vector.memset(g_scale[:].rearrange("p g n -> p (g n)").bitcast(U32), 0)
         make_identity(nc, ident[:])
@@ -272,105 +312,131 @@ def tile_readout_ntk_step_e3_kernel(tc, g_words, g_scales, phi_train, mult, phi_
             )
 
         load_train(0)
-        for g in range(T_GROUPS - 2):
-            load_train(g + 1)
-            load_g(g, g + 1, 0)
-        load_train_last(0)
-        load_g(T_GROUPS - 2, T_GROUPS, 0)
+        load_train(1)
+        load_g(0, 1, 0)
+        load_train(2)
+        load_g(1, 2, 0)
+        load_half(3, 0)
+        load_g(2, 4, 0)
         load_mult(0)
-        if G_FIRST:
-            load_g(0, 2, 1)
-        load_train_last(1)
-        if not G_FIRST:
-            load_g(0, 2, 1)
+        load_half(3, 1)
+        load_g(0, 2, 1)
         load_mult(1)
         load_g(2, 4, 1)
-        for quad in range(2, len(QUADS)):
-            load_mult(quad)
-        for i in range(ROW_TILES // LOAD_TILES):
-            load_test(i)
-            load_f0(i)
+        load_mult(2)
+        load_mult(3)
+        load_test(0)
+        load_test(1)
+        load_f0(0)
+        load_test(2)
+        load_f0(1)
+        load_f0(2)
 
-        pieces = sorted(((g, hg) for g in range(T_GROUPS) for hg in range(H_GROUPS)), key=lambda x: (x[0] + x[1], x[1]))
-        woven = [weave_train(*pieces[0])]
-        for i, (g, hg) in enumerate(pieces[:-1]):
-            if i + 2 < len(pieces):
-                woven.append(weave_train(*pieces[i + 1]))
-            quantise_train(g, hg, woven[i])
-            for t in range(PACK):
-                stage1_pass(hg * PACK + t, g)
-        for pair in range(2):
-            square_pair(pair)
-        for i in range(BEFORE):
-            scale_bank(i, False)
-        last = weave_train(*pieces[-1])
-        for i in range(BEFORE, BETWEEN):
-            scale_bank(i, False)
-        quantise_train(*pieces[-1], last)
-        for i in range(BETWEEN, PACK):
-            scale_bank(i, False)
+        weave(0, 0)
+        weave(0, 1)
+        quant(0, 0)
+        weave(1, 0)
+        quant(0, 1)
+        weave(1, 1)
+        quant(1, 0)
+        weave(2, 0)
+        quant(1, 1)
+        weave(2, 1)
+        quant(2, 0)
+        weave(3, 0, 40)
+        quant(3, 0)
+        quant(2, 1)
+        square(0, 1)
+        square(1, 1)
+        scale_bank(0)
+        weave(3, 1, 32)
+        square(2, 1)
+        square(3, 1)
+        scale_bank(1)
+        quantise_train(3, 1, woven[3, 1])
+        scale_bank(2)
+        scale_bank(3)
         weave_d_on_gpsimd(0)
-        for i in range(BANKS, BANKS + FIRST_EARLY):
-            for g in range(2):
-                stage1_pass(i, g)
-        for t in range(PACK):
-            stage1_pass(PACK + t, T_GROUPS - 1)
-        for i in range(BANKS + FIRST_EARLY, BANKS + EARLY_BANKS):
-            for g in range(2):
-                stage1_pass(i, g)
-        for pair in range(2, 2 + SQUARES_AHEAD):
-            square_pair(pair)
-        for i in range(PACK, BANKS):
+        bank_groups(8, 0, 2)
+        bank_groups(9, 0, 2)
+        quad_group(1, 3)
+        bank_groups(10, 0, 2)
+        bank_groups(11, 0, 2)
+        square(4, 2)
+        square(6, 2)
+        square(8, 2)
+        for i in range(4, 8):
             scale_bank(i)
+            if i % 2:
+                square(i + 5, 2)
         weave_d_on_gpsimd(1)
-        for i in range(BANKS, BANKS + BANKS_BEFORE_TURNS):
-            sum_and_scale(i)
-
+        for i in range(8, 14):
+            bank_groups(i, 2 if i < 12 else 0, 4)
+            scale_bank(i)
+            if i == 9:
+                square(14, 2)
         quantise_d(0)
         quantise_d(1)
-        weave_d_half(2, 0, nc.scalar.copy)
-        turn(0)
-        turn(1)
-        quantise_test(0)
-        weave_d_half(2, 1, nc.scalar.copy)
-        sum_and_scale(2 * BANKS - 2)
-        turn(2)
-        turn(3)
-        quantise_d(2)
-        sum_and_scale(2 * BANKS - 1)
-        quantise_test(1)
 
-        weave_d_half(3, 1, nc.scalar.copy)
-        weave_d_half(3, 0, nc.vector.tensor_copy)
+        weave_d(2, nc.scalar.copy, 0, 256)
+        for j in range(4):
+            turn(j)
+            fetch(j)
+        weave_d(2, nc.scalar.copy, 256, 512)
+        sort_words(4, 2, nc.vector.tensor_copy)
+        quantise_test(0)
+        bank_groups(14, 0, 4)
+        scale_bank(14)
+        quantise_test(1)
+        bank_groups(15, 0, 4)
+        scale_bank(15)
+        quantise_d(2)
+        sort_words(6, 2, nc.scalar.copy)
+        weave_d(3, nc.scalar.copy, 256, 512)
+        weave_d(3, nc.vector.tensor_copy, 0, 256)
         stage2(0, 0)
-        quantise_d(3)
         stage2(1, 0)
-        turn(4)
-        turn(5)
+        store(0, 2, 0)
+        quantise_d(3)
         stage2(2, 0)
         stage2(3, 0)
+        store(2, 2, 0)
+        for j in range(4, 8):
+            turn(j)
+            fetch(j)
         quantise_test(2)
-        turn(6)
-        turn(7)
-        for first in range(2 * LOAD_TILES, ROW_TILES, 2):
-            sort_words(first, 2)
+        sort_words(8, 2, nc.scalar.copy)
         stage2(0, 1)
         stage2(1, 1)
+        store(0, 2, 1)
         quantise_test(3)
-        stage2(2, 1)
+        stage2(2, 1, False)
+        sort_words(10, 2, nc.scalar.copy)
         stage2(3, 1)
+        stage2(4, 0)
+        store(2, 2, 1)
+        stage2(4, 1, False)
+        stage2(5, 0)
+        stage2(5, 1)
+        store(5)
+        store(4)
+        for j in range(8, 12):
+            turn(j)
+            fetch(j)
 
-        pairs = ROW_TILES // 2
-        turned_pairs = 2 * LOAD_TILES // 2
-        for pair in range(LOAD_TILES // 2, pairs):
-            ahead = pair + 1
-            fresh = turned_pairs <= ahead < pairs
-            if fresh:
-                turn(2 * ahead)
-                turn(2 * ahead + 1)
-            stage2(2 * pair, 0)
-            if fresh:
-                quantise_test(ahead)
-            stage2(2 * pair, 1)
-            stage2(2 * pair + 1, 0, on_vector=(pair == pairs - 1))
-            stage2(2 * pair + 1, 1)
+        quantise_test(4)
+        stage2(6, 0)
+        stage2(6, 1)
+        store(6)
+        quantise_test(5)
+        stage2(7, 0, False)
+        stage2(7, 1)
+        store(7, 1, 1)
+        stage2(8, 0)
+        stage2(8, 1)
+        store(7, 1, 0)
+        store(8)
+        for j in range(9, 12):
+            stage2(j, 0)
+            stage2(j, 1)
+            store(j)

@@ -326,10 +326,10 @@ def tile_readout_ntk_step_e3_kernel(tc, g_words, g_scales, phi_train, mult, phi_
         load_mult(2)
         load_mult(3)
         load_test(0)
-        load_test(1)
         load_f0(0)
-        load_test(2)
+        load_test(1)
         load_f0(1)
+        load_test(2)
         load_f0(2)
 
         weave(0, 0)
@@ -379,64 +379,69 @@ def tile_readout_ntk_step_e3_kernel(tc, g_words, g_scales, phi_train, mult, phi_
         quantise_d(1)
 
         weave_d(2, nc.scalar.copy, 0, 256)
-        for j in range(4):
+        for j in (0, 1):
             turn(j)
             fetch(j)
-        weave_d(2, nc.scalar.copy, 256, 512)
-        sort_words(4, 2, nc.vector.tensor_copy)
         quantise_test(0)
+        weave_d(2, nc.scalar.copy, 256, 512)
         bank_groups(14, 0, 4)
         scale_bank(14)
-        quantise_test(1)
+        for j in (2, 3):
+            turn(j)
+            fetch(j)
+        quantise_d(2)
         bank_groups(15, 0, 4)
         scale_bank(15)
-        quantise_d(2)
-        sort_words(6, 2, nc.scalar.copy)
+        quantise_test(1)
         weave_d(3, nc.scalar.copy, 256, 512)
         weave_d(3, nc.vector.tensor_copy, 0, 256)
         stage2(0, 0)
-        stage2(1, 0)
-        store(0, 2, 0)
+        store(0, 1, 0)
         quantise_d(3)
-        stage2(2, 0)
-        stage2(3, 0)
-        store(2, 2, 0)
-        for j in range(4, 8):
+        stage2(1, 0)
+        store(1, 1, 0)
+        for j in (4, 5):
             turn(j)
             fetch(j)
-        quantise_test(2)
-        sort_words(8, 2, nc.scalar.copy)
-        stage2(0, 1)
-        stage2(1, 1)
-        store(0, 2, 1)
-        quantise_test(3)
-        stage2(2, 1, False)
-        sort_words(10, 2, nc.scalar.copy)
-        stage2(3, 1)
-        stage2(4, 0)
-        store(2, 2, 1)
-        stage2(4, 1, False)
-        stage2(5, 0)
-        stage2(5, 1)
-        store(5)
-        store(4)
-        for j in range(8, 12):
-            turn(j)
-            fetch(j)
-
-        quantise_test(4)
-        stage2(6, 0)
-        stage2(6, 1)
-        store(6)
-        quantise_test(5)
-        stage2(7, 0, False)
-        stage2(7, 1)
-        store(7, 1, 1)
-        stage2(8, 0)
-        stage2(8, 1)
-        store(7, 1, 0)
-        store(8)
-        for j in range(9, 12):
+        for j in (2, 3):
             stage2(j, 0)
+            store(j, 1, 0)
+        quantise_test(2)
+        for j in (6, 7):
+            turn(j)
+            fetch(j)
+        sort_words(8, 2, nc.scalar.copy)
+        sort_words(10, 2, nc.scalar.copy)
+        for j in (0, 1):
             stage2(j, 1)
-            store(j)
+            store(j, 1, 1)
+        quantise_test(3)
+        for j in (2, 3):
+            stage2(j, 1)
+            store(j, 1, 1)
+
+        late = None
+        for pair in range(2, 6):
+            ahead = pair + 1
+            fresh = 4 <= ahead < 6
+            if fresh:
+                for j in (2 * ahead, 2 * ahead + 1):
+                    turn(j)
+                    fetch(j)
+            stage2(2 * pair, 0)
+            store(2 * pair, 1, 0)
+            if late is not None and fresh:
+                store(late, 1, 0)
+                late = None
+            if fresh:
+                quantise_test(ahead)
+            stage2(2 * pair, 1)
+            store(2 * pair, 1, 1)
+            stage2(2 * pair + 1, 0, on_vector=(pair == 5))
+            if pair == 5:
+                store(2 * pair + 1, 1, 0)
+                store(late, 1, 0)
+            else:
+                late = 2 * pair + 1
+            stage2(2 * pair + 1, 1)
+            store(2 * pair + 1, 1, 1)

@@ -28,13 +28,12 @@ LOAD_TILES = 4
 
 QUADS = [(0, 0), (1, 0), (0, 1), (1, 1)]
 
-
-VECTOR_STEPS = 32
-SQUARES_AHEAD = 3
-RUN = 8
-WHOLE = (0, 1, 2)
-SLABS = 7
-SLOTS = [1, 1, 1, 1]
+VECTOR_STEPS = 30
+VECTOR_STEPS_LAST = 32
+GPSIMD_COLUMNS = 320
+VECTOR_COLUMNS_LAST = 192
+SLOW_STORE_LAG = 4
+SQUARE_TILES = 4
 
 
 def cols(i, width):
@@ -56,7 +55,7 @@ def tile_readout_ntk_step_e3_kernel(tc, g_words, g_scales, phi_train, mult, phi_
             return work.tile(shape, dtype, name=name, bufs=bufs, align_bytes=64)
 
         def slab(shape, dtype):
-            return rotating("slab", shape, dtype, SLABS)
+            return rotating("slab", shape, dtype, 7)
 
         ident = kept("ident", [P, P], F32)
         g_scale = kept("g_scale", [P, T_GROUPS, C], U8)
@@ -68,10 +67,10 @@ def tile_readout_ntk_step_e3_kernel(tc, g_words, g_scales, phi_train, mult, phi_
         f0_sb = [kept("f0_%d" % i, [P, LOAD_TILES, C], BF16) for i in range(ROW_TILES // LOAD_TILES)]
         test_codes = kept("test_codes", [P, ROW_TILES, H_GROUPS * P], U32)
         test_scale = kept("test_scale", [P, ROW_TILES, H_GROUPS * P], U8)
-        train_sb = {g: slab([P, PACK, H], BF16) for g in WHOLE}
+        train_sb = [slab([P, PACK, H], BF16) for g in range(T_GROUPS - 1)]
         g_codes = [slab([P, T_GROUPS, N], U32) for half in range(2)]
         train_codes = [slab([P, T_GROUPS, K_PASS], U32) for hg in range(H_GROUPS)]
-        halves = {}
+        train_last = [kept("train_last%d" % hg, [P, PACK, K_PASS], BF16) for hg in range(H_GROUPS)]
 
         g_view = g_words.rearrange("g p n t -> p g (n t)")
         train_view = phi_train.rearrange("(g p j) h -> p g j h", p=P, j=PACK)
@@ -81,19 +80,20 @@ def tile_readout_ntk_step_e3_kernel(tc, g_words, g_scales, phi_train, mult, phi_
         out_view = out.rearrange("(i p j) c -> p i j c", p=P, j=LOAD_TILES)
 
         banks = []
-        d_flat = {}
-        a_banks, squares, d_woven, sorted_words, test_woven, turned, results = {}, {}, {}, {}, {}, {}, {}
+        a_banks, squares, d_flat, d_woven, sorted_words, test_woven, results = {}, {}, {}, {}, {}, {}, {}
+        train_woven = {}
+        stored, waiting_stores = [], []
 
         def next_bank():
             banks.append(psum.tile([P, N], F32, name="bank%d" % (len(banks) % BANKS)))
             return banks[-1]
 
+
         def load_train(g):
             nc.sync.dma_start(out=train_sb[g][:], in_=train_view[:, g, :, :])
 
-        def load_half(g, hg):
-            halves[g, hg] = rotating("half", [P, PACK, K_PASS], BF16, 2)
-            nc.sync.dma_start(out=halves[g, hg][:], in_=train_view[:, g, :, cols(hg, K_PASS)])
+        def load_train_last(hg):
+            nc.sync.dma_start(out=train_last[hg][:], in_=train_view[:, T_GROUPS - 1, :, cols(hg, K_PASS)])
 
         def load_g(lo, hi, half):
             nc.sync.dma_start(
@@ -110,11 +110,14 @@ def tile_readout_ntk_step_e3_kernel(tc, g_words, g_scales, phi_train, mult, phi_
         def load_f0(i):
             nc.sync.dma_start(out=f0_sb[i][:], in_=f0_view[:, i, :, :])
 
-        def weave_train(g, hg, cut=VECTOR_STEPS):
-            raw = halves[g, hg][:] if (g, hg) in halves else train_sb[g][:, :, cols(hg, K_PASS)]
-            woven = rotating("train_woven", [P, PACK * K_PASS], BF16, 3)
+
+        def weave_train(g, hg):
+            last = g == T_GROUPS - 1
+            raw = train_last[hg][:] if last else train_sb[g][:, :, cols(hg, K_PASS)]
+            woven = train_woven[g, hg] = rotating("train_woven", [P, PACK * K_PASS], BF16, 3)
             src = raw.rearrange("p j (m n t) -> p m t n j", n=2, t=PACK)
             dst = woven[:].rearrange("p (t m n j) -> p m t n j", t=PACK, n=2, j=PACK)
+            cut = VECTOR_STEPS_LAST if last and hg == H_GROUPS - 1 else VECTOR_STEPS
             nc.vector.tensor_copy(out=dst[:, :cut, :, :, :], in_=src[:, :cut, :, :, :])
             if (g, hg) == (0, 0):
                 src = raw.rearrange("p j (m t) -> p m j t", t=PACK)
@@ -122,106 +125,74 @@ def tile_readout_ntk_step_e3_kernel(tc, g_words, g_scales, phi_train, mult, phi_
                 nc.scalar.activation(out=dst[:, 2 * cut :, :, :], in_=src[:, 2 * cut :, :, :], func=ACT.Copy)
             else:
                 nc.scalar.copy(out=dst[:, cut:, :, :, :], in_=src[:, cut:, :, :, :])
-            return woven
 
-        def quantise_train(g, hg, woven):
+        def quantise_train(g, hg):
             nc.vector.quantize_mx(
-                out=train_codes[hg][:, g, :].bitcast(E4M3X4), scales=train_scale[:, g, cols(hg, K_PASS)], in_=woven[:]
+                out=train_codes[hg][:, g, :].bitcast(E4M3X4),
+                scales=train_scale[:, g, cols(hg, K_PASS)],
+                in_=train_woven[g, hg][:],
             )
 
-        woven = {}
-
-        def weave(g, hg, cut=VECTOR_STEPS):
-            woven[g, hg] = weave_train(g, hg, cut)
-
-        def quant(g, hg):
-            quantise_train(g, hg, woven[g, hg])
-            quad_group(hg, g)
-
-        def stage1_pass(i, g, e):
-            quad = i // PACK
-            hg, half = QUADS[quad]
-            slots = SLOTS[quad]
-            width = N // slots
-            region, block = divmod(i % PACK, slots)
-            t = region * slots + e
-            first = g == 0 and e == 0
-            if first:
+        def stage1_pass(i, g):
+            hg, half = QUADS[i // PACK]
+            if g == 0:
                 a_banks[i] = next_bank()
             nc.tensor.matmul_mx(
-                out=a_banks[i][:, cols(e, width)],
-                lhsT=train_codes[hg][:, g, cols(t, P)].bitcast(E4M3X4),
-                lhsT_scale=train_scale[:, g, cols(hg * PACK + t, P)],
-                rhs=g_codes[half][:, g, cols(block, width)].bitcast(E5M2X4),
-                rhs_scale=g_scale[:, g, cols(half * slots + block, width)],
-                start=first,
-                stop=(g == T_GROUPS - 1 and e == slots - 1),
+                out=a_banks[i][:],
+                lhsT=train_codes[hg][:, g, cols(i % PACK, P)].bitcast(E4M3X4),
+                lhsT_scale=train_scale[:, g, cols(hg * PACK + i % PACK, P)],
+                rhs=g_codes[half][:, g, :].bitcast(E5M2X4),
+                rhs_scale=g_scale[:, g, cols(half, N)],
+                start=(g == 0),
+                stop=(g == T_GROUPS - 1),
             )
+
+        def stage1_passes(i, lo, hi):
+            for g in range(lo, hi):
+                stage1_pass(i, g)
 
         def quad_group(quad, g):
-            slots = SLOTS[quad]
-            for region in range(PACK // slots):
-                for e in range(slots):
-                    for block in range(slots):
-                        stage1_pass(quad * PACK + region * slots + block, g, e)
+            for t in range(PACK):
+                stage1_pass(quad * PACK + t, g)
 
-        def bank_groups(i, lo, hi):
-            for g in range(lo, hi):
-                for e in range(SLOTS[i // PACK]):
-                    stage1_pass(i, g, e)
 
         def square(first, count):
-            quad, place = divmod(first, PACK)
-            slots = SLOTS[quad]
-            region, block = divmod(place, slots)
+            quad, t = divmod(first, PACK)
             if first % 2 == 0:
-                squares[first // 2] = rotating("square", [P, 2 * N], F32, SQUARES_AHEAD + 1)
-            dst = squares[first // 2][:, first % 2 * N : (first % 2 + count) * N]
-            width = N // slots
-            if slots == 1:
-                src = mult_sb[quad][:, place : place + count, :]
-                nc.scalar.activation(out=dst.rearrange("p (t c) -> p t c", c=N), in_=src, func=ACT.Square)
-            else:
-                src = mult_sb[quad][:, cols(region, slots), block * width : (block + count) * width]
-                nc.scalar.activation(
-                    out=dst.rearrange("p (b e c) -> p b e c", e=slots, c=width),
-                    in_=src.rearrange("p e (b c) -> p b e c", c=width),
-                    func=ACT.Square,
-                )
-
-        def scale_bank(i):
-            quad, place = divmod(i, PACK)
-            slots = SLOTS[quad]
-            if place == 0:
-                d_flat[quad] = rotating("d_flat", [P, PACK * N], BF16, 3)
-                if slots == PACK:
-                    d_woven[quad] = d_flat[quad]
-            run = RUN // slots
-            nc.vector.tensor_tensor(
-                out=d_flat[quad][:, cols(place, N)].rearrange("p (c i e) -> p c e i", e=slots, i=run),
-                in0=a_banks[i][:].rearrange("p (e c i) -> p c e i", e=slots, i=run),
-                in1=squares[i // 2][:, cols(i % 2, N)].rearrange("p (e c i) -> p c e i", e=slots, i=run),
-                op=ALU.mult,
+                squares[first // 2] = rotating("square", [P, 2, N], F32, SQUARE_TILES)
+            nc.scalar.activation(
+                out=squares[first // 2][:, first % 2 : first % 2 + count, :],
+                in_=mult_sb[quad][:, t : t + count, :],
+                func=ACT.Square,
             )
 
-        def weave_d(quad, copy, lo=0, hi=N, view=F32):
-            if quad not in d_woven:
-                d_woven[quad] = rotating("d_woven", [P, PACK * N], BF16, 3)
-            if SLOTS[quad] == 2:
-                src = d_flat[quad][:].bitcast(view).rearrange("p (u c) -> p c u", u=2)
-                dst = d_woven[quad][:].bitcast(view).rearrange("p (c u) -> p c u", u=2)
-                copy(out=dst[:, lo:hi, :], in_=src[:, lo:hi, :])
-            else:
-                src = d_flat[quad][:].rearrange("p (t c e) -> p c t e", t=PACK, e=PACK)
-                dst = d_woven[quad][:].rearrange("p (c e t) -> p c t e", t=PACK, e=PACK)
-                copy(out=dst[:, lo // PACK : hi // PACK, :, :], in_=src[:, lo // PACK : hi // PACK, :, :])
+        def scale_bank(i):
+            quad, t = divmod(i, PACK)
+            if t == 0:
+                d_flat[quad] = rotating("d_flat", [P, PACK, N], BF16, 3)
+            nc.vector.tensor_tensor(
+                out=d_flat[quad][:, t, :], in0=a_banks[i][:], in1=squares[i // 2][:, i % 2, :], op=ALU.mult
+            )
 
-        def weave_d_on_gpsimd(quad):
-            slots = SLOTS[quad]
-            d_woven[quad] = rotating("d_woven", [P, PACK * N], BF16, 3)
+        def sum_and_scale(i):
+            stage1_passes(i, 0, T_GROUPS)
+            scale_bank(i)
+
+        def woven_tile(quad):
+            if quad not in d_woven:
+                d_woven[quad] = rotating("d_woven", [P, N, PACK], BF16, 3)
+            return d_woven[quad]
+
+        def weave_d(quad, lo, hi, copy):
+            src = d_flat[quad][:].rearrange("p t (c e) -> p c t e", e=PACK)
+            dst = woven_tile(quad)[:].rearrange("p (c e) t -> p c t e", e=PACK)
+            steps = slice(lo // PACK, hi // PACK)
+            copy(out=dst[:, steps, :, :], in_=src[:, steps, :, :])
+
+        def weave_d_on_gpsimd(quad, hi):
             nc.gpsimd.tensor_scalar(
-                out=d_woven[quad][:].rearrange("p (c u e) -> p c u e", e=slots, u=PACK // slots),
-                in0=d_flat[quad][:].rearrange("p (u c e) -> p c u e", e=slots, u=PACK // slots),
+                out=woven_tile(quad)[:, :hi, :],
+                in0=d_flat[quad][:].rearrange("p t c -> p c t")[:, :hi, :],
                 scalar1=1.0,
                 scalar2=0.0,
                 op0=ALU.mult,
@@ -233,23 +204,24 @@ def tile_readout_ntk_step_e3_kernel(tc, g_words, g_scales, phi_train, mult, phi_
             nc.vector.quantize_mx(
                 out=d_codes[:, hg, cols(half, N)].bitcast(E5M2X4),
                 scales=d_scale[:, hg, cols(half, N)],
-                in_=d_woven[quad][:],
+                in_=d_woven[quad][:].rearrange("p c t -> p (c t)"),
             )
 
-        def sort_words(first, count, copy):
+
+        def sort_words(first):
             load, row = divmod(first, LOAD_TILES)
-            tile = rotating("sorted_words", [P, count, H // 2], F32, 3)
-            for j in range(count):
+            tile = rotating("sorted_words", [P, 2, H // 2], F32, 2)
+            for j in range(2):
                 sorted_words[first + j] = tile[:, j, :]
-            words = test_sb[load][:, row : row + count, :].rearrange("p j h -> p (j h)").bitcast(F32)
-            copy(
+            words = test_sb[load][:, row : row + 2, :].rearrange("p j h -> p (j h)").bitcast(F32)
+            nc.scalar.copy(
                 out=tile[:].rearrange("p j (g u r) -> p (j g) r u", g=H_GROUPS, u=2),
                 in_=words.rearrange("p (g r u) -> p g r u", r=P, u=2),
             )
 
         def turn(j):
             load, row = divmod(j, LOAD_TILES)
-            bank = turned[j] = next_bank()
+            bank = next_bank()
             for hg in range(H_GROUPS):
                 for u in range(2):
                     if j in sorted_words:
@@ -257,14 +229,16 @@ def tile_readout_ntk_step_e3_kernel(tc, g_words, g_scales, phi_train, mult, phi_
                     else:
                         words = test_sb[load][:, row, :].bitcast(F32)[:, 2 * P * hg + u : 2 * P * (hg + 1) : 2]
                     nc.tensor.transpose(bank[:, cols(2 * hg + u, P)], words, ident[:])
-
-        def fetch(j, copy=nc.scalar.copy):
             if j % 2 == 0:
                 test_woven[j // 2] = rotating("test_woven", [P, 2, H], BF16, 2)
-            copy(
+            nc.scalar.copy(
                 out=test_woven[j // 2][:, j % 2, :].bitcast(F32).rearrange("p (g r u) -> p g r u", g=H_GROUPS, u=2),
-                in_=turned[j][:].rearrange("p (g u r) -> p g r u", g=H_GROUPS, u=2),
+                in_=bank[:].rearrange("p (g u r) -> p g r u", g=H_GROUPS, u=2),
             )
+
+        def turn_tiles(lo, hi):
+            for j in range(lo, hi):
+                turn(j)
 
         def quantise_test(pair):
             nc.vector.quantize_mx(
@@ -273,7 +247,8 @@ def tile_readout_ntk_step_e3_kernel(tc, g_words, g_scales, phi_train, mult, phi_
                 in_=test_woven[pair][:].rearrange("p j c -> p (j c)"),
             )
 
-        def stage2(j, half, on_vector=True):
+
+        def stage2(j, half, on_vector=True, then_quantise=None):
             load, row = divmod(j, LOAD_TILES)
             bank = next_bank()
             for hg in range(H_GROUPS):
@@ -295,13 +270,17 @@ def tile_readout_ntk_step_e3_kernel(tc, g_words, g_scales, phi_train, mult, phi_
             else:
                 nc.scalar.copy(out=result, in_=bank[:])
                 nc.gpsimd.tensor_tensor(out=result, in0=result, in1=f0_part, op=ALU.add)
-
-        def store(j, count=1, half=None):
-            load, row = divmod(j, LOAD_TILES)
-            part = slice(0, C) if half is None else cols(half, N)
-            nc.sync.dma_start(
-                out=out_view[:, load, row : row + count, part], in_=results[j // 2][:, j % 2 : j % 2 + count, part]
-            )
+            if then_quantise:
+                quantise_test(then_quantise)
+            stored.append((j, half))
+            waiting_stores.append((len(stored) + (0 if on_vector else SLOW_STORE_LAG), j, half))
+            for due, tile, part in sorted(waiting_stores):
+                if due <= len(stored):
+                    waiting_stores.remove((due, tile, part))
+                    nc.sync.dma_start(
+                        out=out_view[:, tile // LOAD_TILES, tile % LOAD_TILES, cols(part, N)],
+                        in_=results[tile // 2][:, tile % 2, cols(part, N)],
+                    )
 
         nc.vector.memset(g_scale[:].rearrange("p g n -> p (g n)").bitcast(U32), 0)
         make_identity(nc, ident[:])
@@ -311,137 +290,93 @@ def tile_readout_ntk_step_e3_kernel(tc, g_words, g_scales, phi_train, mult, phi_
                 in_=g_scales[:, r:16:4, :].rearrange("g q n -> q g n").bitcast(I32),
             )
 
+        last = T_GROUPS - 1
         load_train(0)
         load_train(1)
         load_g(0, 1, 0)
         load_train(2)
-        load_g(1, 2, 0)
-        load_half(3, 0)
-        load_g(2, 4, 0)
-        load_mult(0)
-        load_half(3, 1)
-        load_g(0, 2, 1)
-        load_mult(1)
-        load_g(2, 4, 1)
+        load_g(1, last, 0)
+        for hg in range(H_GROUPS):
+            load_train_last(hg)
+        load_g(last, T_GROUPS, 0)
+        for part in range(2):
+            load_mult(part)
+            load_g(2 * part, 2 * part + 2, 1)
         load_mult(2)
         load_mult(3)
         load_test(0)
-        load_f0(0)
-        load_test(1)
-        load_f0(1)
-        load_test(2)
-        load_f0(2)
+        for i in range(1, ROW_TILES // LOAD_TILES):
+            load_test(i)
+            load_f0(i - 1)
+        load_f0(ROW_TILES // LOAD_TILES - 1)
 
-        weave(0, 0)
-        weave(0, 1)
-        quant(0, 0)
-        weave(1, 0)
-        quant(0, 1)
-        weave(1, 1)
-        quant(1, 0)
-        weave(2, 0)
-        quant(1, 1)
-        weave(2, 1)
-        quant(2, 0)
-        weave(3, 0, 40)
-        quant(3, 0)
-        quant(2, 1)
-        square(0, 1)
-        square(1, 1)
-        scale_bank(0)
-        weave(3, 1, 32)
-        square(2, 1)
-        square(3, 1)
-        scale_bank(1)
-        quantise_train(3, 1, woven[3, 1])
-        scale_bank(2)
-        scale_bank(3)
-        weave_d_on_gpsimd(0)
-        bank_groups(8, 0, 2)
-        bank_groups(9, 0, 2)
-        quad_group(1, 3)
-        bank_groups(10, 0, 2)
-        bank_groups(11, 0, 2)
+        pieces = [(g, hg) for g in range(T_GROUPS) for hg in range(H_GROUPS)]
+        weave_train(*pieces[0])
+        for i, (g, hg) in enumerate(pieces):
+            if i + 1 < len(pieces):
+                weave_train(*pieces[i + 1])
+            quantise_train(g, hg)
+            quad_group(hg, g)
+
+        for i in range(PACK):
+            square(i, 1)
         square(4, 2)
         square(6, 2)
+        for i in range(PACK):
+            scale_bank(i)
+        weave_d_on_gpsimd(0, N)
+
+        for i in range(BANKS, BANKS + PACK):
+            stage1_passes(i, 0, 2)
         square(8, 2)
-        for i in range(4, 8):
+        for i in range(PACK, BANKS):
             scale_bank(i)
             if i % 2:
                 square(i + 5, 2)
-        weave_d_on_gpsimd(1)
-        for i in range(8, 14):
-            bank_groups(i, 2 if i < 12 else 0, 4)
+        weave_d_on_gpsimd(1, GPSIMD_COLUMNS)
+        for i in range(BANKS, BANKS + PACK):
+            stage1_passes(i, 2, T_GROUPS)
             scale_bank(i)
-            if i == 9:
+            if i == BANKS + 1:
                 square(14, 2)
+
+        sum_and_scale(12)
+        weave_d(2, 0, N // 2, nc.scalar.copy)
+        sum_and_scale(13)
+        weave_d(1, GPSIMD_COLUMNS, N, nc.vector.tensor_copy)
+        turn_tiles(0, 3)
         quantise_d(0)
         quantise_d(1)
-
-        weave_d(2, nc.scalar.copy, 0, 256)
-        for j in (0, 1):
-            turn(j)
-            fetch(j)
+        weave_d(2, N // 2, N, nc.scalar.copy)
         quantise_test(0)
-        weave_d(2, nc.scalar.copy, 256, 512)
-        bank_groups(14, 0, 4)
-        scale_bank(14)
-        for j in (2, 3):
-            turn(j)
-            fetch(j)
+        sum_and_scale(14)
+        sum_and_scale(15)
         quantise_d(2)
-        bank_groups(15, 0, 4)
-        scale_bank(15)
-        quantise_test(1)
-        weave_d(3, nc.scalar.copy, 256, 512)
-        weave_d(3, nc.vector.tensor_copy, 0, 256)
-        stage2(0, 0)
-        store(0, 1, 0)
-        quantise_d(3)
-        stage2(1, 0)
-        store(1, 1, 0)
-        for j in (4, 5):
-            turn(j)
-            fetch(j)
-        for j in (2, 3):
-            stage2(j, 0)
-            store(j, 1, 0)
-        quantise_test(2)
-        for j in (6, 7):
-            turn(j)
-            fetch(j)
-        sort_words(8, 2, nc.scalar.copy)
-        sort_words(10, 2, nc.scalar.copy)
-        for j in (0, 1):
-            stage2(j, 1)
-            store(j, 1, 1)
-        quantise_test(3)
-        for j in (2, 3):
-            stage2(j, 1)
-            store(j, 1, 1)
 
-        late = None
-        for pair in range(2, 6):
-            ahead = pair + 1
-            fresh = 4 <= ahead < 6
-            if fresh:
-                for j in (2 * ahead, 2 * ahead + 1):
-                    turn(j)
-                    fetch(j)
-            stage2(2 * pair, 0)
-            store(2 * pair, 1, 0)
-            if late is not None and fresh:
-                store(late, 1, 0)
-                late = None
-            if fresh:
-                quantise_test(ahead)
-            stage2(2 * pair, 1)
-            store(2 * pair, 1, 1)
-            stage2(2 * pair + 1, 0, on_vector=(pair == 5))
-            if pair == 5:
-                store(2 * pair + 1, 1, 0)
-                store(late, 1, 0)
-            else:
-                late = 2 * pair + 1
-            stage2(2 * pair + 1, 1)
-            store(2 * pair + 1, 1, 1)
+        turn_tiles(3, 4)
+        weave_d(3, VECTOR_COLUMNS_LAST, N, nc.scalar.copy)
+        turn_tiles(4, 6)
+        quantise_test(1)
+        weave_d(3, 0, VECTOR_COLUMNS_LAST, nc.vector.tensor_copy)
+
+        for j in range(LOAD_TILES):
+            stage2(j, 0)
+            if j == 1:
+                quantise_d(3)
+        quantise_test(2)
+        turn_tiles(6, 8)
+        for first in range(2 * LOAD_TILES, ROW_TILES, 2):
+            sort_words(first)
+        for j in range(LOAD_TILES):
+            stage2(j, 1)
+            if j == 1:
+                quantise_test(3)
+
+        turn_before = {(6, 0): 4, (7, 1): 5}
+        slow_banks = [(4, 1), (8, 0)]
+        for j in range(LOAD_TILES, ROW_TILES):
+            for half in range(2):
+                pair = turn_before.get((j, half))
+                if pair:
+                    turn_tiles(2 * pair, 2 * pair + 2)
+                stage2(j, half, (j, half) not in slow_banks, pair)

@@ -28,7 +28,7 @@ LOAD_TILES = 4
 
 QUADS = [(0, 0), (1, 0), (0, 1), (1, 1)]
 
-VECTOR_STEPS = 30
+VECTOR_STEPS = 32
 VECTOR_STEPS_LAST = 32
 GPSIMD_COLUMNS = 320
 VECTOR_COLUMNS_LAST = 192
@@ -58,7 +58,7 @@ def tile_readout_ntk_step_e3_kernel(tc, g_words, g_scales, phi_train, mult, phi_
             return rotating("slab", shape, dtype, 7)
 
         ident = kept("ident", [P, P], F32)
-        g_scale = kept("g_scale", [P, T_GROUPS, C], U8)
+        g_scale = [kept("g_scale%d" % half, [P, T_GROUPS, N], U8) for half in range(2)]
         train_scale = kept("train_scale", [P, T_GROUPS, H], U8)
         mult_sb = [kept("mult%d" % quad, [P, PACK, N], BF16) for quad in range(len(QUADS))]
         d_codes = kept("d_codes", [P, H_GROUPS, C], U32)
@@ -89,8 +89,8 @@ def tile_readout_ntk_step_e3_kernel(tc, g_words, g_scales, phi_train, mult, phi_
             return banks[-1]
 
 
-        def load_train(g):
-            nc.sync.dma_start(out=train_sb[g][:], in_=train_view[:, g, :, :])
+        def load_train(g, features=slice(0, H)):
+            nc.sync.dma_start(out=train_sb[g][:, :, features], in_=train_view[:, g, :, features])
 
         def load_train_last(hg):
             nc.sync.dma_start(out=train_last[hg][:], in_=train_view[:, T_GROUPS - 1, :, cols(hg, K_PASS)])
@@ -99,6 +99,13 @@ def tile_readout_ntk_step_e3_kernel(tc, g_words, g_scales, phi_train, mult, phi_
             nc.sync.dma_start(
                 out=g_codes[half][:, lo:hi, :].bitcast(I32), in_=g_view[:, lo:hi, cols(half, PACK * N)].bitcast(I32)
             )
+
+        def load_g_scales(half, queue):
+            for r in range(4):
+                queue.dma_start(
+                    out=g_scale[half][r:P:32, :, :].bitcast(I32),
+                    in_=g_scales[:, r:16:4, cols(half, N)].rearrange("g q n -> q g n").bitcast(I32),
+                )
 
         def load_mult(quad):
             hg, half = QUADS[quad]
@@ -111,26 +118,29 @@ def tile_readout_ntk_step_e3_kernel(tc, g_words, g_scales, phi_train, mult, phi_
             nc.sync.dma_start(out=f0_sb[i][:], in_=f0_view[:, i, :, :])
 
 
-        def weave_train(g, hg):
+        def weave_train(g, hg, slots=slice(0, PACK)):
             last = g == T_GROUPS - 1
             raw = train_last[hg][:] if last else train_sb[g][:, :, cols(hg, K_PASS)]
-            woven = train_woven[g, hg] = rotating("train_woven", [P, PACK * K_PASS], BF16, 3)
+            if slots.start == 0:
+                train_woven[g, hg] = rotating("train_woven", [P, PACK * K_PASS], BF16, 3)
+            woven = train_woven[g, hg]
             src = raw.rearrange("p j (m n t) -> p m t n j", n=2, t=PACK)
             dst = woven[:].rearrange("p (t m n j) -> p m t n j", t=PACK, n=2, j=PACK)
             cut = VECTOR_STEPS_LAST if last and hg == H_GROUPS - 1 else VECTOR_STEPS
-            nc.vector.tensor_copy(out=dst[:, :cut, :, :, :], in_=src[:, :cut, :, :, :])
+            nc.vector.tensor_copy(out=dst[:, :cut, slots, :, :], in_=src[:, :cut, slots, :, :])
             if (g, hg) == (0, 0):
                 src = raw.rearrange("p j (m t) -> p m j t", t=PACK)
                 dst = woven[:].rearrange("p (t m j) -> p m j t", t=PACK, j=PACK)
                 nc.scalar.activation(out=dst[:, 2 * cut :, :, :], in_=src[:, 2 * cut :, :, :], func=ACT.Copy)
             else:
-                nc.scalar.copy(out=dst[:, cut:, :, :, :], in_=src[:, cut:, :, :, :])
+                nc.scalar.copy(out=dst[:, cut:, slots, :, :], in_=src[:, cut:, slots, :, :])
 
-        def quantise_train(g, hg):
+        def quantise_train(g, hg, slots=slice(0, PACK)):
+            lo, hi = slots.start * P, slots.stop * P
             nc.vector.quantize_mx(
-                out=train_codes[hg][:, g, :].bitcast(E4M3X4),
-                scales=train_scale[:, g, cols(hg, K_PASS)],
-                in_=train_woven[g, hg][:],
+                out=train_codes[hg][:, g, lo:hi].bitcast(E4M3X4),
+                scales=train_scale[:, g, hg * K_PASS + lo : hg * K_PASS + hi],
+                in_=train_woven[g, hg][:, PACK * lo : PACK * hi],
             )
 
         def stage1_pass(i, g):
@@ -142,7 +152,7 @@ def tile_readout_ntk_step_e3_kernel(tc, g_words, g_scales, phi_train, mult, phi_
                 lhsT=train_codes[hg][:, g, cols(i % PACK, P)].bitcast(E4M3X4),
                 lhsT_scale=train_scale[:, g, cols(hg * PACK + i % PACK, P)],
                 rhs=g_codes[half][:, g, :].bitcast(E5M2X4),
-                rhs_scale=g_scale[:, g, cols(half, N)],
+                rhs_scale=g_scale[half][:, g, :],
                 start=(g == 0),
                 stop=(g == T_GROUPS - 1),
             )
@@ -150,10 +160,6 @@ def tile_readout_ntk_step_e3_kernel(tc, g_words, g_scales, phi_train, mult, phi_
         def stage1_passes(i, lo, hi):
             for g in range(lo, hi):
                 stage1_pass(i, g)
-
-        def quad_group(quad, g):
-            for t in range(PACK):
-                stage1_pass(quad * PACK + t, g)
 
 
         def square(first, count):
@@ -184,10 +190,7 @@ def tile_readout_ntk_step_e3_kernel(tc, g_words, g_scales, phi_train, mult, phi_
             return d_woven[quad]
 
         def weave_d(quad, lo, hi, copy):
-            src = d_flat[quad][:].rearrange("p t (c e) -> p c t e", e=PACK)
-            dst = woven_tile(quad)[:].rearrange("p (c e) t -> p c t e", e=PACK)
-            steps = slice(lo // PACK, hi // PACK)
-            copy(out=dst[:, steps, :, :], in_=src[:, steps, :, :])
+            copy(out=woven_tile(quad)[:, lo:hi, :], in_=d_flat[quad][:].rearrange("p t c -> p c t")[:, lo:hi, :])
 
         def weave_d_on_gpsimd(quad, hi):
             nc.gpsimd.tensor_scalar(
@@ -282,25 +285,24 @@ def tile_readout_ntk_step_e3_kernel(tc, g_words, g_scales, phi_train, mult, phi_
                         in_=results[tile // 2][:, tile % 2, cols(part, N)],
                     )
 
-        nc.vector.memset(g_scale[:].rearrange("p g n -> p (g n)").bitcast(U32), 0)
+        for half in range(2):
+            nc.vector.memset(g_scale[half][:].rearrange("p g n -> p (g n)").bitcast(U32), 0)
         make_identity(nc, ident[:])
-        for r in range(4):
-            nc.scalar.dma_start(
-                out=g_scale[r:P:32, :, :].bitcast(I32),
-                in_=g_scales[:, r:16:4, :].rearrange("g q n -> q g n").bitcast(I32),
-            )
+        load_g_scales(0, nc.scalar)
 
         last = T_GROUPS - 1
         load_train(0)
         load_train(1)
         load_g(0, 1, 0)
         load_train(2)
-        load_g(1, last, 0)
         for hg in range(H_GROUPS):
+            load_g(1 + hg, 2 + hg, 0)
             load_train_last(hg)
         load_g(last, T_GROUPS, 0)
         for part in range(2):
             load_mult(part)
+            if part == 0:
+                load_g_scales(1, nc.sync)
             load_g(2 * part, 2 * part + 2, 1)
         load_mult(2)
         load_mult(3)
@@ -311,12 +313,14 @@ def tile_readout_ntk_step_e3_kernel(tc, g_words, g_scales, phi_train, mult, phi_
         load_f0(ROW_TILES // LOAD_TILES - 1)
 
         pieces = [(g, hg) for g in range(T_GROUPS) for hg in range(H_GROUPS)]
-        weave_train(*pieces[0])
-        for i, (g, hg) in enumerate(pieces):
-            if i + 1 < len(pieces):
-                weave_train(*pieces[i + 1])
-            quantise_train(g, hg)
-            quad_group(hg, g)
+        steps = [(g, hg, slice(0, PACK)) for g, hg in pieces[:-1]] + [(*pieces[-1], cols(pair, 2)) for pair in range(2)]
+        weave_train(*steps[0])
+        for i, (g, hg, slots) in enumerate(steps):
+            if i + 1 < len(steps):
+                weave_train(*steps[i + 1])
+            quantise_train(g, hg, slots)
+            for t in range(slots.start, slots.stop):
+                stage1_pass(hg * PACK + t, g)
 
         for i in range(PACK):
             square(i, 1)

@@ -190,7 +190,10 @@ def tile_readout_ntk_step_e3_kernel(tc, g_words, g_scales, phi_train, mult, phi_
             return d_woven[quad]
 
         def weave_d(quad, lo, hi, copy):
-            copy(out=woven_tile(quad)[:, lo:hi, :], in_=d_flat[quad][:].rearrange("p t c -> p c t")[:, lo:hi, :])
+            src = d_flat[quad][:].rearrange("p t (c e) -> p c t e", e=PACK)
+            dst = woven_tile(quad)[:].rearrange("p (c e) t -> p c t e", e=PACK)
+            steps = slice(lo // PACK, hi // PACK)
+            copy(out=dst[:, steps, :, :], in_=src[:, steps, :, :])
 
         def weave_d_on_gpsimd(quad, hi):
             nc.gpsimd.tensor_scalar(
@@ -243,11 +246,11 @@ def tile_readout_ntk_step_e3_kernel(tc, g_words, g_scales, phi_train, mult, phi_
             for j in range(lo, hi):
                 turn(j)
 
-        def quantise_test(pair):
+        def quantise_test(lo, hi):
             nc.vector.quantize_mx(
-                out=test_codes[:, cols(pair, 2), :].rearrange("p j c -> p (j c)").bitcast(E4M3X4),
-                scales=test_scale[:, cols(pair, 2), :].rearrange("p j c -> p (j c)"),
-                in_=test_woven[pair][:].rearrange("p j c -> p (j c)"),
+                out=test_codes[:, lo:hi, :].rearrange("p j c -> p (j c)").bitcast(E4M3X4),
+                scales=test_scale[:, lo:hi, :].rearrange("p j c -> p (j c)"),
+                in_=test_woven[lo // 2][:, lo % 2 : lo % 2 + hi - lo, :].rearrange("p j c -> p (j c)"),
             )
 
 
@@ -274,7 +277,7 @@ def tile_readout_ntk_step_e3_kernel(tc, g_words, g_scales, phi_train, mult, phi_
                 nc.scalar.copy(out=result, in_=bank[:])
                 nc.gpsimd.tensor_tensor(out=result, in0=result, in1=f0_part, op=ALU.add)
             if then_quantise:
-                quantise_test(then_quantise)
+                quantise_test(*then_quantise)
             stored.append((j, half))
             waiting_stores.append((len(stored) + (0 if on_vector else SLOW_STORE_LAG), j, half))
             for due, tile, part in sorted(waiting_stores):
@@ -352,7 +355,7 @@ def tile_readout_ntk_step_e3_kernel(tc, g_words, g_scales, phi_train, mult, phi_
         quantise_d(0)
         quantise_d(1)
         weave_d(2, N // 2, N, nc.scalar.copy)
-        quantise_test(0)
+        quantise_test(0, 2)
         sum_and_scale(14)
         sum_and_scale(15)
         quantise_d(2)
@@ -360,27 +363,27 @@ def tile_readout_ntk_step_e3_kernel(tc, g_words, g_scales, phi_train, mult, phi_
         turn_tiles(3, 4)
         weave_d(3, VECTOR_COLUMNS_LAST, N, nc.scalar.copy)
         turn_tiles(4, 6)
-        quantise_test(1)
+        quantise_test(2, 4)
         weave_d(3, 0, VECTOR_COLUMNS_LAST, nc.vector.tensor_copy)
 
         for j in range(LOAD_TILES):
             stage2(j, 0)
             if j == 1:
                 quantise_d(3)
-        quantise_test(2)
+        quantise_test(4, 6)
         turn_tiles(6, 8)
         for first in range(2 * LOAD_TILES, ROW_TILES, 2):
             sort_words(first)
         for j in range(LOAD_TILES):
             stage2(j, 1)
             if j == 1:
-                quantise_test(3)
+                quantise_test(6, 8)
 
-        turn_before = {(6, 0): 4, (7, 1): 5}
-        slow_banks = [(4, 1), (8, 0)]
+        turn_before = {(6, 0): (8, 11), (9, 0): (11, 12)}
+        quantise_after = {(6, 0): (8, 10), (8, 1): (10, 11), (9, 0): (11, 12)}
+        slow_banks = [(4, 1), (6, 1)]
         for j in range(LOAD_TILES, ROW_TILES):
             for half in range(2):
-                pair = turn_before.get((j, half))
-                if pair:
-                    turn_tiles(2 * pair, 2 * pair + 2)
-                stage2(j, half, (j, half) not in slow_banks, pair)
+                if (j, half) in turn_before:
+                    turn_tiles(*turn_before[j, half])
+                stage2(j, half, (j, half) not in slow_banks, quantise_after.get((j, half)))

@@ -30,7 +30,7 @@ QUADS = [(0, 0), (1, 0), (0, 1), (1, 1)]
 
 VECTOR_STEPS = 32
 VECTOR_STEPS_LAST = 32
-GPSIMD_COLUMNS = 320
+GPSIMD_COLUMNS = 512
 VECTOR_COLUMNS_LAST = 192
 SLOW_STORE_LAG = 4
 SQUARE_TILES = 4
@@ -214,13 +214,13 @@ def tile_readout_ntk_step_e3_kernel(tc, g_words, g_scales, phi_train, mult, phi_
             )
 
 
-        def sort_words(first):
+        def sort_words(first, copy=nc.scalar.copy):
             load, row = divmod(first, LOAD_TILES)
             tile = rotating("sorted_words", [P, 2, H // 2], F32, 2)
             for j in range(2):
                 sorted_words[first + j] = tile[:, j, :]
             words = test_sb[load][:, row : row + 2, :].rearrange("p j h -> p (j h)").bitcast(F32)
-            nc.scalar.copy(
+            copy(
                 out=tile[:].rearrange("p j (g u r) -> p (j g) r u", g=H_GROUPS, u=2),
                 in_=words.rearrange("p (g r u) -> p g r u", r=P, u=2),
             )
@@ -350,11 +350,11 @@ def tile_readout_ntk_step_e3_kernel(tc, g_words, g_scales, phi_train, mult, phi_
         sum_and_scale(12)
         weave_d(2, 0, N // 2, nc.scalar.copy)
         sum_and_scale(13)
-        weave_d(1, GPSIMD_COLUMNS, N, nc.vector.tensor_copy)
         turn_tiles(0, 3)
         quantise_d(0)
         quantise_d(1)
         weave_d(2, N // 2, N, nc.scalar.copy)
+        sort_words(6, nc.vector.tensor_copy)
         quantise_test(0, 2)
         sum_and_scale(14)
         sum_and_scale(15)

from contextlib import ExitStack

import concourse.mybir as mybir
from concourse.masks import make_identity

T, H, C, Q = 2048, 1024, 1024, 1536
FLOPS = 2 * T * H * C + 2 * Q * H * C

F32 = mybir.dt.float32
BF16 = mybir.dt.bfloat16
U32 = mybir.dt.uint32
I32 = mybir.dt.int32
U8 = mybir.dt.uint8
E4M3X4 = mybir.dt.float8_e4m3fn_x4
E5M2X4 = mybir.dt.float8_e5m2_x4
ACT = mybir.ActivationFunctionType
ALU = mybir.AluOpType

P = 128
PACK = 4
K_PASS = P * PACK
N = 512
BANKS = 8
T_GROUPS = T // K_PASS
H_GROUPS = H // K_PASS
ROW_TILES = Q // P
LOAD_TILES = 4

QUADS = [(0, 0), (1, 0), (0, 1), (1, 1)]

VECTOR_STEPS = 32
VECTOR_STEPS_LAST = 32
GPSIMD_COLUMNS = 512
VECTOR_COLUMNS_LAST = 192
SLOW_STORE_LAG = 4
SQUARE_TILES = 4


def cols(i, width):
    return slice(i * width, (i + 1) * width)


def tile_readout_ntk_step_e3_kernel(tc, g_words, g_scales, phi_train, mult, phi_test, f0, out):
    nc = tc.nc
    with ExitStack() as ctx:
        keep = ctx.enter_context(tc.tile_pool(name="keep", bufs=1))
        work = ctx.enter_context(tc.tile_pool(name="work", bufs=1))
        psum = ctx.enter_context(tc.psum_pool(name="psum", bufs=1))
        ctx.enter_context(tc.manual_schedule())

        def kept(name, shape, dtype):
            return keep.tile(shape, dtype, name=name, align_bytes=64)

        def rotating(name, shape, dtype, bufs):
            return work.tile(shape, dtype, name=name, bufs=bufs, align_bytes=64)

        def slab(shape, dtype):
            return rotating("slab", shape, dtype, 7)

        ident = kept("ident", [P, P], F32)
        g_scale = [kept("g_scale%d" % half, [P, T_GROUPS, N], U8) for half in range(2)]
        train_scale = kept("train_scale", [P, T_GROUPS, H], U8)
        mult_sb = [kept("mult%d" % quad, [P, PACK, N], BF16) for quad in range(len(QUADS))]
        d_codes = kept("d_codes", [P, H_GROUPS, C], U32)
        d_scale = kept("d_scale", [P, H_GROUPS, C], U8)
        test_sb = [kept("test%d" % i, [P, LOAD_TILES, H], BF16) for i in range(ROW_TILES // LOAD_TILES)]
        f0_sb = [kept("f0_%d" % i, [P, LOAD_TILES, C], BF16) for i in range(ROW_TILES // LOAD_TILES)]
        test_codes = kept("test_codes", [P, ROW_TILES, H_GROUPS * P], U32)
        test_scale = kept("test_scale", [P, ROW_TILES, H_GROUPS * P], U8)
        train_sb = [slab([P, PACK, H], BF16) for g in range(T_GROUPS - 1)]
        g_codes = [slab([P, T_GROUPS, N], U32) for half in range(2)]
        train_codes = [slab([P, T_GROUPS, K_PASS], U32) for hg in range(H_GROUPS)]
        train_last = [kept("train_last%d" % hg, [P, PACK, K_PASS], BF16) for hg in range(H_GROUPS)]

        g_view = g_words.rearrange("g p n t -> p g (n t)")
        train_view = phi_train.rearrange("(g p j) h -> p g j h", p=P, j=PACK)
        mult_view = mult.rearrange("(g p t) c -> p g t c", p=P, t=PACK)
        test_view = phi_test.rearrange("(i p j) h -> p i j h", p=P, j=LOAD_TILES)
        f0_view = f0.rearrange("(i p j) c -> p i j c", p=P, j=LOAD_TILES)
        out_view = out.rearrange("(i p j) c -> p i j c", p=P, j=LOAD_TILES)

        banks = []
        a_banks, squares, d_flat, d_woven, sorted_words, test_woven, results = {}, {}, {}, {}, {}, {}, {}
        train_woven = {}
        stored, waiting_stores = [], []

        def next_bank():
            banks.append(psum.tile([P, N], F32, name="bank%d" % (len(banks) % BANKS)))
            return banks[-1]


        def load_train(g, features=slice(0, H)):
            nc.sync.dma_start(out=train_sb[g][:, :, features], in_=train_view[:, g, :, features])

        def load_train_last(hg):
            nc.sync.dma_start(out=train_last[hg][:], in_=train_view[:, T_GROUPS - 1, :, cols(hg, K_PASS)])

        def load_g(lo, hi, half):
            nc.sync.dma_start(
                out=g_codes[half][:, lo:hi, :].bitcast(I32), in_=g_view[:, lo:hi, cols(half, PACK * N)].bitcast(I32)
            )

        def load_g_scales(half, queue):
            for r in range(4):
                queue.dma_start(
                    out=g_scale[half][r:P:32, :, :].bitcast(I32),
                    in_=g_scales[:, r:16:4, cols(half, N)].rearrange("g q n -> q g n").bitcast(I32),
                )

        def load_mult(quad):
            hg, half = QUADS[quad]
            nc.sync.dma_start(out=mult_sb[quad][:], in_=mult_view[:, hg, :, cols(half, N)])

        def load_test(i):
            nc.sync.dma_start(out=test_sb[i][:], in_=test_view[:, i, :, :])

        def load_f0(i):
            nc.sync.dma_start(out=f0_sb[i][:], in_=f0_view[:, i, :, :])


        def weave_train(g, hg, slots=slice(0, PACK)):
            last = g == T_GROUPS - 1
            raw = train_last[hg][:] if last else train_sb[g][:, :, cols(hg, K_PASS)]
            if slots.start == 0:
                train_woven[g, hg] = rotating("train_woven", [P, PACK * K_PASS], BF16, 3)
            woven = train_woven[g, hg]
            src = raw.rearrange("p j (m n t) -> p m t n j", n=2, t=PACK)
            dst = woven[:].rearrange("p (t m n j) -> p m t n j", t=PACK, n=2, j=PACK)
            cut = VECTOR_STEPS_LAST if last and hg == H_GROUPS - 1 else VECTOR_STEPS
            nc.vector.tensor_copy(out=dst[:, :cut, slots, :, :], in_=src[:, :cut, slots, :, :])
            if (g, hg) == (0, 0):
                src = raw.rearrange("p j (m t) -> p m j t", t=PACK)
                dst = woven[:].rearrange("p (t m j) -> p m j t", t=PACK, j=PACK)
                nc.scalar.activation(out=dst[:, 2 * cut :, :, :], in_=src[:, 2 * cut :, :, :], func=ACT.Copy)
            else:
                nc.scalar.copy(out=dst[:, cut:, slots, :, :], in_=src[:, cut:, slots, :, :])

        def quantise_train(g, hg, slots=slice(0, PACK)):
            lo, hi = slots.start * P, slots.stop * P
            nc.vector.quantize_mx(
                out=train_codes[hg][:, g, lo:hi].bitcast(E4M3X4),
                scales=train_scale[:, g, hg * K_PASS + lo : hg * K_PASS + hi],
                in_=train_woven[g, hg][:, PACK * lo : PACK * hi],
            )

        def stage1_pass(i, g):
            hg, half = QUADS[i // PACK]
            if g == 0:
                a_banks[i] = next_bank()
            nc.tensor.matmul_mx(
                out=a_banks[i][:],
                lhsT=train_codes[hg][:, g, cols(i % PACK, P)].bitcast(E4M3X4),
                lhsT_scale=train_scale[:, g, cols(hg * PACK + i % PACK, P)],
                rhs=g_codes[half][:, g, :].bitcast(E5M2X4),
                rhs_scale=g_scale[half][:, g, :],
                start=(g == 0),
                stop=(g == T_GROUPS - 1),
            )

        def stage1_passes(i, lo, hi):
            for g in range(lo, hi):
                stage1_pass(i, g)


        def square(first, count):
            quad, t = divmod(first, PACK)
            if first % 2 == 0:
                squares[first // 2] = rotating("square", [P, 2, N], F32, SQUARE_TILES)
            nc.scalar.activation(
                out=squares[first // 2][:, first % 2 : first % 2 + count, :],
                in_=mult_sb[quad][:, t : t + count, :],
                func=ACT.Square,
            )

        def scale_bank(i):
            quad, t = divmod(i, PACK)
            if t == 0:
                d_flat[quad] = rotating("d_flat", [P, PACK, N], BF16, 3)
            nc.vector.tensor_tensor(
                out=d_flat[quad][:, t, :], in0=a_banks[i][:], in1=squares[i // 2][:, i % 2, :], op=ALU.mult
            )

        def sum_and_scale(i):
            stage1_passes(i, 0, T_GROUPS)
            scale_bank(i)

        def woven_tile(quad):
            if quad not in d_woven:
                d_woven[quad] = rotating("d_woven", [P, N, PACK], BF16, 3)
            return d_woven[quad]

        def weave_d(quad, lo, hi, copy):
            src = d_flat[quad][:].rearrange("p t (c e) -> p c t e", e=PACK)
            dst = woven_tile(quad)[:].rearrange("p (c e) t -> p c t e", e=PACK)
            steps = slice(lo // PACK, hi // PACK)
            copy(out=dst[:, steps, :, :], in_=src[:, steps, :, :])

        def weave_d_on_gpsimd(quad, hi):
            nc.gpsimd.tensor_scalar(
                out=woven_tile(quad)[:, :hi, :],
                in0=d_flat[quad][:].rearrange("p t c -> p c t")[:, :hi, :],
                scalar1=1.0,
                scalar2=0.0,
                op0=ALU.mult,
                op1=ALU.add,
            )

        def quantise_d(quad):
            hg, half = QUADS[quad]
            nc.vector.quantize_mx(
                out=d_codes[:, hg, cols(half, N)].bitcast(E5M2X4),
                scales=d_scale[:, hg, cols(half, N)],
                in_=d_woven[quad][:].rearrange("p c t -> p (c t)"),
            )


        def sort_words(first, copy=nc.scalar.copy):
            load, row = divmod(first, LOAD_TILES)
            tile = rotating("sorted_words", [P, 2, H // 2], F32, 2)
            for j in range(2):
                sorted_words[first + j] = tile[:, j, :]
            words = test_sb[load][:, row : row + 2, :].rearrange("p j h -> p (j h)").bitcast(F32)
            copy(
                out=tile[:].rearrange("p j (g u r) -> p (j g) r u", g=H_GROUPS, u=2),
                in_=words.rearrange("p (g r u) -> p g r u", r=P, u=2),
            )

        def turn(j):
            load, row = divmod(j, LOAD_TILES)
            bank = next_bank()
            for hg in range(H_GROUPS):
                for u in range(2):
                    if j in sorted_words:
                        words = sorted_words[j][:, cols(2 * hg + u, P)]
                    else:
                        words = test_sb[load][:, row, :].bitcast(F32)[:, 2 * P * hg + u : 2 * P * (hg + 1) : 2]
                    nc.tensor.transpose(bank[:, cols(2 * hg + u, P)], words, ident[:])
            if j % 2 == 0:
                test_woven[j // 2] = rotating("test_woven", [P, 2, H], BF16, 2)
            nc.scalar.copy(
                out=test_woven[j // 2][:, j % 2, :].bitcast(F32).rearrange("p (g r u) -> p g r u", g=H_GROUPS, u=2),
                in_=bank[:].rearrange("p (g u r) -> p g r u", g=H_GROUPS, u=2),
            )

        def turn_tiles(lo, hi):
            for j in range(lo, hi):
                turn(j)

        def quantise_test(lo, hi):
            nc.vector.quantize_mx(
                out=test_codes[:, lo:hi, :].rearrange("p j c -> p (j c)").bitcast(E4M3X4),
                scales=test_scale[:, lo:hi, :].rearrange("p j c -> p (j c)"),
                in_=test_woven[lo // 2][:, lo % 2 : lo % 2 + hi - lo, :].rearrange("p j c -> p (j c)"),
            )


        def stage2(j, half, on_vector=True, then_quantise=None):
            load, row = divmod(j, LOAD_TILES)
            bank = next_bank()
            for hg in range(H_GROUPS):
                nc.tensor.matmul_mx(
                    out=bank[:],
                    lhsT=test_codes[:, j, cols(hg, P)].bitcast(E4M3X4),
                    lhsT_scale=test_scale[:, j, cols(hg, P)],
                    rhs=d_codes[:, hg, cols(half, N)].bitcast(E5M2X4),
                    rhs_scale=d_scale[:, hg, cols(half, N)],
                    start=(hg == 0),
                    stop=(hg == H_GROUPS - 1),
                )
            if j // 2 not in results:
                results[j // 2] = slab([P, 2, C], F32)
            result = results[j // 2][:, j % 2, cols(half, N)]
            f0_part = f0_sb[load][:, row, cols(half, N)]
            if on_vector:
                nc.vector.tensor_tensor(out=result, in0=bank[:], in1=f0_part, op=ALU.add)
            else:
                nc.scalar.copy(out=result, in_=bank[:])
                nc.gpsimd.tensor_tensor(out=result, in0=result, in1=f0_part, op=ALU.add)
            if then_quantise:
                quantise_test(*then_quantise)
            stored.append((j, half))
            waiting_stores.append((len(stored) + (0 if on_vector else SLOW_STORE_LAG), j, half))
            for due, tile, part in sorted(waiting_stores):
                if due <= len(stored):
                    waiting_stores.remove((due, tile, part))
                    nc.sync.dma_start(
                        out=out_view[:, tile // LOAD_TILES, tile % LOAD_TILES, cols(part, N)],
                        in_=results[tile // 2][:, tile % 2, cols(part, N)],
                    )

        for half in range(2):
            nc.vector.memset(g_scale[half][:].rearrange("p g n -> p (g n)").bitcast(U32), 0)
        make_identity(nc, ident[:])
        load_g_scales(0, nc.scalar)

        last = T_GROUPS - 1
        load_train(0)
        load_train(1)
        load_g(0, 1, 0)
        load_train(2)
        for hg in range(H_GROUPS):
            load_g(1 + hg, 2 + hg, 0)
            load_train_last(hg)
        load_g(last, T_GROUPS, 0)
        for part in range(2):
            load_mult(part)
            if part == 0:
                load_g_scales(1, nc.sync)
            load_g(2 * part, 2 * part + 2, 1)
        load_mult(2)
        load_mult(3)
        load_test(0)
        for i in range(1, ROW_TILES // LOAD_TILES):
            load_test(i)
            load_f0(i - 1)
        load_f0(ROW_TILES // LOAD_TILES - 1)

        pieces = [(g, hg) for g in range(T_GROUPS) for hg in range(H_GROUPS)]
        steps = [(g, hg, slice(0, PACK)) for g, hg in pieces[:-1]] + [(*pieces[-1], cols(pair, 2)) for pair in range(2)]
        weave_train(*steps[0])
        for i, (g, hg, slots) in enumerate(steps):
            if i + 1 < len(steps):
                weave_train(*steps[i + 1])
            quantise_train(g, hg, slots)
            for t in range(slots.start, slots.stop):
                stage1_pass(hg * PACK + t, g)

        for i in range(PACK):
            square(i, 1)
        square(4, 2)
        square(6, 2)
        for i in range(PACK):
            scale_bank(i)
        weave_d_on_gpsimd(0, N)

        for i in range(BANKS, BANKS + PACK):
            stage1_passes(i, 0, 2)
        square(8, 2)
        for i in range(PACK, BANKS):
            scale_bank(i)
            if i % 2:
                square(i + 5, 2)
        weave_d_on_gpsimd(1, GPSIMD_COLUMNS)
        for i in range(BANKS, BANKS + PACK):
            stage1_passes(i, 2, T_GROUPS)
            scale_bank(i)
            if i == BANKS + 1:
                square(14, 2)

        sum_and_scale(12)
        weave_d(2, 0, N // 2, nc.scalar.copy)
        sum_and_scale(13)
        turn_tiles(0, 3)
        quantise_d(0)
        quantise_d(1)
        weave_d(2, N // 2, N, nc.scalar.copy)
        sort_words(6, nc.vector.tensor_copy)
        quantise_test(0, 2)
        sum_and_scale(14)
        sum_and_scale(15)
        quantise_d(2)

        turn_tiles(3, 4)
        weave_d(3, VECTOR_COLUMNS_LAST, N, nc.scalar.copy)
        turn_tiles(4, 6)
        quantise_test(2, 4)
        weave_d(3, 0, VECTOR_COLUMNS_LAST, nc.vector.tensor_copy)

        for j in range(LOAD_TILES):
            stage2(j, 0)
            if j == 1:
                quantise_d(3)
        quantise_test(4, 6)
        turn_tiles(6, 8)
        for first in range(2 * LOAD_TILES, ROW_TILES, 2):
            sort_words(first)
        for j in range(LOAD_TILES):
            stage2(j, 1)
            if j == 1:
                quantise_test(6, 8)

        turn_before = {(6, 0): (8, 11), (9, 0): (11, 12)}
        quantise_after = {(6, 0): (8, 10), (8, 1): (10, 11), (9, 0): (11, 12)}
        slow_banks = [(4, 1), (6, 1)]
        for j in range(LOAD_TILES, ROW_TILES):
            for half in range(2):
                if (j, half) in turn_before:
                    turn_tiles(*turn_before[j, half])
                stage2(j, half, (j, half) not in slow_banks, quantise_after.get((j, half)))
